import numpy as np
import ml_dtypes


def mxq(x, axis, fmt="e4m3"):
    dtype, down = {"e4m3": (ml_dtypes.float8_e4m3fn, 7), "e5m2": (ml_dtypes.float8_e5m2, 14)}[fmt]
    v = np.moveaxis(np.asarray(x, np.float32).astype(ml_dtypes.bfloat16).astype(np.float64), axis, -1)
    blocks = v.reshape(v.shape[:-1] + (-1, 32))
    amax = np.abs(blocks).max(-1, keepdims=True)
    byte = np.maximum(np.where(amax > 0, np.frexp(amax)[1] - 1 + 127, 0) - down, 1)
    scale = np.exp2(byte - 127.0)
    codes = (blocks / scale).astype(np.float32).astype(dtype).astype(np.float64)
    return np.moveaxis((codes * scale).reshape(v.shape), -1, axis)


WIDE = False


def mx_kscale(k):
    if not WIDE:
        return np.ones(k)
    levels = np.array([10, -10, 5, -5, 0])
    if k % 512:
        return np.exp2(np.random.permutation(np.resize(levels, k // 32))).repeat(32)
    a = np.empty((k // 512, 16))
    for p in range(k // 512):
        a[p, :8] = np.random.permutation(np.resize(levels, 8))
        for g in range(8):
            far = levels[np.abs(levels - a[p, g]) >= 10]
            a[p, g + 8] = far[np.random.randint(len(far))]
    return np.exp2(a.ravel()).repeat(32)


def f64(x):
    return np.asarray(x).astype(np.float64)


def striped(idx):
    return np.tile(idx.reshape(-1, 16).T, (8, 1)).astype(np.uint16)


def unstriped(offs):
    return offs[:16].T.reshape(-1).astype(np.int64)


E2M1 = np.array([0.0, 0.5, 1.0, 1.5, 2.0, 3.0, 4.0, 6.0, -0.0, -0.5, -1.0, -1.5, -2.0, -3.0, -4.0, -6.0])


def pack_weight(w, fmt):
    k, n = w.shape
    w = f64(np.asarray(w, np.float32).astype(ml_dtypes.bfloat16)).reshape(k // 32, 32, n)
    amax = np.abs(w).max(1)
    if fmt == "e4m3":
        byte = np.frexp(amax)[1] - 1 + 127 - 7
    else:
        mant, ex = np.frexp(amax / 6.0)
        byte = np.where(mant > 0.5, ex, ex - 1) + 127
    byte = np.clip(np.where(amax > 0, byte, 1), 1, 254)
    scaled = (w * np.exp2(127.0 - byte)[:, None, :]).reshape(k, n).astype(np.float32)
    by_word = np.ascontiguousarray(scaled.reshape(k // 512, 128, 4, n).transpose(0, 1, 3, 2))
    if fmt == "e4m3":
        words = by_word.astype(ml_dtypes.float8_e4m3fn).view(np.uint8)
    else:
        c = by_word.astype(ml_dtypes.float4_e2m1fn).view(np.uint8) & 0xF
        words = (c[..., 0::2] | (c[..., 1::2] << 4)).reshape(k // 512, 128, 2 * n)
    return np.ascontiguousarray(words), np.ascontiguousarray(byte.astype(np.uint8).reshape(k // 512, 16, n))


def unpack_weight(words, scales, fmt):
    g, _, n = scales.shape
    words = np.ascontiguousarray(words).reshape(g, 128, n, -1)
    if fmt == "e4m3":
        vals = words.view(ml_dtypes.float8_e4m3fn).astype(np.float64)
    else:
        nib = np.empty((g, 128, n, 4), np.uint8)
        nib[..., 0::2] = words & 0xF
        nib[..., 1::2] = words >> 4
        vals = E2M1[nib]
    vals = vals * np.repeat(np.exp2(scales.astype(np.float64) - 127.0), 8, axis=1)[..., None]
    return vals.transpose(0, 1, 3, 2).reshape(g * 512, n)


def planes(y):
    n, m = y.shape
    v = y.astype(np.float32).astype(ml_dtypes.bfloat16).astype(np.float64).reshape(n // 32, 32, m)
    top = np.abs(v).max(1)
    byte = np.clip(np.where(top > 0, np.frexp(top)[1] - 1 + 127 - 7, 1), 1, 254)
    codes = (v * np.exp2(127.0 - byte)[:, None, :]).reshape(n, m).astype(np.float32).astype(ml_dtypes.float8_e4m3fn).view(np.uint8)
    words = codes.reshape(n // 512, 128, 4, m).transpose(0, 1, 3, 2)
    return np.ascontiguousarray(words), np.ascontiguousarray(byte.astype(np.uint8).reshape(n // 512, 16, m))


def gelu(v):
    return 0.5 * v * (1.0 + np.tanh(np.sqrt(2.0 / np.pi) * (v + 0.044715 * v**3)))


K, T, E, C, H, N, HOT = 1024, 512, 8, 128, 512, 512, 2


def by_expert(wq, xq):
    return np.concatenate([wq[e].T @ xq[:, e * C:(e + 1) * C] for e in range(E)], axis=1)


def setup_inputs():
    n = np.random.standard_normal
    s = mx_kscale(K)
    u = mx_kscale(H)
    slot_token = np.concatenate([np.random.permutation(T)[:C] for e in range(E)])
    x = pack_weight(n((K, T)) * s[:, None], "e4m3")
    w1h = [pack_weight(m, "e4m3") for m in n((HOT, K, H)) / np.sqrt(K) / s[None, :, None] * u]
    w2h = [pack_weight(m, "e4m3") for m in n((HOT, H, N)) / np.sqrt(H) / u[None, :, None]]
    w1c = [pack_weight(m, "e2m1") for m in n((E - HOT, K, H)) / np.sqrt(K) / s[None, :, None] * u]
    w2c = [pack_weight(m, "e2m1") for m in n((E - HOT, H, N)) / np.sqrt(H) / u[None, :, None]]
    return {
        "x_words": x[0],
        "x_scales": x[1],
        "w1h_words": np.stack([m[0] for m in w1h]),
        "w1h_scales": np.stack([m[1] for m in w1h]),
        "w2h_words": np.stack([m[0] for m in w2h]),
        "w2h_scales": np.stack([m[1] for m in w2h]),
        "w1c_words": np.stack([m[0] for m in w1c]),
        "w1c_scales": np.stack([m[1] for m in w1c]),
        "w2c_words": np.stack([m[0] for m in w2c]),
        "w2c_scales": np.stack([m[1] for m in w2c]),
        "offs": striped(slot_token),
    }


def reference(x_words, x_scales, w1h_words, w1h_scales, w2h_words, w2h_scales, w1c_words, w1c_scales, w2c_words, w2c_scales, offs):
    w1h = np.stack([unpack_weight(w1h_words[e], w1h_scales[e], "e4m3") for e in range(HOT)])
    w2h = np.stack([unpack_weight(w2h_words[e], w2h_scales[e], "e4m3") for e in range(HOT)])
    w1c = np.stack([unpack_weight(w1c_words[e], w1c_scales[e], "e2m1") for e in range(E - HOT)])
    w2c = np.stack([unpack_weight(w2c_words[e], w2c_scales[e], "e2m1") for e in range(E - HOT)])
    idx = unstriped(offs)
    xq = unpack_weight(x_words, x_scales, "e4m3")[:, idx]
    w1 = [*w1h, *w1c]
    w2 = [*w2h, *w2c]
    h = gelu(by_expert(w1, xq))
    y = by_expert(w2, mxq(h, 0, "e4m3"))
    out = y
    out_0 = out
    return (out_0,) + planes(out_0)

@@ -1,0 +1,233 @@
+from contextlib import ExitStack
+
+import concourse.mybir as mybir
+from concourse.masks import make_identity
+
+K, T, E, C, H, N, HOT = 1024, 512, 8, 128, 512, 512, 2
+FLOPS = 2 * E * C * (K * H + H * N)
+
+F32 = mybir.dt.float32
+BF16 = mybir.dt.bfloat16
+I32 = mybir.dt.int32
+U32 = mybir.dt.uint32
+U16 = mybir.dt.uint16
+U8 = mybir.dt.uint8
+FP8X4 = mybir.dt.float8_e4m3fn_x4
+FP4X4 = mybir.dt.float4_e2m1fn_x4
+GELU = mybir.ActivationFunctionType.Gelu_apprx_tanh
+
+P = 128
+PASSES = K // 512
+COLD = E - HOT
+LIST_COLS = C // 16
+GATHER_GROUPS = ((0, 1), (1, 2), (2, 4), (4, 6), (6, 8))
+HELD_GROUPS = {4: 0, 6: 1}
+SUM_BANKS = 4
+LAG = 2
+ROW_GROUPS = ((0, 2), (2, 4), (4, 6), (6, 7), (7, 8))
+CODE_GROUPS = ((0, 6), (6, 8))
+
+
+def tile_moe_hot_s_mlp_gelu_kernel(
+    tc, x_words, x_scales, w1h_words, w1h_scales, w2h_words, w2h_scales,
+    w1c_words, w1c_scales, w2c_words, w2c_scales, offs, out_0, out_1, out_2,
+):
+    nc = tc.nc
+    with ExitStack() as ctx:
+        keep = ctx.enter_context(tc.tile_pool(name="keep", bufs=1))
+        ring = ctx.enter_context(tc.tile_pool(name="ring", bufs=3))
+        psum = ctx.enter_context(tc.psum_pool(name="psum", bufs=2))
+        sums = ctx.enter_context(tc.psum_pool(name="sums", bufs=1))
+
+        def scale_tile(engine, name, planes):
+            tile = keep.tile([P, planes, 512], U8, name=name, align_bytes=64)
+            engine.memset(tile[:].rearrange("p a c -> p (a c)").bitcast(I32), 0)
+            return tile
+
+        def load_scales(queue, tile, rows):
+            for q in range(4):
+                queue.dma_start(out=tile[32 * q : 32 * q + 4].bitcast(I32), in_=rows[q].bitcast(I32))
+
+        def load_words(name, src):
+            tile = keep.tile(list(src.shape), U8, name=name, align_bytes=64)
+            nc.sync.dma_start(out=tile[:].bitcast(I32), in_=src.bitcast(I32))
+            return tile
+
+        x_sc = keep.tile([P, T], U8, name="x_sc", align_bytes=64)
+        nc.gpsimd.memset(x_sc[:].bitcast(I32), 0)
+        w1h_sc = scale_tile(nc.gpsimd, "w1h_sc", HOT * PASSES)
+        w2h_sc = scale_tile(nc.vector, "w2h_sc", HOT)
+        w1c_sc = scale_tile(nc.vector, "w1c_sc", COLD * PASSES)
+        w2c_sc = scale_tile(nc.gpsimd, "w2c_sc", COLD)
+        moved = keep.tile([P, COLD * C], U8, name="moved", align_bytes=64)
+        nc.vector.memset(moved[:].bitcast(I32), 0)
+
+        offsets = keep.tile([P, E * LIST_COLS], U16, name="offsets")
+        nc.sync.dma_start(offsets[:], offs)
+        for q in range(4):
+            queue = nc.sync if q < 2 else nc.scalar
+            queue.dma_start(
+                out=x_sc[32 * q : 32 * q + 4 * PASSES, :].bitcast(I32),
+                in_=x_scales[:, 4 * q : 4 * q + 4, :].bitcast(I32),
+            )
+        x_w = keep.tile([P, PASSES, T], I32, name="x_w", align_bytes=64)
+        nc.sync.dma_start(out=x_w[:], in_=x_words.rearrange("s p t d -> p s (t d)").bitcast(I32))
+
+        by_plane = "e s (q r) c -> q r (e s) c"
+        w1h0 = load_words("w1h0", w1h_words[0].rearrange("s p i d -> p s (i d)"))
+        load_scales(nc.scalar, w1h_sc, w1h_scales.rearrange(by_plane, r=4))
+        w1h1 = load_words("w1h1", w1h_words[1].rearrange("s p i d -> p s (i d)"))
+        w2h = load_words("w2h", w2h_words.rearrange("e s p n d -> p (e s) (n d)"))
+        load_scales(nc.scalar, w2h_sc, w2h_scales.rearrange(by_plane, r=4))
+        half = COLD // 2
+        w1c_first = load_words("w1c_first", w1c_words[:half].rearrange("f s p b -> p (f s) b"))
+        load_scales(nc.sync, w1c_sc, w1c_scales.rearrange(by_plane, r=4))
+
+        def list_slice(first, last):
+            return offsets[:, first * LIST_COLS : last * LIST_COLS]
+
+        hot_sc = keep.tile([P, HOT * C], U8, name="hot_sc", align_bytes=64)
+        nc.vector.tensor_copy(out=hot_sc[:], in_=x_sc[:].indirect(list_slice(0, HOT)))
+        cold_sc = keep.tile([P, COLD * C], U8, name="cold_sc", align_bytes=64)
+        for f in range(0, COLD, half):
+            nc.vector.tensor_copy(
+                out=cold_sc[:, f * C : (f + half) * C],
+                in_=x_sc[:].indirect(list_slice(HOT + f, HOT + f + half)),
+            )
+        for q in range(4):
+            nc.sync.dma_start(
+                out=moved[32 * q : 32 * q + 4, :].bitcast(I32),
+                in_=cold_sc[32 * q + 4 : 32 * q + 8, :].bitcast(I32),
+            )
+
+        w2c = load_words("w2c", w2c_words.rearrange("f s p b -> p (f s) b"))
+        load_scales(nc.sync, w2c_sc, w2c_scales.rearrange(by_plane, r=4))
+        w1c_second = load_words("w1c_second", w1c_words[half:].rearrange("f s p b -> p (f s) b"))
+
+        w1 = {}
+        w2 = {}
+        x_planes = {}
+        for e, tile in enumerate((w1h0, w1h1)):
+            mine = slice(e * C, (e + 1) * C)
+            w1[e] = [(tile[:, s, :].bitcast(FP8X4), w1h_sc[:, PASSES * e + s, :]) for s in range(PASSES)]
+            w2[e] = (w2h[:, e, :].bitcast(FP8X4), w2h_sc[:, e, :])
+            x_planes[e] = [hot_sc[4 * s : P, mine] for s in range(PASSES)]
+        for f in range(COLD):
+            mine = slice(f * C, (f + 1) * C)
+            tile = w1c_first if f < half else w1c_second
+            w1[HOT + f] = [
+                (tile[:, PASSES * (f % half) + s, :].bitcast(FP4X4), w1c_sc[:, PASSES * f + s, :])
+                for s in range(PASSES)
+            ]
+            w2[HOT + f] = (w2c[:, f, :].bitcast(FP4X4), w2c_sc[:, f, :])
+            x_planes[HOT + f] = [cold_sc[:, mine], moved[:, mine]]
+
+        ident = keep.tile([P, P], F32, name="ident")
+        make_identity(nc, ident[:])
+
+        y_codes = keep.tile([P, E * C], U32, name="y_codes", align_bytes=64)
+        y_scales = keep.tile([P, E * C], U8, name="y_scales", align_bytes=64)
+        out_rows = out_0.rearrange("(m t) j -> m t j", t=4)
+        out_words = out_1[0].rearrange("p j d -> p (j d)").bitcast(I32)
+
+        gathered = {}
+        h_acc = {}
+        h_quant = {}
+        y_turned = {}
+        y_rows = {}
+
+        def gather(first, last):
+            tag = "hold%d" % HELD_GROUPS[first] if first in HELD_GROUPS else "words%d" % first
+            words = keep.tile([P, PASSES, (last - first) * C], U32, name="words%d" % first, tag=tag, align_bytes=64)
+            for s in range(PASSES):
+                nc.vector.tensor_copy(out=words[:, s, :], in_=x_w[:, s, :].bitcast(U32).indirect(list_slice(first, last)))
+            for e in range(first, last):
+                gathered[e] = words[:, :, (e - first) * C : (e - first + 1) * C]
+
+        def first_layer(e):
+            for first, last in GATHER_GROUPS:
+                if first == e:
+                    gather(first, last)
+            acc = sums.tile([P, H], F32, name="h_acc", tag="bank%d" % (e % SUM_BANKS))
+            for s in range(PASSES):
+                nc.tensor.matmul_mx(
+                    out=acc[:], lhsT=gathered[e][:, s, :].bitcast(FP8X4), lhsT_scale=x_planes[e][s],
+                    rhs=w1[e][s][0], rhs_scale=w1[e][s][1], start=(s == 0), stop=(s == PASSES - 1),
+                )
+            h_acc[e] = acc
+
+        def hidden(e):
+            act = ring.tile([P, H], BF16, name="act", tag="act", align_bytes=64)
+            nc.scalar.activation(
+                out=act[:].rearrange("p (u m d) -> p u m d", u=2, d=2),
+                in_=h_acc[e][:].rearrange("p (m u d) -> p u m d", u=2, d=2),
+                func=GELU,
+            )
+            pairs = act[:].bitcast(F32)
+            turned = psum.tile([P, 2, C], F32, name="h_turned", tag="h_turned")
+            for u in range(2):
+                nc.tensor.transpose(turned[:, u, :], pairs[:, u * P : (u + 1) * P], ident[:])
+            grouped = keep.tile([P, 4 * C], BF16, name="h_grouped%d" % e, tag="hold%d" % e, align_bytes=64)
+            nc.scalar.copy(
+                out=grouped[:].bitcast(F32).rearrange("p (j u) -> p j u", u=2),
+                in_=turned[:].rearrange("p u j -> p j u"),
+            )
+            codes = ring.tile([P, C], U32, name="h_codes", tag="h_codes", align_bytes=64)
+            scales = keep.tile([P, C], U8, name="h_scales%d" % e, tag="hsc%d" % e, align_bytes=64)
+            nc.vector.quantize_mx(out=codes[:].bitcast(FP8X4), scales=scales[:], in_=grouped[:])
+            h_quant[e] = (codes, scales)
+
+        def second_layer(e):
+            codes, scales = h_quant[e]
+            acc = sums.tile([P, N], F32, name="y_acc", tag="bank%d" % ((e + LAG) % SUM_BANKS))
+            nc.tensor.matmul_mx(
+                out=acc[:], lhsT=codes[:].bitcast(FP8X4), lhsT_scale=scales[:],
+                rhs=w2[e][0], rhs_scale=w2[e][1], start=True, stop=True,
+            )
+            dealt = ring.tile([P, 4, P], F32, name="dealt", tag="dealt")
+            nc.scalar.copy(out=dealt[:], in_=acc[:].rearrange("p (m t) -> p t m", t=4))
+            turned = psum.tile([P, 4, C], F32, name="y_turned", tag="y_turned")
+            for t in range(4):
+                nc.tensor.transpose(turned[:, t, :], dealt[:, t, :], ident[:])
+            y_turned[e] = turned
+
+        def hand_out(e):
+            first, last = [group for group in ROW_GROUPS if group[0] <= e < group[1]][0]
+            if e == first:
+                y_rows[first] = keep.tile([P, 4, (last - first) * C], F32, name="y_rows%d" % first)
+            rows = y_rows[first]
+            mine = rows[:, :, (e - first) * C : (e - first + 1) * C]
+            if e < HOT:
+                nc.scalar.copy(out=mine, in_=y_turned[e][:])
+            else:
+                nc.vector.tensor_copy(out=mine, in_=y_turned[e][:])
+            if e == last - 1:
+                nc.sync.dma_start(out=out_rows[:, :, first * C : last * C], in_=rows[:])
+            grouped = ring.tile([P, C, 4], BF16, name="y_grouped", tag="y_grouped", align_bytes=64)
+            nc.vector.tensor_copy(out=grouped[:], in_=mine.rearrange("p t j -> p j t"))
+            cols = slice(e * C, (e + 1) * C)
+            nc.vector.quantize_mx(
+                out=y_codes[:, cols].bitcast(FP8X4), scales=y_scales[:, cols],
+                in_=grouped[:].rearrange("p j t -> p (j t)"),
+            )
+            for first, last in CODE_GROUPS:
+                if e == last - 1:
+                    cols = slice(first * C, last * C)
+                    nc.sync.dma_start(out=out_words[:, cols], in_=y_codes[:, cols].bitcast(I32))
+
+        first_layer(0)
+        for step in range(E + LAG + 1):
+            if step < E:
+                hidden(step)
+            if 0 <= step - LAG - 1 < E:
+                hand_out(step - LAG - 1)
+            if 0 <= step - LAG < E:
+                second_layer(step - LAG)
+            if step + 1 < E:
+                first_layer(step + 1)
+
+        for q in range(4):
+            nc.scalar.dma_start(
+                out=out_2[0, 4 * q : 4 * q + 4, :].bitcast(I32),
+                in_=y_scales[32 * q : 32 * q + 4, :].bitcast(I32),
+            )

@@ -22,8 +22,9 @@ COLD = E - HOT
 LIST_COLS = C // 16
 GATHER_GROUPS = ((0, 1), (1, 2), (2, 4), (4, 6), (6, 8))
 HELD_GROUPS = {4: 0, 6: 1}
-SUM_BANKS = 4
-LAG = 2
+SUM_BANKS = 6
+SCALAR_ROUNDS_BELOW = 1
+LAG = 1
 ROW_GROUPS = ((0, 2), (2, 4), (4, 6), (6, 7), (7, 8))
 CODE_GROUPS = ((0, 6), (6, 8))
 
@@ -45,8 +46,8 @@ def tile_moe_hot_s_mlp_gelu_kernel(
             return tile
 
         def load_scales(queue, tile, rows):
-            for q in range(4):
-                queue.dma_start(out=tile[32 * q : 32 * q + 4].bitcast(I32), in_=rows[q].bitcast(I32))
+            for r in range(4):
+                queue.dma_start(out=tile[r:P:32].bitcast(I32), in_=rows[r].bitcast(I32))
 
         def load_words(name, src):
             tile = keep.tile(list(src.shape), U8, name=name, align_bytes=64)
@@ -73,14 +74,25 @@ def tile_moe_hot_s_mlp_gelu_kernel(
         x_w = keep.tile([P, PASSES, T], I32, name="x_w", align_bytes=64)
         nc.sync.dma_start(out=x_w[:], in_=x_words.rearrange("s p t d -> p s (t d)").bitcast(I32))
 
-        by_plane = "e s (q r) c -> q r (e s) c"
+        by_plane = "e s (q r) c -> r q (e s) c"
         w1h0 = load_words("w1h0", w1h_words[0].rearrange("s p i d -> p s (i d)"))
         load_scales(nc.scalar, w1h_sc, w1h_scales.rearrange(by_plane, r=4))
         w1h1 = load_words("w1h1", w1h_words[1].rearrange("s p i d -> p s (i d)"))
         w2h = load_words("w2h", w2h_words.rearrange("e s p n d -> p (e s) (n d)"))
         load_scales(nc.scalar, w2h_sc, w2h_scales.rearrange(by_plane, r=4))
         half = COLD // 2
-        w1c_first = load_words("w1c_first", w1c_words[:half].rearrange("f s p b -> p (f s) b"))
+        w1c = {}
+        w2c = {}
+
+        def load_cold_first(f):
+            w1c[f] = load_words("w1c%d" % f, w1c_words[f : f + 2].rearrange("f s p b -> p (f s) b"))
+
+        def load_cold_second(f):
+            w2c[f] = load_words("w2c%d" % f, w2c_words[f : f + 2].rearrange("f s p b -> p (f s) b"))
+
+        load_cold_first(0)
+        load_scales(nc.sync, w2c_sc, w2c_scales.rearrange(by_plane, r=4))
+        load_cold_second(0)
         load_scales(nc.sync, w1c_sc, w1c_scales.rearrange(by_plane, r=4))
 
         def list_slice(first, last):
@@ -94,15 +106,11 @@ def tile_moe_hot_s_mlp_gelu_kernel(
                 out=cold_sc[:, f * C : (f + half) * C],
                 in_=x_sc[:].indirect(list_slice(HOT + f, HOT + f + half)),
             )
-        for q in range(4):
-            nc.sync.dma_start(
-                out=moved[32 * q : 32 * q + 4, :].bitcast(I32),
-                in_=cold_sc[32 * q + 4 : 32 * q + 8, :].bitcast(I32),
-            )
-
-        w2c = load_words("w2c", w2c_words.rearrange("f s p b -> p (f s) b"))
-        load_scales(nc.sync, w2c_sc, w2c_scales.rearrange(by_plane, r=4))
-        w1c_second = load_words("w1c_second", w1c_words[half:].rearrange("f s p b -> p (f s) b"))
+        for r in range(4):
+            nc.sync.dma_start(out=moved[r:P:32, :].bitcast(I32), in_=cold_sc[4 + r : P : 32, :].bitcast(I32))
+        for f in range(2, COLD, 2):
+            load_cold_first(f)
+            load_cold_second(f)
 
         w1 = {}
         w2 = {}
@@ -110,16 +118,16 @@ def tile_moe_hot_s_mlp_gelu_kernel(
         for e, tile in enumerate((w1h0, w1h1)):
             mine = slice(e * C, (e + 1) * C)
             w1[e] = [(tile[:, s, :].bitcast(FP8X4), w1h_sc[:, PASSES * e + s, :]) for s in range(PASSES)]
-            w2[e] = (w2h[:, e, :].bitcast(FP8X4), w2h_sc[:, e, :])
+            w2[e] = (w2h[:, e, :], w2h_sc[:, e, :], I32, FP8X4)
             x_planes[e] = [hot_sc[4 * s : P, mine] for s in range(PASSES)]
         for f in range(COLD):
             mine = slice(f * C, (f + 1) * C)
-            tile = w1c_first if f < half else w1c_second
+            pair, j = f - f % 2, f % 2
             w1[HOT + f] = [
-                (tile[:, PASSES * (f % half) + s, :].bitcast(FP4X4), w1c_sc[:, PASSES * f + s, :])
+                (w1c[pair][:, PASSES * j + s, :].bitcast(FP4X4), w1c_sc[:, PASSES * f + s, :])
                 for s in range(PASSES)
             ]
-            w2[HOT + f] = (w2c[:, f, :].bitcast(FP4X4), w2c_sc[:, f, :])
+            w2[HOT + f] = (w2c[pair][:, j, :], w2c_sc[:, f, :], U16, FP4X4)
             x_planes[HOT + f] = [cold_sc[:, mine], moved[:, mine]]
 
         ident = keep.tile([P, P], F32, name="ident")
@@ -177,19 +185,29 @@ def tile_moe_hot_s_mlp_gelu_kernel(
             nc.vector.quantize_mx(out=codes[:].bitcast(FP8X4), scales=scales[:], in_=grouped[:])
             h_quant[e] = (codes, scales)
 
+        def deal(out, in_, run):
+            nc.vector.tensor_copy(
+                out=out.rearrange("p (t c i) -> p c t i", t=4, i=run),
+                in_=in_.rearrange("p (c i t) -> p c t i", t=4, i=run),
+            )
+
         def second_layer(e):
             codes, scales = h_quant[e]
-            acc = sums.tile([P, N], F32, name="y_acc", tag="bank%d" % ((e + LAG) % SUM_BANKS))
-            nc.tensor.matmul_mx(
-                out=acc[:], lhsT=codes[:].bitcast(FP8X4), lhsT_scale=scales[:],
-                rhs=w2[e][0], rhs_scale=w2[e][1], start=True, stop=True,
-            )
-            dealt = ring.tile([P, 4, P], F32, name="dealt", tag="dealt")
-            nc.scalar.copy(out=dealt[:], in_=acc[:].rearrange("p (m t) -> p t m", t=4))
-            turned = psum.tile([P, 4, C], F32, name="y_turned", tag="y_turned")
+            raw_words, raw_scales, word_dtype, mx_dtype = w2[e]
+            word_bytes = raw_words.shape[1] // N
+            words = ring.tile([P, N * word_bytes], U8, name="w2_words", tag="w2_words", align_bytes=64)
+            planes = ring.tile([P, N], U8, name="w2_scales", tag="w2_scales", align_bytes=64)
+            deal(words[:].bitcast(word_dtype), raw_words.bitcast(word_dtype), 16 // word_bytes)
+            deal(planes[:], raw_scales, 16)
+            acc = sums.tile([P, 4, C], F32, name="y_acc", tag="bank%d" % ((e + LAG) % SUM_BANKS))
             for t in range(4):
-                nc.tensor.transpose(turned[:, t, :], dealt[:, t, :], ident[:])
-            y_turned[e] = turned
+                nc.tensor.matmul_mx(
+                    out=acc[:, t, :],
+                    lhsT=words[:, t * P * word_bytes : (t + 1) * P * word_bytes].bitcast(mx_dtype),
+                    lhsT_scale=planes[:, t * P : (t + 1) * P],
+                    rhs=codes[:].bitcast(FP8X4), rhs_scale=scales[:], start=True, stop=True,
+                )
+            y_turned[e] = acc
 
         def hand_out(e):
             first, last = [group for group in ROW_GROUPS if group[0] <= e < group[1]][0]
@@ -197,14 +215,14 @@ def tile_moe_hot_s_mlp_gelu_kernel(
                 y_rows[first] = keep.tile([P, 4, (last - first) * C], F32, name="y_rows%d" % first)
             rows = y_rows[first]
             mine = rows[:, :, (e - first) * C : (e - first + 1) * C]
-            if e < HOT:
-                nc.scalar.copy(out=mine, in_=y_turned[e][:])
-            else:
-                nc.vector.tensor_copy(out=mine, in_=y_turned[e][:])
+            nc.scalar.copy(out=mine, in_=y_turned[e][:])
             if e == last - 1:
                 nc.sync.dma_start(out=out_rows[:, :, first * C : last * C], in_=rows[:])
             grouped = ring.tile([P, C, 4], BF16, name="y_grouped", tag="y_grouped", align_bytes=64)
-            nc.vector.tensor_copy(out=grouped[:], in_=mine.rearrange("p t j -> p j t"))
+            if e < SCALAR_ROUNDS_BELOW:
+                nc.scalar.copy(out=grouped[:], in_=y_turned[e][:].rearrange("p t j -> p j t"))
+            else:
+                nc.vector.tensor_copy(out=grouped[:], in_=mine.rearrange("p t j -> p j t"))
             cols = slice(e * C, (e + 1) * C)
             nc.vector.quantize_mx(
                 out=y_codes[:, cols].bitcast(FP8X4), scales=y_scales[:, cols],

@@ -20,13 +20,15 @@ P = 128
 PASSES = K // 512
 COLD = E - HOT
 LIST_COLS = C // 16
-GATHER_GROUPS = ((0, 1), (1, 2), (2, 4), (4, 6), (6, 8))
-HELD_GROUPS = {4: 0, 6: 1}
+LINE = 16
+
+GATHER_GROUPS = tuple((e, e + 1) for e in range(HOT)) + tuple((e, e + 2) for e in range(HOT, E, 2))
+HELD_GROUPS = {E - 4: 0, E - 2: 1}
 SUM_BANKS = 6
-SCALAR_ROUNDS_BELOW = 1
 LAG = 1
-ROW_GROUPS = ((0, 2), (2, 4), (4, 6), (6, 7), (7, 8))
-CODE_GROUPS = ((0, 6), (6, 8))
+SCALAR_ROUNDS_BELOW = 1
+ROW_GROUPS = tuple((e, e + 2) for e in range(0, E - 2, 2)) + ((E - 2, E - 1), (E - 1, E))
+CODE_GROUPS = ((0, E - 2), (E - 2, E))
 
 
 def tile_moe_hot_s_mlp_gelu_kernel(
@@ -45,9 +47,18 @@ def tile_moe_hot_s_mlp_gelu_kernel(
             engine.memset(tile[:].rearrange("p a c -> p (a c)").bitcast(I32), 0)
             return tile
 
-        def load_scales(queue, tile, rows):
+        def load_side_by_side(tile, scales):
+            rows = scales.rearrange("e s (q r) c -> r q (e s) c", r=4)
             for r in range(4):
-                queue.dma_start(out=tile[r:P:32].bitcast(I32), in_=rows[r].bitcast(I32))
+                nc.sync.dma_start(out=tile[r:P:32].bitcast(I32), in_=rows[r].bitcast(I32))
+
+        def load_packed(tile, scales):
+            planes = scales.rearrange("e s b c -> (e s) b c")
+            for q in range(4):
+                nc.scalar.dma_start(
+                    out=tile[32 * q : 32 * q + 4 * planes.shape[0], :].bitcast(I32),
+                    in_=planes[:, 4 * q : 4 * q + 4, :].bitcast(I32),
+                )
 
         def load_words(name, src):
             tile = keep.tile(list(src.shape), U8, name=name, align_bytes=64)
@@ -56,12 +67,14 @@ def tile_moe_hot_s_mlp_gelu_kernel(
 
         x_sc = keep.tile([P, T], U8, name="x_sc", align_bytes=64)
         nc.gpsimd.memset(x_sc[:].bitcast(I32), 0)
-        w1h_sc = scale_tile(nc.gpsimd, "w1h_sc", HOT * PASSES)
-        w2h_sc = scale_tile(nc.vector, "w2h_sc", HOT)
+        w1h_sc = keep.tile([P, H], U8, name="w1h_sc", align_bytes=64)
+        nc.gpsimd.memset(w1h_sc[:].bitcast(I32), 0)
+        w2h_sc = keep.tile([P, N], U8, name="w2h_sc", align_bytes=64)
+        nc.gpsimd.memset(w2h_sc[:].bitcast(I32), 0)
         w1c_sc = scale_tile(nc.vector, "w1c_sc", COLD * PASSES)
         w2c_sc = scale_tile(nc.gpsimd, "w2c_sc", COLD)
-        moved = keep.tile([P, COLD * C], U8, name="moved", align_bytes=64)
-        nc.vector.memset(moved[:].bitcast(I32), 0)
+        cold_sc_pass1 = keep.tile([P, COLD * C], U8, name="cold_sc_pass1", align_bytes=64)
+        nc.vector.memset(cold_sc_pass1[:].bitcast(I32), 0)
 
         offsets = keep.tile([P, E * LIST_COLS], U16, name="offsets")
         nc.sync.dma_start(offsets[:], offs)
@@ -74,13 +87,11 @@ def tile_moe_hot_s_mlp_gelu_kernel(
         x_w = keep.tile([P, PASSES, T], I32, name="x_w", align_bytes=64)
         nc.sync.dma_start(out=x_w[:], in_=x_words.rearrange("s p t d -> p s (t d)").bitcast(I32))
 
-        by_plane = "e s (q r) c -> r q (e s) c"
         w1h0 = load_words("w1h0", w1h_words[0].rearrange("s p i d -> p s (i d)"))
-        load_scales(nc.scalar, w1h_sc, w1h_scales.rearrange(by_plane, r=4))
+        load_packed(w1h_sc, w1h_scales)
         w1h1 = load_words("w1h1", w1h_words[1].rearrange("s p i d -> p s (i d)"))
         w2h = load_words("w2h", w2h_words.rearrange("e s p n d -> p (e s) (n d)"))
-        load_scales(nc.scalar, w2h_sc, w2h_scales.rearrange(by_plane, r=4))
-        half = COLD // 2
+        load_packed(w2h_sc, w2h_scales)
         w1c = {}
         w2c = {}
 
@@ -91,13 +102,14 @@ def tile_moe_hot_s_mlp_gelu_kernel(
             w2c[f] = load_words("w2c%d" % f, w2c_words[f : f + 2].rearrange("f s p b -> p (f s) b"))
 
         load_cold_first(0)
-        load_scales(nc.sync, w2c_sc, w2c_scales.rearrange(by_plane, r=4))
+        load_side_by_side(w2c_sc, w2c_scales)
         load_cold_second(0)
-        load_scales(nc.sync, w1c_sc, w1c_scales.rearrange(by_plane, r=4))
+        load_side_by_side(w1c_sc, w1c_scales)
 
         def list_slice(first, last):
             return offsets[:, first * LIST_COLS : last * LIST_COLS]
 
+        half = COLD // 2
         hot_sc = keep.tile([P, HOT * C], U8, name="hot_sc", align_bytes=64)
         nc.vector.tensor_copy(out=hot_sc[:], in_=x_sc[:].indirect(list_slice(0, HOT)))
         cold_sc = keep.tile([P, COLD * C], U8, name="cold_sc", align_bytes=64)
@@ -107,9 +119,12 @@ def tile_moe_hot_s_mlp_gelu_kernel(
                 in_=x_sc[:].indirect(list_slice(HOT + f, HOT + f + half)),
             )
         for r in range(4):
-            nc.sync.dma_start(out=moved[r:P:32, :].bitcast(I32), in_=cold_sc[4 + r : P : 32, :].bitcast(I32))
+            nc.sync.dma_start(
+                out=cold_sc_pass1[r:P:32, :].bitcast(I32), in_=cold_sc[4 + r : P : 32, :].bitcast(I32)
+            )
         for f in range(2, COLD, 2):
             load_cold_first(f)
+        for f in range(2, COLD, 2):
             load_cold_second(f)
 
         w1 = {}
@@ -117,8 +132,8 @@ def tile_moe_hot_s_mlp_gelu_kernel(
         x_planes = {}
         for e, tile in enumerate((w1h0, w1h1)):
             mine = slice(e * C, (e + 1) * C)
-            w1[e] = [(tile[:, s, :].bitcast(FP8X4), w1h_sc[:, PASSES * e + s, :]) for s in range(PASSES)]
-            w2[e] = (w2h[:, e, :], w2h_sc[:, e, :], I32, FP8X4)
+            w1[e] = [(tile[:, s, :].bitcast(FP8X4), w1h_sc[4 * (PASSES * e + s) : P, :]) for s in range(PASSES)]
+            w2[e] = (w2h[:, e, :], I32, FP8X4)
             x_planes[e] = [hot_sc[4 * s : P, mine] for s in range(PASSES)]
         for f in range(COLD):
             mine = slice(f * C, (f + 1) * C)
@@ -127,8 +142,8 @@ def tile_moe_hot_s_mlp_gelu_kernel(
                 (w1c[pair][:, PASSES * j + s, :].bitcast(FP4X4), w1c_sc[:, PASSES * f + s, :])
                 for s in range(PASSES)
             ]
-            w2[HOT + f] = (w2c[pair][:, j, :], w2c_sc[:, f, :], U16, FP4X4)
-            x_planes[HOT + f] = [cold_sc[:, mine], moved[:, mine]]
+            w2[HOT + f] = (w2c[pair][:, j, :], U16, FP4X4)
+            x_planes[HOT + f] = [cold_sc[:, mine], cold_sc_pass1[:, mine]]
 
         ident = keep.tile([P, P], F32, name="ident")
         make_identity(nc, ident[:])
@@ -141,14 +156,16 @@ def tile_moe_hot_s_mlp_gelu_kernel(
         gathered = {}
         h_acc = {}
         h_quant = {}
-        y_turned = {}
+        y_acc = {}
         y_rows = {}
+        w2h_dealt = keep.tile([P, N], U8, name="w2h_dealt", align_bytes=64)
 
         def gather(first, last):
             tag = "hold%d" % HELD_GROUPS[first] if first in HELD_GROUPS else "words%d" % first
             words = keep.tile([P, PASSES, (last - first) * C], U32, name="words%d" % first, tag=tag, align_bytes=64)
             for s in range(PASSES):
-                nc.vector.tensor_copy(out=words[:, s, :], in_=x_w[:, s, :].bitcast(U32).indirect(list_slice(first, last)))
+                window = x_w[:, s, :].bitcast(U32)
+                nc.vector.tensor_copy(out=words[:, s, :], in_=window.indirect(list_slice(first, last)))
             for e in range(first, last):
                 gathered[e] = words[:, :, (e - first) * C : (e - first + 1) * C]
 
@@ -181,7 +198,7 @@ def tile_moe_hot_s_mlp_gelu_kernel(
                 in_=turned[:].rearrange("p u j -> p j u"),
             )
             codes = ring.tile([P, C], U32, name="h_codes", tag="h_codes", align_bytes=64)
-            scales = keep.tile([P, C], U8, name="h_scales%d" % e, tag="hsc%d" % e, align_bytes=64)
+            scales = keep.tile([P, C], U8, name="h_scales%d" % e, align_bytes=64)
             nc.vector.quantize_mx(out=codes[:].bitcast(FP8X4), scales=scales[:], in_=grouped[:])
             h_quant[e] = (codes, scales)
 
@@ -193,21 +210,26 @@ def tile_moe_hot_s_mlp_gelu_kernel(
 
         def second_layer(e):
             codes, scales = h_quant[e]
-            raw_words, raw_scales, word_dtype, mx_dtype = w2[e]
+            raw_words, word_dtype, mx_dtype = w2[e]
             word_bytes = raw_words.shape[1] // N
             words = ring.tile([P, N * word_bytes], U8, name="w2_words", tag="w2_words", align_bytes=64)
-            planes = ring.tile([P, N], U8, name="w2_scales", tag="w2_scales", align_bytes=64)
-            deal(words[:].bitcast(word_dtype), raw_words.bitcast(word_dtype), 16 // word_bytes)
-            deal(planes[:], raw_scales, 16)
+            deal(words[:].bitcast(word_dtype), raw_words.bitcast(word_dtype), LINE // word_bytes)
+            if e == 0:
+                deal(w2h_dealt[:], w2h_sc[:], LINE)
+            if e < HOT:
+                plane = w2h_dealt[4 * e : P, :]
+            else:
+                plane = ring.tile([P, N], U8, name="w2_scales", tag="w2_scales", align_bytes=64)
+                deal(plane[:], w2c_sc[:, e - HOT, :], LINE)
             acc = sums.tile([P, 4, C], F32, name="y_acc", tag="bank%d" % ((e + LAG) % SUM_BANKS))
             for t in range(4):
                 nc.tensor.matmul_mx(
                     out=acc[:, t, :],
                     lhsT=words[:, t * P * word_bytes : (t + 1) * P * word_bytes].bitcast(mx_dtype),
-                    lhsT_scale=planes[:, t * P : (t + 1) * P],
+                    lhsT_scale=plane[:, t * P : (t + 1) * P],
                     rhs=codes[:].bitcast(FP8X4), rhs_scale=scales[:], start=True, stop=True,
                 )
-            y_turned[e] = acc
+            y_acc[e] = acc
 
         def hand_out(e):
             first, last = [group for group in ROW_GROUPS if group[0] <= e < group[1]][0]
@@ -215,12 +237,12 @@ def tile_moe_hot_s_mlp_gelu_kernel(
                 y_rows[first] = keep.tile([P, 4, (last - first) * C], F32, name="y_rows%d" % first)
             rows = y_rows[first]
             mine = rows[:, :, (e - first) * C : (e - first + 1) * C]
-            nc.scalar.copy(out=mine, in_=y_turned[e][:])
+            nc.scalar.copy(out=mine, in_=y_acc[e][:])
             if e == last - 1:
                 nc.sync.dma_start(out=out_rows[:, :, first * C : last * C], in_=rows[:])
             grouped = ring.tile([P, C, 4], BF16, name="y_grouped", tag="y_grouped", align_bytes=64)
             if e < SCALAR_ROUNDS_BELOW:
-                nc.scalar.copy(out=grouped[:], in_=y_turned[e][:].rearrange("p t j -> p j t"))
+                nc.scalar.copy(out=grouped[:], in_=y_acc[e][:].rearrange("p t j -> p j t"))
             else:
                 nc.vector.tensor_copy(out=grouped[:], in_=mine.rearrange("p t j -> p j t"))
             cols = slice(e * C, (e + 1) * C)
@@ -228,10 +250,10 @@ def tile_moe_hot_s_mlp_gelu_kernel(
                 out=y_codes[:, cols].bitcast(FP8X4), scales=y_scales[:, cols],
                 in_=grouped[:].rearrange("p j t -> p (j t)"),
             )
-            for first, last in CODE_GROUPS:
-                if e == last - 1:
-                    cols = slice(first * C, last * C)
-                    nc.sync.dma_start(out=out_words[:, cols], in_=y_codes[:, cols].bitcast(I32))
+            for code_first, code_last in CODE_GROUPS:
+                if e == code_last - 1:
+                    done = slice(code_first * C, code_last * C)
+                    nc.sync.dma_start(out=out_words[:, done], in_=y_codes[:, done].bitcast(I32))
 
         first_layer(0)
         for step in range(E + LAG + 1):
@@ -245,7 +267,8 @@ def tile_moe_hot_s_mlp_gelu_kernel(
                 first_layer(step + 1)
 
         for q in range(4):
-            nc.scalar.dma_start(
+            queue = nc.scalar if q < 2 else nc.sync
+            queue.dma_start(
                 out=out_2[0, 4 * q : 4 * q + 4, :].bitcast(I32),
                 in_=y_scales[32 * q : 32 * q + 4, :].bitcast(I32),
             )

@@ -22,13 +22,18 @@ COLD = E - HOT
 LIST_COLS = C // 16
 LINE = 16
 
-GATHER_GROUPS = tuple((e, e + 1) for e in range(HOT)) + tuple((e, e + 2) for e in range(HOT, E, 2))
-HELD_GROUPS = {E - 4: 0, E - 2: 1}
-SUM_BANKS = 6
-LAG = 1
-SCALAR_ROUNDS_BELOW = 1
-ROW_GROUPS = tuple((e, e + 2) for e in range(0, E - 2, 2)) + ((E - 2, E - 1), (E - 1, E))
-CODE_GROUPS = ((0, E - 2), (E - 2, E))
+ORDER = tuple(range(HOT, E)) + tuple(range(HOT))
+PLACE = {e: k for k, e in enumerate(ORDER)}
+X_SC_AT = 8192 * (E + 1) + 2048 - 64
+W1_AT = 2048
+DEALT_END = W1_AT + 64
+CODES_AT = DEALT_END
+GROUPED_AT = CODES_AT + 512
+ROUNDED_AT = W1_AT + 2048 - 64
+SLOT = 8192
+SCALAR_ROUNDS = (0,)
+ROW_GROUPS = ((2, 4), (4, 5), (5, 6), (6, 7), (7, 8), (0, 1), (1, 2))
+CODE_GROUPS = ((2, 6), (6, 8), (0, 2))
 
 
 def tile_moe_hot_s_mlp_gelu_kernel(
@@ -38,169 +43,80 @@ def tile_moe_hot_s_mlp_gelu_kernel(
     nc = tc.nc
     with ExitStack() as ctx:
         keep = ctx.enter_context(tc.tile_pool(name="keep", bufs=1))
+        placed = ctx.enter_context(tc.tile_pool(name="placed", bufs=1))
         ring = ctx.enter_context(tc.tile_pool(name="ring", bufs=3))
+        psc = ctx.enter_context(tc.tile_pool(name="psc", bufs=3))
         psum = ctx.enter_context(tc.psum_pool(name="psum", bufs=2))
-        sums = ctx.enter_context(tc.psum_pool(name="sums", bufs=1))
+        sums = ctx.enter_context(tc.psum_pool(name="sums", bufs=3))
 
-        def scale_tile(engine, name, planes):
-            tile = keep.tile([P, planes, 512], U8, name=name, align_bytes=64)
-            engine.memset(tile[:].rearrange("p a c -> p (a c)").bitcast(I32), 0)
-            return tile
-
-        def load_side_by_side(tile, scales):
-            rows = scales.rearrange("e s (q r) c -> r q (e s) c", r=4)
-            for r in range(4):
-                nc.sync.dma_start(out=tile[r:P:32].bitcast(I32), in_=rows[r].bitcast(I32))
-
-        def load_packed(tile, scales):
-            planes = scales.rearrange("e s b c -> (e s) b c")
-            for q in range(4):
-                nc.scalar.dma_start(
-                    out=tile[32 * q : 32 * q + 4 * planes.shape[0], :].bitcast(I32),
-                    in_=planes[:, 4 * q : 4 * q + 4, :].bitcast(I32),
-                )
-
-        def load_words(name, src):
-            tile = keep.tile(list(src.shape), U8, name=name, align_bytes=64)
-            nc.sync.dma_start(out=tile[:].bitcast(I32), in_=src.bitcast(I32))
-            return tile
-
-        x_sc = keep.tile([P, T], U8, name="x_sc", align_bytes=64)
+        x_sc = placed.tile([P, T], U8, name="x_sc", align_bytes=64, offset=X_SC_AT)
         nc.gpsimd.memset(x_sc[:].bitcast(I32), 0)
+        zero = keep.tile([P, 1], F32, name="zero")
+        nc.gpsimd.memset(zero[:], 0.0)
+        ident = keep.tile([P, P], F32, name="ident")
+        make_identity(nc, ident[:])
         w1h_sc = keep.tile([P, H], U8, name="w1h_sc", align_bytes=64)
-        nc.gpsimd.memset(w1h_sc[:].bitcast(I32), 0)
+        nc.vector.memset(w1h_sc[:].bitcast(I32), 0)
         w2h_sc = keep.tile([P, N], U8, name="w2h_sc", align_bytes=64)
-        nc.gpsimd.memset(w2h_sc[:].bitcast(I32), 0)
-        w1c_sc = scale_tile(nc.vector, "w1c_sc", COLD * PASSES)
-        w2c_sc = scale_tile(nc.gpsimd, "w2c_sc", COLD)
+        nc.vector.memset(w2h_sc[:].bitcast(I32), 0)
+        w1c_sc = keep.tile([P, COLD * PASSES, H], U8, name="w1c_sc", align_bytes=64)
+        nc.vector.memset(w1c_sc[:].rearrange("p a c -> p (a c)").bitcast(I32), 0)
         cold_sc_pass1 = keep.tile([P, COLD * C], U8, name="cold_sc_pass1", align_bytes=64)
         nc.vector.memset(cold_sc_pass1[:].bitcast(I32), 0)
+        w2c_sc = keep.tile([P, COLD, N], U8, name="w2c_sc", align_bytes=64)
+        nc.vector.memset(w2c_sc[:].rearrange("p a c -> p (a c)").bitcast(I32), 0)
 
         offsets = keep.tile([P, E * LIST_COLS], U16, name="offsets")
         nc.sync.dma_start(offsets[:], offs)
-        for q in range(4):
-            queue = nc.sync if q < 2 else nc.scalar
+        x_w = keep.tile([P, PASSES, T], I32, name="x_w", align_bytes=64)
+
+        def load_token_scales(q, queue):
             queue.dma_start(
                 out=x_sc[32 * q : 32 * q + 4 * PASSES, :].bitcast(I32),
                 in_=x_scales[:, 4 * q : 4 * q + 4, :].bitcast(I32),
             )
-        x_w = keep.tile([P, PASSES, T], I32, name="x_w", align_bytes=64)
-        nc.sync.dma_start(out=x_w[:], in_=x_words.rearrange("s p t d -> p s (t d)").bitcast(I32))
 
-        w1h0 = load_words("w1h0", w1h_words[0].rearrange("s p i d -> p s (i d)"))
-        load_packed(w1h_sc, w1h_scales)
-        w1h1 = load_words("w1h1", w1h_words[1].rearrange("s p i d -> p s (i d)"))
-        w2h = load_words("w2h", w2h_words.rearrange("e s p n d -> p (e s) (n d)"))
-        load_packed(w2h_sc, w2h_scales)
-        w1c = {}
-        w2c = {}
+        w1_raw = {}
+        w2_raw = {}
 
-        def load_cold_first(f):
-            w1c[f] = load_words("w1c%d" % f, w1c_words[f : f + 2].rearrange("f s p b -> p (f s) b"))
+        def load_first(e, queue, count=1):
+            if e < HOT:
+                src = w1h_words[e].rearrange("s p i d -> p s (i d)")
+            else:
+                src = w1c_words[e - HOT : e - HOT + count].rearrange("f s p b -> p (f s) b")
+            last = e + count - 1
+            tile = placed.tile(list(src.shape), U8, name="w1_%d" % e, align_bytes=64, offset=SLOT * PLACE[last] + W1_AT)
+            queue.dma_start(out=tile[:].bitcast(I32), in_=src.bitcast(I32))
+            for j in range(count):
+                w1_raw[e + j] = tile[:, PASSES * j : PASSES * (j + 1), :]
 
-        def load_cold_second(f):
-            w2c[f] = load_words("w2c%d" % f, w2c_words[f : f + 2].rearrange("f s p b -> p (f s) b"))
+        def load_second(e, queue):
+            if e < HOT:
+                src = w2h_words[e].rearrange("s p n d -> p s (n d)")
+            else:
+                src = w2c_words[e - HOT : e - HOT + 2].rearrange("f s p b -> p (f s) b")
+            tile = keep.tile(list(src.shape), U8, name="w2_%d" % e, align_bytes=64)
+            queue.dma_start(out=tile[:].bitcast(I32), in_=src.bitcast(I32))
+            for j in range(src.shape[1]):
+                w2_raw[e + j] = tile[:, j, :]
 
-        load_cold_first(0)
-        load_side_by_side(w2c_sc, w2c_scales)
-        load_cold_second(0)
-        load_side_by_side(w1c_sc, w1c_scales)
+        def load_cold_first_scales(r, queue):
+            rows = w1c_scales.rearrange("e s (q r) c -> r q (e s) c", r=4)
+            queue.dma_start(out=w1c_sc[r:P:32].bitcast(I32), in_=rows[r].bitcast(I32))
+
+        def load_hot_scales(tile, scales, q, queue):
+            planes = scales.rearrange("e s b c -> (e s) b c")
+            queue.dma_start(
+                out=tile[32 * q : 32 * q + 4 * planes.shape[0], :].bitcast(I32),
+                in_=planes[:, 4 * q : 4 * q + 4, :].bitcast(I32),
+            )
+
+        def load_cold_second_scales(r, queue):
+            rows = w2c_scales.rearrange("e s (q r) c -> r q (e s) c", r=4)
+            queue.dma_start(out=w2c_sc[r:P:32].bitcast(I32), in_=rows[r].bitcast(I32))
 
         def list_slice(first, last):
             return offsets[:, first * LIST_COLS : last * LIST_COLS]
-
-        half = COLD // 2
-        hot_sc = keep.tile([P, HOT * C], U8, name="hot_sc", align_bytes=64)
-        nc.vector.tensor_copy(out=hot_sc[:], in_=x_sc[:].indirect(list_slice(0, HOT)))
-        cold_sc = keep.tile([P, COLD * C], U8, name="cold_sc", align_bytes=64)
-        for f in range(0, COLD, half):
-            nc.vector.tensor_copy(
-                out=cold_sc[:, f * C : (f + half) * C],
-                in_=x_sc[:].indirect(list_slice(HOT + f, HOT + f + half)),
-            )
-        for r in range(4):
-            nc.sync.dma_start(
-                out=cold_sc_pass1[r:P:32, :].bitcast(I32), in_=cold_sc[4 + r : P : 32, :].bitcast(I32)
-            )
-        for f in range(2, COLD, 2):
-            load_cold_first(f)
-        for f in range(2, COLD, 2):
-            load_cold_second(f)
-
-        w1 = {}
-        w2 = {}
-        x_planes = {}
-        for e, tile in enumerate((w1h0, w1h1)):
-            mine = slice(e * C, (e + 1) * C)
-            w1[e] = [(tile[:, s, :].bitcast(FP8X4), w1h_sc[4 * (PASSES * e + s) : P, :]) for s in range(PASSES)]
-            w2[e] = (w2h[:, e, :], I32, FP8X4)
-            x_planes[e] = [hot_sc[4 * s : P, mine] for s in range(PASSES)]
-        for f in range(COLD):
-            mine = slice(f * C, (f + 1) * C)
-            pair, j = f - f % 2, f % 2
-            w1[HOT + f] = [
-                (w1c[pair][:, PASSES * j + s, :].bitcast(FP4X4), w1c_sc[:, PASSES * f + s, :])
-                for s in range(PASSES)
-            ]
-            w2[HOT + f] = (w2c[pair][:, j, :], U16, FP4X4)
-            x_planes[HOT + f] = [cold_sc[:, mine], cold_sc_pass1[:, mine]]
-
-        ident = keep.tile([P, P], F32, name="ident")
-        make_identity(nc, ident[:])
-
-        y_codes = keep.tile([P, E * C], U32, name="y_codes", align_bytes=64)
-        y_scales = keep.tile([P, E * C], U8, name="y_scales", align_bytes=64)
-        out_rows = out_0.rearrange("(m t) j -> m t j", t=4)
-        out_words = out_1[0].rearrange("p j d -> p (j d)").bitcast(I32)
-
-        gathered = {}
-        h_acc = {}
-        h_quant = {}
-        y_acc = {}
-        y_rows = {}
-        w2h_dealt = keep.tile([P, N], U8, name="w2h_dealt", align_bytes=64)
-
-        def gather(first, last):
-            tag = "hold%d" % HELD_GROUPS[first] if first in HELD_GROUPS else "words%d" % first
-            words = keep.tile([P, PASSES, (last - first) * C], U32, name="words%d" % first, tag=tag, align_bytes=64)
-            for s in range(PASSES):
-                window = x_w[:, s, :].bitcast(U32)
-                nc.vector.tensor_copy(out=words[:, s, :], in_=window.indirect(list_slice(first, last)))
-            for e in range(first, last):
-                gathered[e] = words[:, :, (e - first) * C : (e - first + 1) * C]
-
-        def first_layer(e):
-            for first, last in GATHER_GROUPS:
-                if first == e:
-                    gather(first, last)
-            acc = sums.tile([P, H], F32, name="h_acc", tag="bank%d" % (e % SUM_BANKS))
-            for s in range(PASSES):
-                nc.tensor.matmul_mx(
-                    out=acc[:], lhsT=gathered[e][:, s, :].bitcast(FP8X4), lhsT_scale=x_planes[e][s],
-                    rhs=w1[e][s][0], rhs_scale=w1[e][s][1], start=(s == 0), stop=(s == PASSES - 1),
-                )
-            h_acc[e] = acc
-
-        def hidden(e):
-            act = ring.tile([P, H], BF16, name="act", tag="act", align_bytes=64)
-            nc.scalar.activation(
-                out=act[:].rearrange("p (u m d) -> p u m d", u=2, d=2),
-                in_=h_acc[e][:].rearrange("p (m u d) -> p u m d", u=2, d=2),
-                func=GELU,
-            )
-            pairs = act[:].bitcast(F32)
-            turned = psum.tile([P, 2, C], F32, name="h_turned", tag="h_turned")
-            for u in range(2):
-                nc.tensor.transpose(turned[:, u, :], pairs[:, u * P : (u + 1) * P], ident[:])
-            grouped = keep.tile([P, 4 * C], BF16, name="h_grouped%d" % e, tag="hold%d" % e, align_bytes=64)
-            nc.scalar.copy(
-                out=grouped[:].bitcast(F32).rearrange("p (j u) -> p j u", u=2),
-                in_=turned[:].rearrange("p u j -> p j u"),
-            )
-            codes = ring.tile([P, C], U32, name="h_codes", tag="h_codes", align_bytes=64)
-            scales = keep.tile([P, C], U8, name="h_scales%d" % e, align_bytes=64)
-            nc.vector.quantize_mx(out=codes[:].bitcast(FP8X4), scales=scales[:], in_=grouped[:])
-            h_quant[e] = (codes, scales)
 
         def deal(out, in_, run):
             nc.vector.tensor_copy(
@@ -208,20 +124,159 @@ def tile_moe_hot_s_mlp_gelu_kernel(
                 in_=in_.rearrange("p (c i t) -> p c t i", t=4, i=run),
             )
 
+        hot_sc = keep.tile([P, HOT * C], U8, name="hot_sc", align_bytes=64)
+        cold_sc = keep.tile([P, COLD * C], U8, name="cold_sc", align_bytes=64)
+        gathered = {}
+
+        def gather_cold_scales():
+            half = COLD // 2
+            for f in range(0, COLD, half):
+                nc.vector.tensor_copy(
+                    out=cold_sc[:, f * C : (f + half) * C],
+                    in_=x_sc[:].indirect(list_slice(HOT + f, HOT + f + half)),
+                )
+
+        def move_token_scales(r, queue):
+            queue.dma_start(out=cold_sc_pass1[r:P:32, :].bitcast(I32), in_=cold_sc[4 + r : P : 32, :].bitcast(I32))
+
+        def gather(pairs, passes, offset):
+            words = placed.tile(
+                [P, len(pairs), len(passes), 2 * C], U32, name="words%d_%d" % (pairs[0], passes[0]),
+                align_bytes=64, offset=offset,
+            )
+            for b, first in enumerate(pairs):
+                for a, s in enumerate(passes):
+                    window = x_w[:, s, :].bitcast(U32)
+                    nc.vector.tensor_copy(out=words[:, b, a, :], in_=window.indirect(list_slice(first, first + 2)))
+                    for j in range(2):
+                        gathered[first + j, s] = words[:, b, a, j * C : (j + 1) * C]
+
+        nc.scalar.dma_start(out=x_w[:], in_=x_words.rearrange("s p t d -> p s (t d)").bitcast(I32))
+        load_token_scales(0, nc.sync)
+        load_token_scales(1, nc.sync)
+        load_token_scales(2, nc.sync)
+        load_token_scales(3, nc.sync)
+        no_bias = keep.tile([P, 1], F32, name="no_bias")
+        nc.scalar.activation(out=no_bias[:], in_=zero[:], func=GELU)
+        load_hot_scales(w1h_sc, w1h_scales, 0, nc.gpsimd)
+        load_hot_scales(w1h_sc, w1h_scales, 1, nc.gpsimd)
+        load_hot_scales(w1h_sc, w1h_scales, 2, nc.gpsimd)
+        load_hot_scales(w1h_sc, w1h_scales, 3, nc.gpsimd)
+        load_hot_scales(w2h_sc, w2h_scales, 0, nc.gpsimd)
+        load_hot_scales(w2h_sc, w2h_scales, 1, nc.gpsimd)
+        load_hot_scales(w2h_sc, w2h_scales, 2, nc.gpsimd)
+        load_hot_scales(w2h_sc, w2h_scales, 3, nc.gpsimd)
+        load_first(2, nc.sync)
+        load_first(3, nc.sync)
+        load_cold_first_scales(0, nc.scalar)
+        load_cold_first_scales(1, nc.scalar)
+        load_cold_first_scales(2, nc.scalar)
+        load_cold_first_scales(3, nc.scalar)
+        load_first(4, nc.sync)
+        gather_cold_scales()
+        move_token_scales(0, nc.sync)
+        move_token_scales(1, nc.sync)
+        move_token_scales(2, nc.sync)
+        move_token_scales(3, nc.sync)
+        nc.vector.tensor_copy(out=hot_sc[:], in_=x_sc[:].indirect(list_slice(0, HOT)))
+        gather((2,), (1, 0), X_SC_AT + 64 - 2048)
+        gather((4, 6), (1, 0), X_SC_AT + 64)
+        load_cold_second_scales(0, nc.sync)
+        load_cold_second_scales(1, nc.sync)
+        load_cold_second_scales(2, nc.sync)
+        load_cold_second_scales(3, nc.sync)
+        load_second(2, nc.sync)
+        load_first(5, nc.sync)
+        load_first(6, nc.sync)
+        load_second(4, nc.sync)
+        load_first(7, nc.sync)
+        load_second(6, nc.sync)
+        load_first(0, nc.sync)
+        load_second(0, nc.sync)
+        load_first(1, nc.sync)
+        load_second(1, nc.sync)
+
+        y_codes = keep.tile([P, E * C], U32, name="y_codes", align_bytes=64)
+        y_scales = keep.tile([P, E * C], U8, name="y_scales", align_bytes=64)
+        out_rows = out_0.rearrange("(m t) j -> m t j", t=4)
+        out_words = out_1[0].rearrange("p j d -> p (j d)").bitcast(I32)
+
+        h_acc = {}
+        h_turned = {}
+        h_grouped = {}
+        h_quant = {}
+        dealt = {}
+        planes = {}
+        y_acc = {}
+        y_rows = {}
+        y_mine = {}
+        y_grouped = {}
+
+        def first_layer(e):
+            acc = sums.tile([P, H], F32, name="h_acc", tag="h_acc")
+            for s in reversed(range(PASSES)):
+                if e < HOT:
+                    words, plane = w1_raw[e][:, s, :].bitcast(FP8X4), w1h_sc[4 * (PASSES * e + s) : P, :]
+                    x_plane = hot_sc[4 * s : P, e * C : (e + 1) * C]
+                else:
+                    f = e - HOT
+                    words, plane = w1_raw[e][:, s, :].bitcast(FP4X4), w1c_sc[:, PASSES * f + s, :]
+                    x_plane = (cold_sc, cold_sc_pass1)[s][:, f * C : (f + 1) * C]
+                nc.tensor.matmul_mx(
+                    out=acc[:], lhsT=gathered[e, s].bitcast(FP8X4), lhsT_scale=x_plane,
+                    rhs=words, rhs_scale=plane, start=(s == PASSES - 1), stop=(s == 0),
+                )
+            h_acc[e] = acc
+
+        def activate(e):
+            act = ring.tile([P, H], BF16, name="act", tag="act", align_bytes=64)
+            nc.scalar.activation(
+                out=act[:].rearrange("p (u m d) -> p u m d", u=2, d=2),
+                in_=h_acc[e][:].rearrange("p (m u d) -> p u m d", u=2, d=2),
+                func=GELU,
+                bias=no_bias[:],
+            )
+            pairs = act[:].bitcast(F32)
+            turned = psum.tile([P, 2, C], F32, name="h_turned", tag="h_turned")
+            for u in range(2):
+                nc.tensor.transpose(turned[:, u, :], pairs[:, u * P : (u + 1) * P], ident[:])
+            h_turned[e] = turned
+
+        def group_hidden(e):
+            grouped = placed.tile(
+                [P, 4 * C], BF16, name="h_grouped%d" % e, align_bytes=64, offset=SLOT * (PLACE[e] + 1) + GROUPED_AT
+            )
+            nc.scalar.copy(
+                out=grouped[:].bitcast(F32).rearrange("p (j u) -> p j u", u=2),
+                in_=h_turned[e][:].rearrange("p u j -> p j u"),
+            )
+            h_grouped[e] = grouped
+
+        def quantise_hidden(e):
+            codes = keep.tile([P, C], U32, name="h_codes%d" % e, align_bytes=64)
+            scales = keep.tile([P, C], U8, name="h_scales%d" % e, align_bytes=64)
+            nc.vector.quantize_mx(out=codes[:].bitcast(FP8X4), scales=scales[:], in_=h_grouped[e][:])
+            h_quant[e] = (codes, scales)
+
+        def deal_second(e):
+            word_dtype, word_bytes, mx_dtype = (I32, 4, FP8X4) if e < HOT else (U16, 2, FP4X4)
+            words = ring.tile([P, N * word_bytes], U8, name="w2_words", tag="w2_words", align_bytes=64)
+            deal(words[:].bitcast(word_dtype), w2_raw[e].bitcast(word_dtype), LINE // word_bytes)
+            dealt[e] = (words, word_bytes, mx_dtype)
+
+        def deal_scales(e):
+            if e != 1:
+                tile = psc.tile([P, N], U8, name="w2_scales", tag="w2_scales", align_bytes=64)
+                deal(tile[:], w2h_sc[:] if e == 0 else w2c_sc[:, e - HOT, :], LINE)
+                planes[e] = tile[:]
+            if e == 0:
+                planes[1] = tile[4:P, :]
+
         def second_layer(e):
             codes, scales = h_quant[e]
-            raw_words, word_dtype, mx_dtype = w2[e]
-            word_bytes = raw_words.shape[1] // N
-            words = ring.tile([P, N * word_bytes], U8, name="w2_words", tag="w2_words", align_bytes=64)
-            deal(words[:].bitcast(word_dtype), raw_words.bitcast(word_dtype), LINE // word_bytes)
-            if e == 0:
-                deal(w2h_dealt[:], w2h_sc[:], LINE)
-            if e < HOT:
-                plane = w2h_dealt[4 * e : P, :]
-            else:
-                plane = ring.tile([P, N], U8, name="w2_scales", tag="w2_scales", align_bytes=64)
-                deal(plane[:], w2c_sc[:, e - HOT, :], LINE)
-            acc = sums.tile([P, 4, C], F32, name="y_acc", tag="bank%d" % ((e + LAG) % SUM_BANKS))
+            words, word_bytes, mx_dtype = dealt[e]
+            plane = planes[e]
+            acc = sums.tile([P, 4, C], F32, name="y_acc", tag="y_acc")
             for t in range(4):
                 nc.tensor.matmul_mx(
                     out=acc[:, t, :],
@@ -240,31 +295,51 @@ def tile_moe_hot_s_mlp_gelu_kernel(
             nc.scalar.copy(out=mine, in_=y_acc[e][:])
             if e == last - 1:
                 nc.sync.dma_start(out=out_rows[:, :, first * C : last * C], in_=rows[:])
-            grouped = ring.tile([P, C, 4], BF16, name="y_grouped", tag="y_grouped", align_bytes=64)
-            if e < SCALAR_ROUNDS_BELOW:
+            y_mine[e] = mine
+            if PLACE[e] in SCALAR_ROUNDS:
+                grouped = keep.tile([P, C, 4], BF16, name="y_grouped%d" % e, align_bytes=64)
                 nc.scalar.copy(out=grouped[:], in_=y_acc[e][:].rearrange("p t j -> p j t"))
-            else:
-                nc.vector.tensor_copy(out=grouped[:], in_=mine.rearrange("p t j -> p j t"))
+                y_grouped[e] = grouped
+
+        def round_result(e):
+            if PLACE[e] not in SCALAR_ROUNDS:
+                grouped = keep.tile([P, C, 4], BF16, name="y_grouped%d" % e, align_bytes=64)
+                nc.vector.tensor_copy(out=grouped[:], in_=y_mine[e].rearrange("p t j -> p j t"))
+                y_grouped[e] = grouped
+
+        def quantise_result(e):
             cols = slice(e * C, (e + 1) * C)
             nc.vector.quantize_mx(
                 out=y_codes[:, cols].bitcast(FP8X4), scales=y_scales[:, cols],
-                in_=grouped[:].rearrange("p j t -> p (j t)"),
+                in_=y_grouped[e][:].rearrange("p j t -> p (j t)"),
             )
             for code_first, code_last in CODE_GROUPS:
                 if e == code_last - 1:
                     done = slice(code_first * C, code_last * C)
                     nc.sync.dma_start(out=out_words[:, done], in_=y_codes[:, done].bitcast(I32))
 
-        first_layer(0)
-        for step in range(E + LAG + 1):
-            if step < E:
-                hidden(step)
-            if 0 <= step - LAG - 1 < E:
-                hand_out(step - LAG - 1)
-            if 0 <= step - LAG < E:
-                second_layer(step - LAG)
-            if step + 1 < E:
-                first_layer(step + 1)
+        def at(place, stage):
+            if 0 <= place < E:
+                stage(ORDER[place])
+
+        at(0, deal_scales)
+        at(1, deal_scales)
+        at(0, first_layer)
+        at(0, activate)
+        for step in range(-1, E + 1):
+            at(step + 2, first_layer)
+            at(step, quantise_hidden)
+            at(step, second_layer)
+            at(step + 2, activate)
+            at(step + 1, group_hidden)
+            at(step, hand_out)
+            if step in (0, 1):
+                gather((0,), (1 - step,), SLOT * (step + 1) + GROUPED_AT)
+            at(step + 1, deal_second)
+            at(step - 1, round_result)
+            if step >= 0:
+                at(step + 2, deal_scales)
+            at(step - 1, quantise_result)
 
         for q in range(4):
             queue = nc.scalar if q < 2 else nc.sync

@@ -24,14 +24,14 @@ LINE = 16
 
 ORDER = tuple(range(HOT, E)) + tuple(range(HOT))
 PLACE = {e: k for k, e in enumerate(ORDER)}
-X_SC_AT = 8192 * (E + 1) + 2048 - 64
+X_SC_AT = 8192 * (E + 1) + 6144 - 64
 W1_AT = 2048
 DEALT_END = W1_AT + 64
 CODES_AT = DEALT_END
 GROUPED_AT = CODES_AT + 512
 ROUNDED_AT = W1_AT + 2048 - 64
 SLOT = 8192
-SCALAR_ROUNDS = (0,)
+SCALAR_ROUNDS = ()
 ROW_GROUPS = ((2, 4), (4, 5), (5, 6), (6, 7), (7, 8), (0, 1), (1, 2))
 CODE_GROUPS = ((2, 6), (6, 8), (0, 2))
 
@@ -45,7 +45,6 @@ def tile_moe_hot_s_mlp_gelu_kernel(
         keep = ctx.enter_context(tc.tile_pool(name="keep", bufs=1))
         placed = ctx.enter_context(tc.tile_pool(name="placed", bufs=1))
         ring = ctx.enter_context(tc.tile_pool(name="ring", bufs=3))
-        psc = ctx.enter_context(tc.tile_pool(name="psc", bufs=3))
         psum = ctx.enter_context(tc.psum_pool(name="psum", bufs=2))
         sums = ctx.enter_context(tc.psum_pool(name="sums", bufs=3))
 
@@ -55,12 +54,14 @@ def tile_moe_hot_s_mlp_gelu_kernel(
         nc.gpsimd.memset(zero[:], 0.0)
         ident = keep.tile([P, P], F32, name="ident")
         make_identity(nc, ident[:])
+        w2c_staged = keep.tile([P, N], U8, name="w2c_staged", align_bytes=64)
+        nc.vector.memset(w2c_staged[:].bitcast(I32), 0)
+        w1c_sc = keep.tile([P, COLD * PASSES, H], U8, name="w1c_sc", align_bytes=64)
+        nc.vector.memset(w1c_sc[:].rearrange("p a c -> p (a c)").bitcast(I32), 0)
         w1h_sc = keep.tile([P, H], U8, name="w1h_sc", align_bytes=64)
         nc.vector.memset(w1h_sc[:].bitcast(I32), 0)
         w2h_sc = keep.tile([P, N], U8, name="w2h_sc", align_bytes=64)
         nc.vector.memset(w2h_sc[:].bitcast(I32), 0)
-        w1c_sc = keep.tile([P, COLD * PASSES, H], U8, name="w1c_sc", align_bytes=64)
-        nc.vector.memset(w1c_sc[:].rearrange("p a c -> p (a c)").bitcast(I32), 0)
         cold_sc_pass1 = keep.tile([P, COLD * C], U8, name="cold_sc_pass1", align_bytes=64)
         nc.vector.memset(cold_sc_pass1[:].bitcast(I32), 0)
         w2c_sc = keep.tile([P, COLD, N], U8, name="w2c_sc", align_bytes=64)
@@ -78,6 +79,7 @@ def tile_moe_hot_s_mlp_gelu_kernel(
 
         w1_raw = {}
         w2_raw = {}
+        w2_pairs = {}
 
         def load_first(e, queue, count=1):
             if e < HOT:
@@ -97,8 +99,10 @@ def tile_moe_hot_s_mlp_gelu_kernel(
                 src = w2c_words[e - HOT : e - HOT + 2].rearrange("f s p b -> p (f s) b")
             tile = keep.tile(list(src.shape), U8, name="w2_%d" % e, align_bytes=64)
             queue.dma_start(out=tile[:].bitcast(I32), in_=src.bitcast(I32))
-            for j in range(src.shape[1]):
-                w2_raw[e + j] = tile[:, j, :]
+            if e < HOT:
+                w2_raw[e] = tile[:, 0, :]
+            else:
+                w2_pairs[e] = tile
 
         def load_cold_first_scales(r, queue):
             rows = w1c_scales.rearrange("e s (q r) c -> r q (e s) c", r=4)
@@ -111,9 +115,17 @@ def tile_moe_hot_s_mlp_gelu_kernel(
                 in_=planes[:, 4 * q : 4 * q + 4, :].bitcast(I32),
             )
 
-        def load_cold_second_scales(r, queue):
-            rows = w2c_scales.rearrange("e s (q r) c -> r q (e s) c", r=4)
-            queue.dma_start(out=w2c_sc[r:P:32].bitcast(I32), in_=rows[r].bitcast(I32))
+        def load_staged(queue):
+            queue.dma_start(
+                out=w2c_staged[0 : 16 * COLD, :].bitcast(I32),
+                in_=w2c_scales.rearrange("f s b c -> (s b) f c").bitcast(I32),
+            )
+
+        def move_second_scales(q, queue):
+            queue.dma_start(
+                out=w2c_sc[32 * q : 32 * q + 4].bitcast(I32),
+                in_=w2c_dealt[4 * COLD * q : 4 * COLD * (q + 1), :].bitcast(I32),
+            )
 
         def list_slice(first, last):
             return offsets[:, first * LIST_COLS : last * LIST_COLS]
@@ -126,6 +138,7 @@ def tile_moe_hot_s_mlp_gelu_kernel(
 
         hot_sc = keep.tile([P, HOT * C], U8, name="hot_sc", align_bytes=64)
         cold_sc = keep.tile([P, COLD * C], U8, name="cold_sc", align_bytes=64)
+        w2c_dealt = placed.tile([P, N], U8, name="w2c_dealt", align_bytes=64, offset=X_SC_AT + 64)
         gathered = {}
 
         def gather_cold_scales():
@@ -139,17 +152,25 @@ def tile_moe_hot_s_mlp_gelu_kernel(
         def move_token_scales(r, queue):
             queue.dma_start(out=cold_sc_pass1[r:P:32, :].bitcast(I32), in_=cold_sc[4 + r : P : 32, :].bitcast(I32))
 
-        def gather(pairs, passes, offset):
+        cold_words = placed.tile(
+            [P, PASSES, COLD * C], U32, name="cold_words", align_bytes=64, offset=X_SC_AT + 64 - 6144
+        )
+
+        def gather(words, first, last, s):
+            window = x_w[:, s, :].bitcast(U32)
+            nc.vector.tensor_copy(out=words, in_=window.indirect(list_slice(first, last)))
+            for e in range(first, last):
+                gathered[e, s] = words[:, (e - first) * C : (e - first + 1) * C]
+
+        def gather_cold(first, last):
+            for s in range(PASSES):
+                gather(cold_words[:, s, (first - HOT) * C : (last - HOT) * C], first, last, s)
+
+        def gather_hot(s, place):
             words = placed.tile(
-                [P, len(pairs), len(passes), 2 * C], U32, name="words%d_%d" % (pairs[0], passes[0]),
-                align_bytes=64, offset=offset,
+                [P, HOT * C], U32, name="hot_words%d" % s, align_bytes=64, offset=SLOT * (place + 1) + GROUPED_AT
             )
-            for b, first in enumerate(pairs):
-                for a, s in enumerate(passes):
-                    window = x_w[:, s, :].bitcast(U32)
-                    nc.vector.tensor_copy(out=words[:, b, a, :], in_=window.indirect(list_slice(first, first + 2)))
-                    for j in range(2):
-                        gathered[first + j, s] = words[:, b, a, j * C : (j + 1) * C]
+            gather(words[:], 0, HOT, s)
 
         nc.scalar.dma_start(out=x_w[:], in_=x_words.rearrange("s p t d -> p s (t d)").bitcast(I32))
         load_token_scales(0, nc.sync)
@@ -158,6 +179,7 @@ def tile_moe_hot_s_mlp_gelu_kernel(
         load_token_scales(3, nc.sync)
         no_bias = keep.tile([P, 1], F32, name="no_bias")
         nc.scalar.activation(out=no_bias[:], in_=zero[:], func=GELU)
+        load_staged(nc.gpsimd)
         load_hot_scales(w1h_sc, w1h_scales, 0, nc.gpsimd)
         load_hot_scales(w1h_sc, w1h_scales, 1, nc.gpsimd)
         load_hot_scales(w1h_sc, w1h_scales, 2, nc.gpsimd)
@@ -167,25 +189,27 @@ def tile_moe_hot_s_mlp_gelu_kernel(
         load_hot_scales(w2h_sc, w2h_scales, 2, nc.gpsimd)
         load_hot_scales(w2h_sc, w2h_scales, 3, nc.gpsimd)
         load_first(2, nc.sync)
-        load_first(3, nc.sync)
         load_cold_first_scales(0, nc.scalar)
-        load_cold_first_scales(1, nc.scalar)
+        load_cold_first_scales(1, nc.sync)
         load_cold_first_scales(2, nc.scalar)
-        load_cold_first_scales(3, nc.scalar)
-        load_first(4, nc.sync)
+        load_cold_first_scales(3, nc.sync)
         gather_cold_scales()
-        move_token_scales(0, nc.sync)
-        move_token_scales(1, nc.sync)
-        move_token_scales(2, nc.sync)
-        move_token_scales(3, nc.sync)
+        move_token_scales(0, nc.scalar)
+        move_token_scales(1, nc.scalar)
+        move_token_scales(2, nc.scalar)
+        move_token_scales(3, nc.scalar)
         nc.vector.tensor_copy(out=hot_sc[:], in_=x_sc[:].indirect(list_slice(0, HOT)))
-        gather((2,), (1, 0), X_SC_AT + 64 - 2048)
-        gather((4, 6), (1, 0), X_SC_AT + 64)
-        load_cold_second_scales(0, nc.sync)
-        load_cold_second_scales(1, nc.sync)
-        load_cold_second_scales(2, nc.sync)
-        load_cold_second_scales(3, nc.sync)
+        deal(w2c_dealt[:], w2c_staged[:], LINE)
+        gather_cold(2, 4)
+        gather_cold(4, 6)
+        gather_cold(6, 8)
+        load_first(3, nc.sync)
+        load_first(4, nc.sync)
+        move_second_scales(0, nc.scalar)
+        move_second_scales(1, nc.scalar)
         load_second(2, nc.sync)
+        move_second_scales(2, nc.sync)
+        move_second_scales(3, nc.sync)
         load_first(5, nc.sync)
         load_first(6, nc.sync)
         load_second(4, nc.sync)
@@ -214,7 +238,7 @@ def tile_moe_hot_s_mlp_gelu_kernel(
 
         def first_layer(e):
             acc = sums.tile([P, H], F32, name="h_acc", tag="h_acc")
-            for s in reversed(range(PASSES)):
+            for s in range(PASSES):
                 if e < HOT:
                     words, plane = w1_raw[e][:, s, :].bitcast(FP8X4), w1h_sc[4 * (PASSES * e + s) : P, :]
                     x_plane = hot_sc[4 * s : P, e * C : (e + 1) * C]
@@ -224,7 +248,7 @@ def tile_moe_hot_s_mlp_gelu_kernel(
                     x_plane = (cold_sc, cold_sc_pass1)[s][:, f * C : (f + 1) * C]
                 nc.tensor.matmul_mx(
                     out=acc[:], lhsT=gathered[e, s].bitcast(FP8X4), lhsT_scale=x_plane,
-                    rhs=words, rhs_scale=plane, start=(s == PASSES - 1), stop=(s == 0),
+                    rhs=words, rhs_scale=plane, start=(s == 0), stop=(s == PASSES - 1),
                 )
             h_acc[e] = acc
 
@@ -259,18 +283,25 @@ def tile_moe_hot_s_mlp_gelu_kernel(
             h_quant[e] = (codes, scales)
 
         def deal_second(e):
-            word_dtype, word_bytes, mx_dtype = (I32, 4, FP8X4) if e < HOT else (U16, 2, FP4X4)
-            words = ring.tile([P, N * word_bytes], U8, name="w2_words", tag="w2_words", align_bytes=64)
-            deal(words[:].bitcast(word_dtype), w2_raw[e].bitcast(word_dtype), LINE // word_bytes)
-            dealt[e] = (words, word_bytes, mx_dtype)
+            if e in w2_pairs:
+                words = keep.tile([P, 2, 2 * N], U8, name="w2_words%d" % e, align_bytes=64)
+                nc.vector.tensor_copy(
+                    out=words[:].bitcast(U16).rearrange("p e (t c i) -> p e c t i", t=4, i=LINE // 2),
+                    in_=w2_pairs[e][:].bitcast(U16).rearrange("p e (c i t) -> p e c t i", t=4, i=LINE // 2),
+                )
+                dealt[e], dealt[e + 1] = (words[:, 0, :], 2, FP4X4), (words[:, 1, :], 2, FP4X4)
+            elif e < HOT:
+                words = keep.tile([P, 4 * N], U8, name="w2_words%d" % e, align_bytes=64)
+                deal(words[:].bitcast(I32), w2_raw[e].bitcast(I32), LINE // 4)
+                dealt[e] = (words[:], 4, FP8X4)
 
         def deal_scales(e):
-            if e != 1:
-                tile = psc.tile([P, N], U8, name="w2_scales", tag="w2_scales", align_bytes=64)
-                deal(tile[:], w2h_sc[:] if e == 0 else w2c_sc[:, e - HOT, :], LINE)
-                planes[e] = tile[:]
             if e == 0:
-                planes[1] = tile[4:P, :]
+                tile = placed.tile([P, N], U8, name="w2h_dealt", align_bytes=64, offset=SLOT * COLD + CODES_AT)
+                deal(tile[:], w2h_sc[:], LINE)
+                planes[0], planes[1] = tile[:], tile[4:P, :]
+            elif e >= HOT:
+                planes[e] = w2c_sc[:, e - HOT, :]
 
         def second_layer(e):
             codes, scales = h_quant[e]
@@ -334,7 +365,7 @@ def tile_moe_hot_s_mlp_gelu_kernel(
             at(step + 1, group_hidden)
             at(step, hand_out)
             if step in (0, 1):
-                gather((0,), (1 - step,), SLOT * (step + 1) + GROUPED_AT)
+                gather_hot(step - 0, step)
             at(step + 1, deal_second)
             at(step - 1, round_result)
             if step >= 0:

@@ -23,8 +23,9 @@ LIST_COLS = C // 16
 LINE = 16
 
 ORDER = tuple(range(HOT, E)) + tuple(range(HOT))
+PAIRS = ORDER[::2]
 PLACE = {e: k for k, e in enumerate(ORDER)}
-X_SC_AT = 8192 * (E + 1) + 6144 - 64
+X_SC_AT = 8192 * (E + 2) + 6144 - 64
 W1_AT = 2048
 DEALT_END = W1_AT + 64
 CODES_AT = DEALT_END
@@ -32,7 +33,7 @@ GROUPED_AT = CODES_AT + 512
 ROUNDED_AT = W1_AT + 2048 - 64
 SLOT = 8192
 SCALAR_ROUNDS = ()
-ROW_GROUPS = ((2, 4), (4, 5), (5, 6), (6, 7), (7, 8), (0, 1), (1, 2))
+ROW_GROUPS = ()
 CODE_GROUPS = ((2, 6), (6, 8), (0, 2))
 
 
@@ -45,7 +46,7 @@ def tile_moe_hot_s_mlp_gelu_kernel(
         keep = ctx.enter_context(tc.tile_pool(name="keep", bufs=1))
         placed = ctx.enter_context(tc.tile_pool(name="placed", bufs=1))
         ring = ctx.enter_context(tc.tile_pool(name="ring", bufs=3))
-        psum = ctx.enter_context(tc.psum_pool(name="psum", bufs=2))
+        psum = ctx.enter_context(tc.psum_pool(name="psum", bufs=1))
         sums = ctx.enter_context(tc.psum_pool(name="sums", bufs=3))
 
         x_sc = placed.tile([P, T], U8, name="x_sc", align_bytes=64, offset=X_SC_AT)
@@ -79,30 +80,25 @@ def tile_moe_hot_s_mlp_gelu_kernel(
 
         w1_raw = {}
         w2_raw = {}
-        w2_pairs = {}
 
-        def load_first(e, queue, count=1):
+        def load_first(e, queue):
             if e < HOT:
                 src = w1h_words[e].rearrange("s p i d -> p s (i d)")
+                tile = placed.tile(list(src.shape), U8, name="w1_%d" % e, align_bytes=64, offset=SLOT * PLACE[0] + W1_AT * (1 + 2 * (1 - e)))
+                w1_raw[e] = tile[:]
             else:
-                src = w1c_words[e - HOT : e - HOT + count].rearrange("f s p b -> p (f s) b")
-            last = e + count - 1
-            tile = placed.tile(list(src.shape), U8, name="w1_%d" % e, align_bytes=64, offset=SLOT * PLACE[last] + W1_AT)
+                src = w1c_words[e - HOT : e - HOT + 2].rearrange("f s p b -> p (f s) b")
+                tile = placed.tile(list(src.shape), U8, name="w1_%d" % e, align_bytes=64, offset=SLOT * PLACE[e] + W1_AT)
+                w1_raw[e], w1_raw[e + 1] = tile[:, 0:PASSES, :], tile[:, PASSES : 2 * PASSES, :]
             queue.dma_start(out=tile[:].bitcast(I32), in_=src.bitcast(I32))
-            for j in range(count):
-                w1_raw[e + j] = tile[:, PASSES * j : PASSES * (j + 1), :]
 
         def load_second(e, queue):
             if e < HOT:
-                src = w2h_words[e].rearrange("s p n d -> p s (n d)")
+                src = w2h_words.rearrange("e s p n d -> p (e s) (n d)")
             else:
                 src = w2c_words[e - HOT : e - HOT + 2].rearrange("f s p b -> p (f s) b")
-            tile = keep.tile(list(src.shape), U8, name="w2_%d" % e, align_bytes=64)
-            queue.dma_start(out=tile[:].bitcast(I32), in_=src.bitcast(I32))
-            if e < HOT:
-                w2_raw[e] = tile[:, 0, :]
-            else:
-                w2_pairs[e] = tile
+            w2_raw[e] = keep.tile(list(src.shape), U8, name="w2_%d" % e, align_bytes=64)
+            queue.dma_start(out=w2_raw[e][:].bitcast(I32), in_=src.bitcast(I32))
 
         def load_cold_first_scales(r, queue):
             rows = w1c_scales.rearrange("e s (q r) c -> r q (e s) c", r=4)
@@ -168,15 +164,15 @@ def tile_moe_hot_s_mlp_gelu_kernel(
 
         def gather_hot(s, place):
             words = placed.tile(
-                [P, HOT * C], U32, name="hot_words%d" % s, align_bytes=64, offset=SLOT * (place + 1) + GROUPED_AT
+                [P, HOT * C], U32, name="hot_words%d" % s, align_bytes=64, offset=SLOT * place + W1_AT + 1024 * s
             )
             gather(words[:], 0, HOT, s)
 
-        nc.scalar.dma_start(out=x_w[:], in_=x_words.rearrange("s p t d -> p s (t d)").bitcast(I32))
         load_token_scales(0, nc.sync)
         load_token_scales(1, nc.sync)
         load_token_scales(2, nc.sync)
         load_token_scales(3, nc.sync)
+        nc.sync.dma_start(out=x_w[:], in_=x_words.rearrange("s p t d -> p s (t d)").bitcast(I32))
         no_bias = keep.tile([P, 1], F32, name="no_bias")
         nc.scalar.activation(out=no_bias[:], in_=zero[:], func=GELU)
         load_staged(nc.gpsimd)
@@ -203,22 +199,20 @@ def tile_moe_hot_s_mlp_gelu_kernel(
         gather_cold(2, 4)
         gather_cold(4, 6)
         gather_cold(6, 8)
-        load_first(3, nc.sync)
+        for s in range(PASSES):
+            gather_hot(s, 0)
         load_first(4, nc.sync)
         move_second_scales(0, nc.scalar)
         move_second_scales(1, nc.scalar)
         load_second(2, nc.sync)
+        load_first(6, nc.sync)
         move_second_scales(2, nc.sync)
         move_second_scales(3, nc.sync)
-        load_first(5, nc.sync)
-        load_first(6, nc.sync)
         load_second(4, nc.sync)
-        load_first(7, nc.sync)
-        load_second(6, nc.sync)
         load_first(0, nc.sync)
-        load_second(0, nc.sync)
         load_first(1, nc.sync)
-        load_second(1, nc.sync)
+        load_second(6, nc.sync)
+        load_second(0, nc.sync)
 
         y_codes = keep.tile([P, E * C], U32, name="y_codes", align_bytes=64)
         y_scales = keep.tile([P, E * C], U8, name="y_scales", align_bytes=64)
@@ -237,7 +231,7 @@ def tile_moe_hot_s_mlp_gelu_kernel(
         y_grouped = {}
 
         def first_layer(e):
-            acc = sums.tile([P, H], F32, name="h_acc", tag="h_acc")
+            acc = sums.tile([P, H], F32, name="h_acc", tag="h_acc", bufs=4)
             for s in range(PASSES):
                 if e < HOT:
                     words, plane = w1_raw[e][:, s, :].bitcast(FP8X4), w1h_sc[4 * (PASSES * e + s) : P, :]
@@ -252,125 +246,116 @@ def tile_moe_hot_s_mlp_gelu_kernel(
                 )
             h_acc[e] = acc
 
-        def activate(e):
-            act = ring.tile([P, H], BF16, name="act", tag="act", align_bytes=64)
-            nc.scalar.activation(
-                out=act[:].rearrange("p (u m d) -> p u m d", u=2, d=2),
-                in_=h_acc[e][:].rearrange("p (m u d) -> p u m d", u=2, d=2),
-                func=GELU,
-                bias=no_bias[:],
-            )
-            pairs = act[:].bitcast(F32)
-            turned = psum.tile([P, 2, C], F32, name="h_turned", tag="h_turned")
-            for u in range(2):
-                nc.tensor.transpose(turned[:, u, :], pairs[:, u * P : (u + 1) * P], ident[:])
-            h_turned[e] = turned
+        def activate(first):
+            act = ring.tile([P, 2, H], BF16, name="act", tag="act", align_bytes=64)
+            for j in range(2):
+                nc.scalar.activation(
+                    out=act[:, j, :].rearrange("p (u m d) -> p u m d", u=2, d=2),
+                    in_=h_acc[first + j][:].rearrange("p (m u d) -> p u m d", u=2, d=2),
+                    func=GELU,
+                    bias=no_bias[:],
+                )
+            pairs = act[:].rearrange("p j i -> p (j i)").bitcast(F32)
+            turned = psum.tile([P, 4, C], F32, name="h_turned", tag="h_turned")
+            for block in range(4):
+                nc.tensor.transpose(turned[:, block, :], pairs[:, block * P : (block + 1) * P], ident[:])
+            h_turned[first] = turned
 
-        def group_hidden(e):
+        def group_hidden(first):
             grouped = placed.tile(
-                [P, 4 * C], BF16, name="h_grouped%d" % e, align_bytes=64, offset=SLOT * (PLACE[e] + 1) + GROUPED_AT
+                [P, 8 * C], BF16, name="h_grouped%d" % first, align_bytes=64,
+                offset=SLOT * (PLACE[first] + 2) + GROUPED_AT,
             )
             nc.scalar.copy(
-                out=grouped[:].bitcast(F32).rearrange("p (j u) -> p j u", u=2),
-                in_=h_turned[e][:].rearrange("p u j -> p j u"),
+                out=grouped[:].bitcast(F32).rearrange("p (e j u) -> p e j u", e=2, u=2),
+                in_=h_turned[first][:].rearrange("p (e u) j -> p e j u", u=2),
             )
-            h_grouped[e] = grouped
+            h_grouped[first] = grouped
 
-        def quantise_hidden(e):
-            codes = keep.tile([P, C], U32, name="h_codes%d" % e, align_bytes=64)
-            scales = keep.tile([P, C], U8, name="h_scales%d" % e, align_bytes=64)
-            nc.vector.quantize_mx(out=codes[:].bitcast(FP8X4), scales=scales[:], in_=h_grouped[e][:])
-            h_quant[e] = (codes, scales)
+        def quantise_hidden(first):
+            codes = keep.tile([P, 2 * C], U32, name="h_codes%d" % first, align_bytes=64)
+            scales = keep.tile([P, 2 * C], U8, name="h_scales%d" % first, align_bytes=64)
+            nc.vector.quantize_mx(out=codes[:].bitcast(FP8X4), scales=scales[:], in_=h_grouped[first][:])
+            h_quant[first] = (codes, scales)
 
-        def deal_second(e):
-            if e in w2_pairs:
-                words = keep.tile([P, 2, 2 * N], U8, name="w2_words%d" % e, align_bytes=64)
-                nc.vector.tensor_copy(
-                    out=words[:].bitcast(U16).rearrange("p e (t c i) -> p e c t i", t=4, i=LINE // 2),
-                    in_=w2_pairs[e][:].bitcast(U16).rearrange("p e (c i t) -> p e c t i", t=4, i=LINE // 2),
-                )
-                dealt[e], dealt[e + 1] = (words[:, 0, :], 2, FP4X4), (words[:, 1, :], 2, FP4X4)
-            elif e < HOT:
-                words = keep.tile([P, 4 * N], U8, name="w2_words%d" % e, align_bytes=64)
-                deal(words[:].bitcast(I32), w2_raw[e].bitcast(I32), LINE // 4)
-                dealt[e] = (words[:], 4, FP8X4)
-
-        def deal_scales(e):
-            if e == 0:
-                tile = placed.tile([P, N], U8, name="w2h_dealt", align_bytes=64, offset=SLOT * COLD + CODES_AT)
+        def deal_second(first):
+            word_dtype, word_bytes = (I32, 4) if first < HOT else (U16, 2)
+            words = keep.tile([P, 2, N * word_bytes], U8, name="w2_words%d" % first, align_bytes=64)
+            nc.vector.tensor_copy(
+                out=words[:].bitcast(word_dtype).rearrange("p e (t c i) -> p e c t i", t=4, i=LINE // word_bytes),
+                in_=w2_raw[first][:].bitcast(word_dtype).rearrange("p e (c i t) -> p e c t i", t=4, i=LINE // word_bytes),
+            )
+            if first < HOT:
+                tile = placed.tile([P, N], U8, name="w2h_dealt", align_bytes=64, offset=SLOT * PLACE[0] + CODES_AT)
                 deal(tile[:], w2h_sc[:], LINE)
-                planes[0], planes[1] = tile[:], tile[4:P, :]
-            elif e >= HOT:
-                planes[e] = w2c_sc[:, e - HOT, :]
+                dealt[first] = (words, word_bytes, FP8X4, [tile[:], tile[4:P, :]])
+            else:
+                dealt[first] = (words, word_bytes, FP4X4, [w2c_sc[:, first - HOT + j, :] for j in range(2)])
 
-        def second_layer(e):
-            codes, scales = h_quant[e]
-            words, word_bytes, mx_dtype = dealt[e]
-            plane = planes[e]
-            acc = sums.tile([P, 4, C], F32, name="y_acc", tag="y_acc")
-            for t in range(4):
-                nc.tensor.matmul_mx(
-                    out=acc[:, t, :],
-                    lhsT=words[:, t * P * word_bytes : (t + 1) * P * word_bytes].bitcast(mx_dtype),
-                    lhsT_scale=plane[:, t * P : (t + 1) * P],
-                    rhs=codes[:].bitcast(FP8X4), rhs_scale=scales[:], start=True, stop=True,
+        def second_layer(first):
+            codes, scales = h_quant[first]
+            words, word_bytes, mx_dtype, planes = dealt[first]
+            for j in range(2):
+                acc = sums.tile([P, 4, C], F32, name="y_acc", tag="y_acc", bufs=3)
+                mine = slice(j * C, (j + 1) * C)
+                for t in range(4):
+                    nc.tensor.matmul_mx(
+                        out=acc[:, t, :],
+                        lhsT=words[:, j, t * P * word_bytes : (t + 1) * P * word_bytes].bitcast(mx_dtype),
+                        lhsT_scale=planes[j][:, t * P : (t + 1) * P],
+                        rhs=codes[:, mine].bitcast(FP8X4), rhs_scale=scales[:, mine], start=True, stop=True,
+                    )
+                y_acc[first + j] = acc
+
+        def hand_out(first):
+            rows = keep.tile([P, 4, 2 * C], F32, name="y_rows%d" % first)
+            for j in range(2):
+                nc.scalar.copy(out=rows[:, :, j * C : (j + 1) * C], in_=y_acc[first + j][:])
+                if first == PAIRS[-1]:
+                    cols = slice((first + j) * C, (first + j + 1) * C)
+                    nc.sync.dma_start(out=out_rows[:, :, cols], in_=rows[:, :, j * C : (j + 1) * C])
+            if first != PAIRS[-1]:
+                nc.sync.dma_start(out=out_rows[:, :, first * C : (first + 2) * C], in_=rows[:])
+            y_rows[first] = rows
+
+        def planes_out(first):
+            width = C if first == PAIRS[-1] else 2 * C
+            parts = range(0, 2 * C, width)
+            grouped = keep.tile([P, 2 * C, 4], BF16, name="y_grouped%d" % first, align_bytes=64)
+            for c in parts:
+                nc.vector.tensor_copy(
+                    out=grouped[:, c : c + width, :], in_=y_rows[first][:, :, c : c + width].rearrange("p t j -> p j t")
                 )
-            y_acc[e] = acc
-
-        def hand_out(e):
-            first, last = [group for group in ROW_GROUPS if group[0] <= e < group[1]][0]
-            if e == first:
-                y_rows[first] = keep.tile([P, 4, (last - first) * C], F32, name="y_rows%d" % first)
-            rows = y_rows[first]
-            mine = rows[:, :, (e - first) * C : (e - first + 1) * C]
-            nc.scalar.copy(out=mine, in_=y_acc[e][:])
-            if e == last - 1:
-                nc.sync.dma_start(out=out_rows[:, :, first * C : last * C], in_=rows[:])
-            y_mine[e] = mine
-            if PLACE[e] in SCALAR_ROUNDS:
-                grouped = keep.tile([P, C, 4], BF16, name="y_grouped%d" % e, align_bytes=64)
-                nc.scalar.copy(out=grouped[:], in_=y_acc[e][:].rearrange("p t j -> p j t"))
-                y_grouped[e] = grouped
-
-        def round_result(e):
-            if PLACE[e] not in SCALAR_ROUNDS:
-                grouped = keep.tile([P, C, 4], BF16, name="y_grouped%d" % e, align_bytes=64)
-                nc.vector.tensor_copy(out=grouped[:], in_=y_mine[e].rearrange("p t j -> p j t"))
-                y_grouped[e] = grouped
-
-        def quantise_result(e):
-            cols = slice(e * C, (e + 1) * C)
-            nc.vector.quantize_mx(
-                out=y_codes[:, cols].bitcast(FP8X4), scales=y_scales[:, cols],
-                in_=y_grouped[e][:].rearrange("p j t -> p (j t)"),
-            )
+            for c in parts:
+                cols = slice(first * C + c, first * C + c + width)
+                nc.vector.quantize_mx(
+                    out=y_codes[:, cols].bitcast(FP8X4), scales=y_scales[:, cols],
+                    in_=grouped[:, c : c + width, :].rearrange("p j t -> p (j t)"),
+                )
             for code_first, code_last in CODE_GROUPS:
-                if e == code_last - 1:
+                if first + 2 == code_last:
                     done = slice(code_first * C, code_last * C)
                     nc.sync.dma_start(out=out_words[:, done], in_=y_codes[:, done].bitcast(I32))
 
-        def at(place, stage):
-            if 0 <= place < E:
-                stage(ORDER[place])
+        def first_layers(first):
+            first_layer(first)
+            first_layer(first + 1)
 
-        at(0, deal_scales)
-        at(1, deal_scales)
-        at(0, first_layer)
+        def at(step, stage):
+            if 0 <= step < len(PAIRS):
+                stage(PAIRS[step])
+
+        at(0, first_layers)
         at(0, activate)
-        for step in range(-1, E + 1):
-            at(step + 2, first_layer)
+        for step in range(-1, len(PAIRS) + 1):
+            at(step + 2, first_layers)
             at(step, quantise_hidden)
             at(step, second_layer)
             at(step + 2, activate)
             at(step + 1, group_hidden)
             at(step, hand_out)
-            if step in (0, 1):
-                gather_hot(step - 0, step)
             at(step + 1, deal_second)
-            at(step - 1, round_result)
-            if step >= 0:
-                at(step + 2, deal_scales)
-            at(step - 1, quantise_result)
+            at(step - 1, planes_out)
 
         for q in range(4):
             queue = nc.scalar if q < 2 else nc.sync

@@ -26,6 +26,8 @@ ORDER = tuple(range(HOT, E)) + tuple(range(HOT))
 PAIRS = ORDER[::2]
 PLACE = {e: k for k, e in enumerate(ORDER)}
 X_SC_AT = 8192 * (E + 2) + 6144 - 64
+HELD = (2,)
+VECTOR_GROUPS = (0,)
 W1_AT = 2048
 DEALT_END = W1_AT + 64
 CODES_AT = DEALT_END
@@ -201,15 +203,15 @@ def tile_moe_hot_s_mlp_gelu_kernel(
         gather_cold(6, 8)
         for s in range(PASSES):
             gather_hot(s, 0)
-        load_first(4, nc.sync)
         move_second_scales(0, nc.scalar)
         move_second_scales(1, nc.scalar)
+        move_second_scales(2, nc.scalar)
+        move_second_scales(3, nc.scalar)
+        load_first(4, nc.sync)
         load_second(2, nc.sync)
         load_first(6, nc.sync)
-        move_second_scales(2, nc.sync)
-        move_second_scales(3, nc.sync)
-        load_second(4, nc.sync)
         load_first(0, nc.sync)
+        load_second(4, nc.sync)
         load_first(1, nc.sync)
         load_second(6, nc.sync)
         load_second(0, nc.sync)
@@ -264,9 +266,10 @@ def tile_moe_hot_s_mlp_gelu_kernel(
         def group_hidden(first):
             grouped = placed.tile(
                 [P, 8 * C], BF16, name="h_grouped%d" % first, align_bytes=64,
-                offset=SLOT * (PLACE[first] + 2) + GROUPED_AT,
+                offset=SLOT * (PLACE[first] + (2 if first in HELD else 3)) + GROUPED_AT + (0 if first in HELD else 4096),
             )
-            nc.scalar.copy(
+            copy = nc.vector.tensor_copy if first in VECTOR_GROUPS else nc.scalar.copy
+            copy(
                 out=grouped[:].bitcast(F32).rearrange("p (e j u) -> p e j u", e=2, u=2),
                 in_=h_turned[first][:].rearrange("p (e u) j -> p e j u", u=2),
             )
@@ -309,7 +312,11 @@ def tile_moe_hot_s_mlp_gelu_kernel(
 
         def hand_out(first):
             rows = keep.tile([P, 4, 2 * C], F32, name="y_rows%d" % first)
+            grouped = keep.tile([P, 2 * C, 4], BF16, name="y_grouped%d" % first, align_bytes=64)
+            y_grouped[first] = grouped
             for j in range(2):
+                if first == PAIRS[-1] and j == 1:
+                    nc.vector.tensor_copy(out=grouped[:, C : 2 * C, :], in_=y_acc[first + 1][:].rearrange("p t j -> p j t"))
                 nc.scalar.copy(out=rows[:, :, j * C : (j + 1) * C], in_=y_acc[first + j][:])
                 if first == PAIRS[-1]:
                     cols = slice((first + j) * C, (first + j + 1) * C)
@@ -319,14 +326,12 @@ def tile_moe_hot_s_mlp_gelu_kernel(
             y_rows[first] = rows
 
         def planes_out(first):
+            grouped = y_grouped[first]
             width = C if first == PAIRS[-1] else 2 * C
-            parts = range(0, 2 * C, width)
-            grouped = keep.tile([P, 2 * C, 4], BF16, name="y_grouped%d" % first, align_bytes=64)
-            for c in parts:
-                nc.vector.tensor_copy(
-                    out=grouped[:, c : c + width, :], in_=y_rows[first][:, :, c : c + width].rearrange("p t j -> p j t")
-                )
-            for c in parts:
+            nc.vector.tensor_copy(
+                out=grouped[:, 0:width, :], in_=y_rows[first][:, :, 0:width].rearrange("p t j -> p j t")
+            )
+            for c in reversed(range(0, 2 * C, width)):
                 cols = slice(first * C + c, first * C + c + width)
                 nc.vector.quantize_mx(
                     out=y_codes[:, cols].bitcast(FP8X4), scales=y_scales[:, cols],

@@ -22,21 +22,15 @@ COLD = E - HOT
 LIST_COLS = C // 16
 LINE = 16
 
-ORDER = tuple(range(HOT, E)) + tuple(range(HOT))
-PAIRS = ORDER[::2]
-PLACE = {e: k for k, e in enumerate(ORDER)}
-X_SC_AT = 8192 * (E + 2) + 6144 - 64
-HELD = (2,)
+PAIRS = (2, 4, 6, 0)
 VECTOR_GROUPS = (0,)
-W1_AT = 2048
-DEALT_END = W1_AT + 64
-CODES_AT = DEALT_END
-GROUPED_AT = CODES_AT + 512
-ROUNDED_AT = W1_AT + 2048 - 64
-SLOT = 8192
-SCALAR_ROUNDS = ()
-ROW_GROUPS = ()
-CODE_GROUPS = ((2, 6), (6, 8), (0, 2))
+GROUPS = 4
+STAGED = 2 * N
+
+STAGED_AT = 0
+SLOT_WORDS_AT = STAGED_AT + HOT * C
+H_GROUPED_AT = {2: 10240, 4: 12288, 6: 16384, 0: 20480}
+DEALT_AT = {2: 22528, 4: 28672, 6: H_GROUPED_AT[6], 0: 24576}
 
 
 def tile_moe_hot_s_mlp_gelu_kernel(
@@ -51,28 +45,26 @@ def tile_moe_hot_s_mlp_gelu_kernel(
         psum = ctx.enter_context(tc.psum_pool(name="psum", bufs=1))
         sums = ctx.enter_context(tc.psum_pool(name="sums", bufs=3))
 
-        x_sc = placed.tile([P, T], U8, name="x_sc", align_bytes=64, offset=X_SC_AT)
+        x_sc = keep.tile([P, T], U8, name="x_sc", align_bytes=64)
         nc.gpsimd.memset(x_sc[:].bitcast(I32), 0)
+        staged = placed.tile([P, 2, N], U8, name="staged", align_bytes=64, offset=STAGED_AT)
+        nc.gpsimd.memset(staged[:].rearrange("p a c -> p (a c)").bitcast(I32), 0)
         zero = keep.tile([P, 1], F32, name="zero")
         nc.gpsimd.memset(zero[:], 0.0)
-        ident = keep.tile([P, P], F32, name="ident")
-        make_identity(nc, ident[:])
-        w2c_staged = keep.tile([P, N], U8, name="w2c_staged", align_bytes=64)
-        nc.vector.memset(w2c_staged[:].bitcast(I32), 0)
         w1c_sc = keep.tile([P, COLD * PASSES, H], U8, name="w1c_sc", align_bytes=64)
         nc.vector.memset(w1c_sc[:].rearrange("p a c -> p (a c)").bitcast(I32), 0)
-        w1h_sc = keep.tile([P, H], U8, name="w1h_sc", align_bytes=64)
-        nc.vector.memset(w1h_sc[:].bitcast(I32), 0)
-        w2h_sc = keep.tile([P, N], U8, name="w2h_sc", align_bytes=64)
-        nc.vector.memset(w2h_sc[:].bitcast(I32), 0)
         cold_sc_pass1 = keep.tile([P, COLD * C], U8, name="cold_sc_pass1", align_bytes=64)
         nc.vector.memset(cold_sc_pass1[:].bitcast(I32), 0)
-        w2c_sc = keep.tile([P, COLD, N], U8, name="w2c_sc", align_bytes=64)
-        nc.vector.memset(w2c_sc[:].rearrange("p a c -> p (a c)").bitcast(I32), 0)
+        planes = keep.tile([P, GROUPS, STAGED], U8, name="planes", align_bytes=64)
 
+        w1h_sc = keep.tile([P, H], U8, name="w1h_sc", align_bytes=64)
         offsets = keep.tile([P, E * LIST_COLS], U16, name="offsets")
         nc.sync.dma_start(offsets[:], offs)
         x_w = keep.tile([P, PASSES, T], I32, name="x_w", align_bytes=64)
+        regrouped = keep.tile([P, STAGED], U8, name="regrouped", align_bytes=64)
+
+        w1_raw = {}
+        w2_raw = {}
 
         def load_token_scales(q, queue):
             queue.dma_start(
@@ -80,63 +72,54 @@ def tile_moe_hot_s_mlp_gelu_kernel(
                 in_=x_scales[:, 4 * q : 4 * q + 4, :].bitcast(I32),
             )
 
-        w1_raw = {}
-        w2_raw = {}
-
-        def load_first(e, queue):
+        def load_first(e):
             if e < HOT:
                 src = w1h_words[e].rearrange("s p i d -> p s (i d)")
-                tile = placed.tile(list(src.shape), U8, name="w1_%d" % e, align_bytes=64, offset=SLOT * PLACE[0] + W1_AT * (1 + 2 * (1 - e)))
+                tile = keep.tile(list(src.shape), U8, name="w1_%d" % e, align_bytes=64)
                 w1_raw[e] = tile[:]
             else:
                 src = w1c_words[e - HOT : e - HOT + 2].rearrange("f s p b -> p (f s) b")
-                tile = placed.tile(list(src.shape), U8, name="w1_%d" % e, align_bytes=64, offset=SLOT * PLACE[e] + W1_AT)
+                tile = keep.tile(list(src.shape), U8, name="w1_%d" % e, align_bytes=64)
                 w1_raw[e], w1_raw[e + 1] = tile[:, 0:PASSES, :], tile[:, PASSES : 2 * PASSES, :]
-            queue.dma_start(out=tile[:].bitcast(I32), in_=src.bitcast(I32))
+            nc.sync.dma_start(out=tile[:].bitcast(I32), in_=src.bitcast(I32))
 
-        def load_second(e, queue):
+        def load_second(e):
             if e < HOT:
                 src = w2h_words.rearrange("e s p n d -> p (e s) (n d)")
             else:
                 src = w2c_words[e - HOT : e - HOT + 2].rearrange("f s p b -> p (f s) b")
             w2_raw[e] = keep.tile(list(src.shape), U8, name="w2_%d" % e, align_bytes=64)
-            queue.dma_start(out=w2_raw[e][:].bitcast(I32), in_=src.bitcast(I32))
+            nc.sync.dma_start(out=w2_raw[e][:].bitcast(I32), in_=src.bitcast(I32))
 
         def load_cold_first_scales(r, queue):
             rows = w1c_scales.rearrange("e s (q r) c -> r q (e s) c", r=4)
             queue.dma_start(out=w1c_sc[r:P:32].bitcast(I32), in_=rows[r].bitcast(I32))
 
-        def load_hot_scales(tile, scales, q, queue):
-            planes = scales.rearrange("e s b c -> (e s) b c")
+        def stage_second_scales(g, queue):
+            src = w2h_scales if g == 0 else w2c_scales[2 * g - HOT : 2 * g - HOT + 2]
             queue.dma_start(
-                out=tile[32 * q : 32 * q + 4 * planes.shape[0], :].bitcast(I32),
-                in_=planes[:, 4 * q : 4 * q + 4, :].bitcast(I32),
+                out=staged[g : 16 * GROUPS : GROUPS].bitcast(I32),
+                in_=src.rearrange("e s b c -> b (e s) c").bitcast(I32),
             )
 
-        def load_staged(queue):
+        def load_hot_first_scales(q, queue):
+            rows = w1h_scales.rearrange("e s b c -> (e s) b c")
             queue.dma_start(
-                out=w2c_staged[0 : 16 * COLD, :].bitcast(I32),
-                in_=w2c_scales.rearrange("f s b c -> (s b) f c").bitcast(I32),
+                out=w1h_sc[32 * q : 32 * q + 4 * HOT * PASSES, :].bitcast(I32),
+                in_=rows[:, 4 * q : 4 * q + 4, :].bitcast(I32),
             )
 
-        def move_second_scales(q, queue):
+        def move_staged(q, queue):
             queue.dma_start(
-                out=w2c_sc[32 * q : 32 * q + 4].bitcast(I32),
-                in_=w2c_dealt[4 * COLD * q : 4 * COLD * (q + 1), :].bitcast(I32),
+                out=planes[32 * q : 32 * q + 4].bitcast(I32),
+                in_=regrouped[4 * GROUPS * q : 4 * GROUPS * (q + 1), :].bitcast(I32),
             )
 
         def list_slice(first, last):
             return offsets[:, first * LIST_COLS : last * LIST_COLS]
 
-        def deal(out, in_, run):
-            nc.vector.tensor_copy(
-                out=out.rearrange("p (t c i) -> p c t i", t=4, i=run),
-                in_=in_.rearrange("p (c i t) -> p c t i", t=4, i=run),
-            )
-
-        hot_sc = keep.tile([P, HOT * C], U8, name="hot_sc", align_bytes=64)
         cold_sc = keep.tile([P, COLD * C], U8, name="cold_sc", align_bytes=64)
-        w2c_dealt = placed.tile([P, N], U8, name="w2c_dealt", align_bytes=64, offset=X_SC_AT + 64)
+        slot_words = placed.tile([P, PASSES, E * C], U32, name="slot_words", align_bytes=64, offset=SLOT_WORDS_AT)
         gathered = {}
 
         def gather_cold_scales():
@@ -150,71 +133,52 @@ def tile_moe_hot_s_mlp_gelu_kernel(
         def move_token_scales(r, queue):
             queue.dma_start(out=cold_sc_pass1[r:P:32, :].bitcast(I32), in_=cold_sc[4 + r : P : 32, :].bitcast(I32))
 
-        cold_words = placed.tile(
-            [P, PASSES, COLD * C], U32, name="cold_words", align_bytes=64, offset=X_SC_AT + 64 - 6144
-        )
-
-        def gather(words, first, last, s):
-            window = x_w[:, s, :].bitcast(U32)
-            nc.vector.tensor_copy(out=words, in_=window.indirect(list_slice(first, last)))
-            for e in range(first, last):
-                gathered[e, s] = words[:, (e - first) * C : (e - first + 1) * C]
-
-        def gather_cold(first, last):
+        def gather_pair(first):
             for s in range(PASSES):
-                gather(cold_words[:, s, (first - HOT) * C : (last - HOT) * C], first, last, s)
+                words = slot_words[:, s, first * C : (first + 2) * C]
+                nc.vector.tensor_copy(out=words, in_=x_w[:, s, :].bitcast(U32).indirect(list_slice(first, first + 2)))
+                for j in range(2):
+                    gathered[first + j, s] = words[:, j * C : (j + 1) * C]
 
-        def gather_hot(s, place):
-            words = placed.tile(
-                [P, HOT * C], U32, name="hot_words%d" % s, align_bytes=64, offset=SLOT * place + W1_AT + 1024 * s
-            )
-            gather(words[:], 0, HOT, s)
-
-        load_token_scales(0, nc.sync)
-        load_token_scales(1, nc.sync)
-        load_token_scales(2, nc.sync)
-        load_token_scales(3, nc.sync)
+        for q in range(4):
+            load_token_scales(q, nc.sync if q % 2 else nc.scalar)
         nc.sync.dma_start(out=x_w[:], in_=x_words.rearrange("s p t d -> p s (t d)").bitcast(I32))
+        load_first(2)
+        for g in range(GROUPS):
+            stage_second_scales(g, nc.scalar)
+        for r in range(4):
+            load_cold_first_scales(r, nc.gpsimd)
         no_bias = keep.tile([P, 1], F32, name="no_bias")
         nc.scalar.activation(out=no_bias[:], in_=zero[:], func=GELU)
-        load_staged(nc.gpsimd)
-        load_hot_scales(w1h_sc, w1h_scales, 0, nc.gpsimd)
-        load_hot_scales(w1h_sc, w1h_scales, 1, nc.gpsimd)
-        load_hot_scales(w1h_sc, w1h_scales, 2, nc.gpsimd)
-        load_hot_scales(w1h_sc, w1h_scales, 3, nc.gpsimd)
-        load_hot_scales(w2h_sc, w2h_scales, 0, nc.gpsimd)
-        load_hot_scales(w2h_sc, w2h_scales, 1, nc.gpsimd)
-        load_hot_scales(w2h_sc, w2h_scales, 2, nc.gpsimd)
-        load_hot_scales(w2h_sc, w2h_scales, 3, nc.gpsimd)
-        load_first(2, nc.sync)
-        load_cold_first_scales(0, nc.scalar)
-        load_cold_first_scales(1, nc.sync)
-        load_cold_first_scales(2, nc.scalar)
-        load_cold_first_scales(3, nc.sync)
+        nc.vector.memset(planes[:].rearrange("p a c -> p (a c)").bitcast(I32), 0)
+        nc.vector.memset(w1h_sc[:].bitcast(I32), 0)
+        ident = keep.tile([P, P], F32, name="ident")
+        make_identity(nc, ident[:])
+        for q in range(4):
+            load_hot_first_scales(q, nc.gpsimd)
+
         gather_cold_scales()
-        move_token_scales(0, nc.scalar)
-        move_token_scales(1, nc.scalar)
-        move_token_scales(2, nc.scalar)
-        move_token_scales(3, nc.scalar)
+        for r in range(4):
+            move_token_scales(r, nc.scalar)
+        nc.vector.tensor_copy(
+            out=regrouped[:].rearrange("p (e t c i) -> p e c t i", e=2, t=4, i=LINE),
+            in_=staged[:].rearrange("p e (c i t) -> p e c t i", t=4, i=LINE),
+        )
+        for first in PAIRS:
+            gather_pair(first)
+        hot_sc = placed.tile([P, HOT * C], U8, name="hot_sc", align_bytes=64, offset=STAGED_AT)
         nc.vector.tensor_copy(out=hot_sc[:], in_=x_sc[:].indirect(list_slice(0, HOT)))
-        deal(w2c_dealt[:], w2c_staged[:], LINE)
-        gather_cold(2, 4)
-        gather_cold(4, 6)
-        gather_cold(6, 8)
-        for s in range(PASSES):
-            gather_hot(s, 0)
-        move_second_scales(0, nc.scalar)
-        move_second_scales(1, nc.scalar)
-        move_second_scales(2, nc.scalar)
-        move_second_scales(3, nc.scalar)
-        load_first(4, nc.sync)
-        load_second(2, nc.sync)
-        load_first(6, nc.sync)
-        load_first(0, nc.sync)
-        load_second(4, nc.sync)
-        load_first(1, nc.sync)
-        load_second(6, nc.sync)
-        load_second(0, nc.sync)
+
+        load_first(4)
+        load_second(2)
+        load_first(6)
+        for q in range(4):
+            move_staged(q, nc.sync)
+        load_second(4)
+        load_first(0)
+        load_first(1)
+        load_second(6)
+        load_second(0)
 
         y_codes = keep.tile([P, E * C], U32, name="y_codes", align_bytes=64)
         y_scales = keep.tile([P, E * C], U8, name="y_scales", align_bytes=64)
@@ -222,14 +186,13 @@ def tile_moe_hot_s_mlp_gelu_kernel(
         out_words = out_1[0].rearrange("p j d -> p (j d)").bitcast(I32)
 
         h_acc = {}
+        h_act = {}
         h_turned = {}
         h_grouped = {}
         h_quant = {}
         dealt = {}
-        planes = {}
         y_acc = {}
         y_rows = {}
-        y_mine = {}
         y_grouped = {}
 
         def first_layer(e):
@@ -246,28 +209,24 @@ def tile_moe_hot_s_mlp_gelu_kernel(
                     out=acc[:], lhsT=gathered[e, s].bitcast(FP8X4), lhsT_scale=x_plane,
                     rhs=words, rhs_scale=plane, start=(s == 0), stop=(s == PASSES - 1),
                 )
-            h_acc[e] = acc
+            if e % 2 == 0:
+                h_act[e] = ring.tile([P, 2, H], BF16, name="act", tag="act", align_bytes=64)
+            nc.scalar.activation(
+                out=h_act[e - e % 2][:, e % 2, :].rearrange("p (u m d) -> p u m d", u=2, d=2),
+                in_=acc[:].rearrange("p (m u d) -> p u m d", u=2, d=2),
+                func=GELU,
+                bias=no_bias[:],
+            )
 
-        def activate(first):
-            act = ring.tile([P, 2, H], BF16, name="act", tag="act", align_bytes=64)
-            for j in range(2):
-                nc.scalar.activation(
-                    out=act[:, j, :].rearrange("p (u m d) -> p u m d", u=2, d=2),
-                    in_=h_acc[first + j][:].rearrange("p (m u d) -> p u m d", u=2, d=2),
-                    func=GELU,
-                    bias=no_bias[:],
-                )
-            pairs = act[:].rearrange("p j i -> p (j i)").bitcast(F32)
-            turned = psum.tile([P, 4, C], F32, name="h_turned", tag="h_turned")
+        def turn(first):
+            pairs = h_act[first][:].rearrange("p j i -> p (j i)").bitcast(F32)
+            turned = psum.tile([P, 4, C], F32, name="h_turned", tag="h_turned", bufs=1)
             for block in range(4):
                 nc.tensor.transpose(turned[:, block, :], pairs[:, block * P : (block + 1) * P], ident[:])
             h_turned[first] = turned
 
         def group_hidden(first):
-            grouped = placed.tile(
-                [P, 8 * C], BF16, name="h_grouped%d" % first, align_bytes=64,
-                offset=SLOT * (PLACE[first] + (2 if first in HELD else 3)) + GROUPED_AT + (0 if first in HELD else 4096),
-            )
+            grouped = placed.tile([P, 8 * C], BF16, name="h_grouped%d" % first, align_bytes=64, offset=H_GROUPED_AT[first])
             copy = nc.vector.tensor_copy if first in VECTOR_GROUPS else nc.scalar.copy
             copy(
                 out=grouped[:].bitcast(F32).rearrange("p (e j u) -> p e j u", e=2, u=2),
@@ -283,21 +242,19 @@ def tile_moe_hot_s_mlp_gelu_kernel(
 
         def deal_second(first):
             word_dtype, word_bytes = (I32, 4) if first < HOT else (U16, 2)
-            words = keep.tile([P, 2, N * word_bytes], U8, name="w2_words%d" % first, align_bytes=64)
+            words = placed.tile([P, 2, N * word_bytes], U8, name="w2_words%d" % first, align_bytes=64, offset=DEALT_AT[first])
             nc.vector.tensor_copy(
                 out=words[:].bitcast(word_dtype).rearrange("p e (t c i) -> p e c t i", t=4, i=LINE // word_bytes),
                 in_=w2_raw[first][:].bitcast(word_dtype).rearrange("p e (c i t) -> p e c t i", t=4, i=LINE // word_bytes),
             )
-            if first < HOT:
-                tile = placed.tile([P, N], U8, name="w2h_dealt", align_bytes=64, offset=SLOT * PLACE[0] + CODES_AT)
-                deal(tile[:], w2h_sc[:], LINE)
-                dealt[first] = (words, word_bytes, FP8X4, [tile[:], tile[4:P, :]])
-            else:
-                dealt[first] = (words, word_bytes, FP4X4, [w2c_sc[:, first - HOT + j, :] for j in range(2)])
+            dealt[first] = (words, word_bytes, FP8X4 if first < HOT else FP4X4)
 
         def second_layer(first):
             codes, scales = h_quant[first]
-            words, word_bytes, mx_dtype, planes = dealt[first]
+            words, word_bytes, mx_dtype = dealt[first]
+            rows = keep.tile([P, 4, 2 * C], F32, name="y_rows%d" % first)
+            grouped = keep.tile([P, 2 * C, 4], BF16, name="y_grouped%d" % first, align_bytes=64)
+            y_rows[first], y_grouped[first] = rows, grouped
             for j in range(2):
                 acc = sums.tile([P, 4, C], F32, name="y_acc", tag="y_acc", bufs=3)
                 mine = slice(j * C, (j + 1) * C)
@@ -305,15 +262,13 @@ def tile_moe_hot_s_mlp_gelu_kernel(
                     nc.tensor.matmul_mx(
                         out=acc[:, t, :],
                         lhsT=words[:, j, t * P * word_bytes : (t + 1) * P * word_bytes].bitcast(mx_dtype),
-                        lhsT_scale=planes[j][:, t * P : (t + 1) * P],
+                        lhsT_scale=planes[:, first // 2, j * N + t * P : j * N + (t + 1) * P],
                         rhs=codes[:, mine].bitcast(FP8X4), rhs_scale=scales[:, mine], start=True, stop=True,
                     )
                 y_acc[first + j] = acc
 
         def hand_out(first):
-            rows = keep.tile([P, 4, 2 * C], F32, name="y_rows%d" % first)
-            grouped = keep.tile([P, 2 * C, 4], BF16, name="y_grouped%d" % first, align_bytes=64)
-            y_grouped[first] = grouped
+            rows, grouped = y_rows[first], y_grouped[first]
             for j in range(2):
                 if first == PAIRS[-1] and j == 1:
                     nc.vector.tensor_copy(out=grouped[:, C : 2 * C, :], in_=y_acc[first + 1][:].rearrange("p t j -> p j t"))
@@ -323,7 +278,6 @@ def tile_moe_hot_s_mlp_gelu_kernel(
                     nc.sync.dma_start(out=out_rows[:, :, cols], in_=rows[:, :, j * C : (j + 1) * C])
             if first != PAIRS[-1]:
                 nc.sync.dma_start(out=out_rows[:, :, first * C : (first + 2) * C], in_=rows[:])
-            y_rows[first] = rows
 
         def planes_out(first):
             grouped = y_grouped[first]
@@ -337,30 +291,50 @@ def tile_moe_hot_s_mlp_gelu_kernel(
                     out=y_codes[:, cols].bitcast(FP8X4), scales=y_scales[:, cols],
                     in_=grouped[:, c : c + width, :].rearrange("p j t -> p (j t)"),
                 )
-            for code_first, code_last in CODE_GROUPS:
-                if first + 2 == code_last:
-                    done = slice(code_first * C, code_last * C)
-                    nc.sync.dma_start(out=out_words[:, done], in_=y_codes[:, done].bitcast(I32))
 
-        def first_layers(first):
-            first_layer(first)
-            first_layer(first + 1)
+        def store_codes(first, last):
+            done = slice(first * C, last * C)
+            nc.sync.dma_start(out=out_words[:, done], in_=y_codes[:, done].bitcast(I32))
 
-        def at(step, stage):
-            if 0 <= step < len(PAIRS):
-                stage(PAIRS[step])
-
-        at(0, first_layers)
-        at(0, activate)
-        for step in range(-1, len(PAIRS) + 1):
-            at(step + 2, first_layers)
-            at(step, quantise_hidden)
-            at(step, second_layer)
-            at(step + 2, activate)
-            at(step + 1, group_hidden)
-            at(step, hand_out)
-            at(step + 1, deal_second)
-            at(step - 1, planes_out)
+        first_layer(2)
+        first_layer(3)
+        first_layer(4)
+        turn(2)
+        group_hidden(2)
+        first_layer(5)
+        deal_second(2)
+        quantise_hidden(2)
+        first_layer(6)
+        turn(4)
+        group_hidden(4)
+        quantise_hidden(4)
+        deal_second(4)
+        first_layer(7)
+        second_layer(2)
+        turn(6)
+        hand_out(2)
+        group_hidden(6)
+        quantise_hidden(6)
+        second_layer(4)
+        first_layer(0)
+        first_layer(1)
+        deal_second(6)
+        planes_out(2)
+        turn(0)
+        second_layer(6)
+        group_hidden(0)
+        quantise_hidden(0)
+        deal_second(0)
+        hand_out(4)
+        second_layer(0)
+        planes_out(4)
+        store_codes(2, 6)
+        hand_out(6)
+        planes_out(6)
+        store_codes(6, 8)
+        hand_out(0)
+        planes_out(0)
+        store_codes(0, 2)
 
         for q in range(4):
             queue = nc.scalar if q < 2 else nc.sync

@@ -23,14 +23,23 @@ LIST_COLS = C // 16
 LINE = 16
 
 PAIRS = (2, 4, 6, 0)
-VECTOR_GROUPS = (0,)
+VECTOR_GROUPS = ()
 GROUPS = 4
-STAGED = 2 * N
+STAGED = 2 * N + H
 
-STAGED_AT = 0
-SLOT_WORDS_AT = STAGED_AT + HOT * C
-H_GROUPED_AT = {2: 10240, 4: 12288, 6: 16384, 0: 20480}
-DEALT_AT = {2: 22528, 4: 28672, 6: H_GROUPED_AT[6], 0: 24576}
+BANK = 2048
+H_BANK = {2: 0, 3: 1, 4: 2, 5: 3, 6: 0, 7: 1, 0: 2, 1: 3}
+Y_BANK = {2: 5, 3: 6, 4: 7, 5: 5, 6: 6, 7: 0, 0: 1, 1: 7}
+TURN_BANK = 4
+X_SC_AT = 0
+EARLY_WORDS_AT = X_SC_AT
+LATE_WORDS_AT = 36864
+STAGED_AT = LATE_WORDS_AT + 6144 - 512
+PLANES_AT = LATE_WORDS_AT + 6144
+H_GROUPED_AT = {2: 10240, 4: 12288, 6: 14336, 0: 16384}
+DEALT_AT = {2: 18432, 4: 20480, 6: 8192, 0: 22528}
+W2_RAW_AT = {2: 26624, 4: 28672, 6: 30720, 0: 32768}
+Y_GROUPED_AT = {2: W2_RAW_AT[4], 4: W2_RAW_AT[2], 6: W2_RAW_AT[6], 0: W2_RAW_AT[0]}
 
 
 def tile_moe_hot_s_mlp_gelu_kernel(
@@ -43,21 +52,21 @@ def tile_moe_hot_s_mlp_gelu_kernel(
         placed = ctx.enter_context(tc.tile_pool(name="placed", bufs=1))
         ring = ctx.enter_context(tc.tile_pool(name="ring", bufs=3))
         psum = ctx.enter_context(tc.psum_pool(name="psum", bufs=1))
-        sums = ctx.enter_context(tc.psum_pool(name="sums", bufs=3))
 
-        x_sc = keep.tile([P, T], U8, name="x_sc", align_bytes=64)
+        x_sc = placed.tile([P, T], U8, name="x_sc", align_bytes=64, offset=X_SC_AT)
         nc.gpsimd.memset(x_sc[:].bitcast(I32), 0)
-        staged = placed.tile([P, 2, N], U8, name="staged", align_bytes=64, offset=STAGED_AT)
-        nc.gpsimd.memset(staged[:].rearrange("p a c -> p (a c)").bitcast(I32), 0)
         zero = keep.tile([P, 1], F32, name="zero")
         nc.gpsimd.memset(zero[:], 0.0)
+        ident = keep.tile([P, P], F32, name="ident")
+        make_identity(nc, ident[:])
+        staged = placed.tile([P, 2, N], U8, name="staged", align_bytes=64, offset=STAGED_AT)
         w1c_sc = keep.tile([P, COLD * PASSES, H], U8, name="w1c_sc", align_bytes=64)
         nc.vector.memset(w1c_sc[:].rearrange("p a c -> p (a c)").bitcast(I32), 0)
-        cold_sc_pass1 = keep.tile([P, COLD * C], U8, name="cold_sc_pass1", align_bytes=64)
-        nc.vector.memset(cold_sc_pass1[:].bitcast(I32), 0)
-        planes = keep.tile([P, GROUPS, STAGED], U8, name="planes", align_bytes=64)
+        nc.vector.memset(staged[:].rearrange("p a c -> p (a c)").bitcast(I32), 0)
+        slot_planes = keep.tile([P, PASSES, E * C], U8, name="slot_planes", align_bytes=64)
+        nc.vector.memset(slot_planes[:].rearrange("p a c -> p (a c)").bitcast(I32), 0)
+        planes = placed.tile([P, GROUPS, STAGED], U8, name="planes", align_bytes=64, offset=PLANES_AT)
 
-        w1h_sc = keep.tile([P, H], U8, name="w1h_sc", align_bytes=64)
         offsets = keep.tile([P, E * LIST_COLS], U16, name="offsets")
         nc.sync.dma_start(offsets[:], offs)
         x_w = keep.tile([P, PASSES, T], I32, name="x_w", align_bytes=64)
@@ -66,10 +75,9 @@ def tile_moe_hot_s_mlp_gelu_kernel(
         w1_raw = {}
         w2_raw = {}
 
-        def load_token_scales(q, queue):
+        def load_token_scales(queue):
             queue.dma_start(
-                out=x_sc[32 * q : 32 * q + 4 * PASSES, :].bitcast(I32),
-                in_=x_scales[:, 4 * q : 4 * q + 4, :].bitcast(I32),
+                out=x_sc[0 : 16 * PASSES, :].bitcast(I32), in_=x_scales.rearrange("s b t -> b s t").bitcast(I32)
             )
 
         def load_first(e):
@@ -88,7 +96,7 @@ def tile_moe_hot_s_mlp_gelu_kernel(
                 src = w2h_words.rearrange("e s p n d -> p (e s) (n d)")
             else:
                 src = w2c_words[e - HOT : e - HOT + 2].rearrange("f s p b -> p (f s) b")
-            w2_raw[e] = keep.tile(list(src.shape), U8, name="w2_%d" % e, align_bytes=64)
+            w2_raw[e] = placed.tile(list(src.shape), U8, name="w2_%d" % e, align_bytes=64, offset=W2_RAW_AT[e])
             nc.sync.dma_start(out=w2_raw[e][:].bitcast(I32), in_=src.bitcast(I32))
 
         def load_cold_first_scales(r, queue):
@@ -102,11 +110,10 @@ def tile_moe_hot_s_mlp_gelu_kernel(
                 in_=src.rearrange("e s b c -> b (e s) c").bitcast(I32),
             )
 
-        def load_hot_first_scales(q, queue):
-            rows = w1h_scales.rearrange("e s b c -> (e s) b c")
+        def stage_hot_first_scales(queue):
             queue.dma_start(
-                out=w1h_sc[32 * q : 32 * q + 4 * HOT * PASSES, :].bitcast(I32),
-                in_=rows[:, 4 * q : 4 * q + 4, :].bitcast(I32),
+                out=regrouped[0 : 16 * GROUPS, 2 * N : STAGED].bitcast(I32),
+                in_=w1h_scales.rearrange("e s b c -> b (e s) c").bitcast(I32),
             )
 
         def move_staged(q, queue):
@@ -118,62 +125,59 @@ def tile_moe_hot_s_mlp_gelu_kernel(
         def list_slice(first, last):
             return offsets[:, first * LIST_COLS : last * LIST_COLS]
 
-        cold_sc = keep.tile([P, COLD * C], U8, name="cold_sc", align_bytes=64)
-        slot_words = placed.tile([P, PASSES, E * C], U32, name="slot_words", align_bytes=64, offset=SLOT_WORDS_AT)
+        slot_sc = keep.tile([P, E * C], U8, name="slot_sc", align_bytes=64)
+        early_words = placed.tile([P, PASSES, 2 * C], U32, name="early_words", align_bytes=64, offset=EARLY_WORDS_AT)
+        late_words = placed.tile([P, PASSES, 6 * C], U32, name="late_words", align_bytes=64, offset=LATE_WORDS_AT)
         gathered = {}
 
-        def gather_cold_scales():
-            half = COLD // 2
-            for f in range(0, COLD, half):
-                nc.vector.tensor_copy(
-                    out=cold_sc[:, f * C : (f + half) * C],
-                    in_=x_sc[:].indirect(list_slice(HOT + f, HOT + f + half)),
-                )
+        def gather_scales():
+            for first in range(0, E, 3):
+                last = min(first + 3, E)
+                nc.vector.tensor_copy(out=slot_sc[:, first * C : last * C], in_=x_sc[:].indirect(list_slice(first, last)))
 
-        def move_token_scales(r, queue):
-            queue.dma_start(out=cold_sc_pass1[r:P:32, :].bitcast(I32), in_=cold_sc[4 + r : P : 32, :].bitcast(I32))
+        def move_token_scales(q, queue):
+            queue.dma_start(
+                out=slot_planes[32 * q : 32 * q + 4].bitcast(I32),
+                in_=slot_sc[4 * PASSES * q : 4 * PASSES * (q + 1), :].bitcast(I32),
+            )
 
         def gather_pair(first):
             for s in range(PASSES):
-                words = slot_words[:, s, first * C : (first + 2) * C]
+                place = PAIRS.index(first)
+                words = early_words[:, s, :] if place == 0 else late_words[:, s, (place - 1) * 2 * C : place * 2 * C]
                 nc.vector.tensor_copy(out=words, in_=x_w[:, s, :].bitcast(U32).indirect(list_slice(first, first + 2)))
                 for j in range(2):
                     gathered[first + j, s] = words[:, j * C : (j + 1) * C]
 
-        for q in range(4):
-            load_token_scales(q, nc.sync if q % 2 else nc.scalar)
-        nc.sync.dma_start(out=x_w[:], in_=x_words.rearrange("s p t d -> p s (t d)").bitcast(I32))
-        load_first(2)
-        for g in range(GROUPS):
-            stage_second_scales(g, nc.scalar)
-        for r in range(4):
-            load_cold_first_scales(r, nc.gpsimd)
+        load_token_scales(nc.sync)
+        stage_hot_first_scales(nc.scalar)
         no_bias = keep.tile([P, 1], F32, name="no_bias")
         nc.scalar.activation(out=no_bias[:], in_=zero[:], func=GELU)
-        nc.vector.memset(planes[:].rearrange("p a c -> p (a c)").bitcast(I32), 0)
-        nc.vector.memset(w1h_sc[:].bitcast(I32), 0)
-        ident = keep.tile([P, P], F32, name="ident")
-        make_identity(nc, ident[:])
-        for q in range(4):
-            load_hot_first_scales(q, nc.gpsimd)
+        for g in range(GROUPS):
+            stage_second_scales(g, nc.scalar)
+        nc.sync.dma_start(out=x_w[:], in_=x_words.rearrange("s p t d -> p s (t d)").bitcast(I32))
+        load_cold_first_scales(0, nc.sync)
+        load_cold_first_scales(1, nc.sync)
+        load_first(2)
+        load_cold_first_scales(2, nc.sync)
+        load_cold_first_scales(3, nc.sync)
 
-        gather_cold_scales()
+        gather_scales()
         for r in range(4):
-            move_token_scales(r, nc.scalar)
+            move_token_scales(r, nc.sync)
+        gather_pair(2)
         nc.vector.tensor_copy(
-            out=regrouped[:].rearrange("p (e t c i) -> p e c t i", e=2, t=4, i=LINE),
+            out=regrouped[:, 0 : 2 * N].rearrange("p (e t c i) -> p e c t i", e=2, t=4, i=LINE),
             in_=staged[:].rearrange("p e (c i t) -> p e c t i", t=4, i=LINE),
         )
-        for first in PAIRS:
+        nc.vector.memset(planes[:].rearrange("p a c -> p (a c)").bitcast(I32), 0)
+        for first in PAIRS[1:]:
             gather_pair(first)
-        hot_sc = placed.tile([P, HOT * C], U8, name="hot_sc", align_bytes=64, offset=STAGED_AT)
-        nc.vector.tensor_copy(out=hot_sc[:], in_=x_sc[:].indirect(list_slice(0, HOT)))
-
         load_first(4)
         load_second(2)
-        load_first(6)
         for q in range(4):
             move_staged(q, nc.sync)
+        load_first(6)
         load_second(4)
         load_first(0)
         load_first(1)
@@ -193,18 +197,16 @@ def tile_moe_hot_s_mlp_gelu_kernel(
         dealt = {}
         y_acc = {}
         y_rows = {}
-        y_grouped = {}
 
         def first_layer(e):
-            acc = sums.tile([P, H], F32, name="h_acc", tag="h_acc", bufs=4)
+            acc = psum.tile([P, H], F32, name="h_acc%d" % e, offset=BANK * H_BANK[e])
             for s in range(PASSES):
                 if e < HOT:
-                    words, plane = w1_raw[e][:, s, :].bitcast(FP8X4), w1h_sc[4 * (PASSES * e + s) : P, :]
-                    x_plane = hot_sc[4 * s : P, e * C : (e + 1) * C]
+                    words, plane = w1_raw[e][:, s, :].bitcast(FP8X4), planes[:, PASSES * e + s, 2 * N : STAGED]
                 else:
                     f = e - HOT
                     words, plane = w1_raw[e][:, s, :].bitcast(FP4X4), w1c_sc[:, PASSES * f + s, :]
-                    x_plane = (cold_sc, cold_sc_pass1)[s][:, f * C : (f + 1) * C]
+                x_plane = slot_planes[:, s, e * C : (e + 1) * C]
                 nc.tensor.matmul_mx(
                     out=acc[:], lhsT=gathered[e, s].bitcast(FP8X4), lhsT_scale=x_plane,
                     rhs=words, rhs_scale=plane, start=(s == 0), stop=(s == PASSES - 1),
@@ -220,7 +222,7 @@ def tile_moe_hot_s_mlp_gelu_kernel(
 
         def turn(first):
             pairs = h_act[first][:].rearrange("p j i -> p (j i)").bitcast(F32)
-            turned = psum.tile([P, 4, C], F32, name="h_turned", tag="h_turned", bufs=1)
+            turned = psum.tile([P, 4, C], F32, name="h_turned%d" % first, offset=BANK * TURN_BANK)
             for block in range(4):
                 nc.tensor.transpose(turned[:, block, :], pairs[:, block * P : (block + 1) * P], ident[:])
             h_turned[first] = turned
@@ -253,10 +255,9 @@ def tile_moe_hot_s_mlp_gelu_kernel(
             codes, scales = h_quant[first]
             words, word_bytes, mx_dtype = dealt[first]
             rows = keep.tile([P, 4, 2 * C], F32, name="y_rows%d" % first)
-            grouped = keep.tile([P, 2 * C, 4], BF16, name="y_grouped%d" % first, align_bytes=64)
-            y_rows[first], y_grouped[first] = rows, grouped
+            y_rows[first] = rows
             for j in range(2):
-                acc = sums.tile([P, 4, C], F32, name="y_acc", tag="y_acc", bufs=3)
+                acc = psum.tile([P, 4, C], F32, name="y_acc%d" % (first + j), offset=BANK * Y_BANK[first + j])
                 mine = slice(j * C, (j + 1) * C)
                 for t in range(4):
                     nc.tensor.matmul_mx(
@@ -267,30 +268,21 @@ def tile_moe_hot_s_mlp_gelu_kernel(
                     )
                 y_acc[first + j] = acc
 
-        def hand_out(first):
-            rows, grouped = y_rows[first], y_grouped[first]
-            for j in range(2):
-                if first == PAIRS[-1] and j == 1:
-                    nc.vector.tensor_copy(out=grouped[:, C : 2 * C, :], in_=y_acc[first + 1][:].rearrange("p t j -> p j t"))
-                nc.scalar.copy(out=rows[:, :, j * C : (j + 1) * C], in_=y_acc[first + j][:])
-                if first == PAIRS[-1]:
-                    cols = slice((first + j) * C, (first + j + 1) * C)
-                    nc.sync.dma_start(out=out_rows[:, :, cols], in_=rows[:, :, j * C : (j + 1) * C])
-            if first != PAIRS[-1]:
+        def hand_out(e):
+            first, j = e - e % 2, e % 2
+            rows = y_rows[first]
+            nc.scalar.copy(out=rows[:, :, j * C : (j + 1) * C], in_=y_acc[e][:])
+            if j == 1:
                 nc.sync.dma_start(out=out_rows[:, :, first * C : (first + 2) * C], in_=rows[:])
 
         def planes_out(first):
-            grouped = y_grouped[first]
-            width = C if first == PAIRS[-1] else 2 * C
-            nc.vector.tensor_copy(
-                out=grouped[:, 0:width, :], in_=y_rows[first][:, :, 0:width].rearrange("p t j -> p j t")
+            grouped = placed.tile([P, 2 * C, 4], BF16, name="y_grouped%d" % first, align_bytes=64, offset=Y_GROUPED_AT[first])
+            cols = slice(first * C, (first + 2) * C)
+            nc.vector.tensor_copy(out=grouped[:], in_=y_rows[first][:].rearrange("p t j -> p j t"))
+            nc.vector.quantize_mx(
+                out=y_codes[:, cols].bitcast(FP8X4), scales=y_scales[:, cols],
+                in_=grouped[:].rearrange("p j t -> p (j t)"),
             )
-            for c in reversed(range(0, 2 * C, width)):
-                cols = slice(first * C + c, first * C + c + width)
-                nc.vector.quantize_mx(
-                    out=y_codes[:, cols].bitcast(FP8X4), scales=y_scales[:, cols],
-                    in_=grouped[:, c : c + width, :].rearrange("p j t -> p (j t)"),
-                )
 
         def store_codes(first, last):
             done = slice(first * C, last * C)
@@ -304,35 +296,39 @@ def tile_moe_hot_s_mlp_gelu_kernel(
         first_layer(5)
         deal_second(2)
         quantise_hidden(2)
-        first_layer(6)
         turn(4)
+        second_layer(2)
         group_hidden(4)
         quantise_hidden(4)
-        deal_second(4)
-        first_layer(7)
-        second_layer(2)
-        turn(6)
         hand_out(2)
+        hand_out(3)
+        first_layer(6)
+        first_layer(7)
+        deal_second(4)
+        second_layer(4)
+        hand_out(4)
+        turn(6)
         group_hidden(6)
         quantise_hidden(6)
-        second_layer(4)
         first_layer(0)
         first_layer(1)
         deal_second(6)
-        planes_out(2)
         turn(0)
-        second_layer(6)
         group_hidden(0)
         quantise_hidden(0)
+        second_layer(6)
         deal_second(0)
-        hand_out(4)
         second_layer(0)
+        hand_out(5)
+        planes_out(2)
         planes_out(4)
         store_codes(2, 6)
         hand_out(6)
+        hand_out(7)
+        hand_out(0)
+        hand_out(1)
         planes_out(6)
         store_codes(6, 8)
-        hand_out(0)
         planes_out(0)
         store_codes(0, 2)
 

@@ -23,23 +23,18 @@ LIST_COLS = C // 16
 LINE = 16
 
 PAIRS = (2, 4, 6, 0)
-VECTOR_GROUPS = ()
-GROUPS = 4
-STAGED = 2 * N + H
+VECTOR_GROUPS = (6,)
 
 BANK = 2048
+W2H_SC_AT = 1024
 H_BANK = {2: 0, 3: 1, 4: 2, 5: 3, 6: 0, 7: 1, 0: 2, 1: 3}
-Y_BANK = {2: 5, 3: 6, 4: 7, 5: 5, 6: 6, 7: 0, 0: 1, 1: 7}
-TURN_BANK = 4
-X_SC_AT = 0
-EARLY_WORDS_AT = X_SC_AT
-LATE_WORDS_AT = 36864
-STAGED_AT = LATE_WORDS_AT + 6144 - 512
-PLANES_AT = LATE_WORDS_AT + 6144
-H_GROUPED_AT = {2: 10240, 4: 12288, 6: 14336, 0: 16384}
-DEALT_AT = {2: 18432, 4: 20480, 6: 8192, 0: 22528}
+Y_BANK = {2: 5, 3: 6, 4: 2, 5: 3, 6: 2, 7: 3, 0: 5, 1: 6}
+TURN_BANK = {2: 4, 4: 7, 6: 4, 0: 7}
 W2_RAW_AT = {2: 26624, 4: 28672, 6: 30720, 0: 32768}
-Y_GROUPED_AT = {2: W2_RAW_AT[4], 4: W2_RAW_AT[2], 6: W2_RAW_AT[6], 0: W2_RAW_AT[0]}
+H_GROUPED_AT = {2: 10240, 4: 12288, 6: 14336, 0: 16384}
+DEALT_AT = {2: 18432, 4: H_GROUPED_AT[2], 6: 8192, 0: 22528}
+Y_GROUPED_AT = {2: W2_RAW_AT[6], 4: H_GROUPED_AT[0] - 1024, 6: H_GROUPED_AT[0] + 1024, 0: 43008}
+H_CODES_AT = {2: W2_RAW_AT[2], 4: W2_RAW_AT[4], 6: 39936, 0: W2H_SC_AT}
 
 
 def tile_moe_hot_s_mlp_gelu_kernel(
@@ -53,31 +48,34 @@ def tile_moe_hot_s_mlp_gelu_kernel(
         ring = ctx.enter_context(tc.tile_pool(name="ring", bufs=3))
         psum = ctx.enter_context(tc.psum_pool(name="psum", bufs=1))
 
-        x_sc = placed.tile([P, T], U8, name="x_sc", align_bytes=64, offset=X_SC_AT)
-        nc.gpsimd.memset(x_sc[:].bitcast(I32), 0)
         zero = keep.tile([P, 1], F32, name="zero")
         nc.gpsimd.memset(zero[:], 0.0)
+        x_sc = keep.tile([P, T], U8, name="x_sc", align_bytes=64)
+        nc.gpsimd.memset(x_sc[:].bitcast(I32), 0)
         ident = keep.tile([P, P], F32, name="ident")
         make_identity(nc, ident[:])
-        staged = placed.tile([P, 2, N], U8, name="staged", align_bytes=64, offset=STAGED_AT)
         w1c_sc = keep.tile([P, COLD * PASSES, H], U8, name="w1c_sc", align_bytes=64)
         nc.vector.memset(w1c_sc[:].rearrange("p a c -> p (a c)").bitcast(I32), 0)
-        nc.vector.memset(staged[:].rearrange("p a c -> p (a c)").bitcast(I32), 0)
-        slot_planes = keep.tile([P, PASSES, E * C], U8, name="slot_planes", align_bytes=64)
-        nc.vector.memset(slot_planes[:].rearrange("p a c -> p (a c)").bitcast(I32), 0)
-        planes = placed.tile([P, GROUPS, STAGED], U8, name="planes", align_bytes=64, offset=PLANES_AT)
+        cold_sc_pass1 = keep.tile([P, COLD * C], U8, name="cold_sc_pass1", align_bytes=64)
+        nc.vector.memset(cold_sc_pass1[:].bitcast(I32), 0)
+        w1h_sc = keep.tile([P, H], U8, name="w1h_sc", align_bytes=64)
+        nc.vector.memset(w1h_sc[:].bitcast(I32), 0)
+        w2c_sc = keep.tile([P, COLD, N], U8, name="w2c_sc", align_bytes=64)
+        nc.vector.memset(w2c_sc[:].rearrange("p a c -> p (a c)").bitcast(I32), 0)
+        w2h_sc = placed.tile([P, 1, N], U8, name="w2h_sc", align_bytes=64, offset=W2H_SC_AT)
+        nc.vector.memset(w2h_sc[:].rearrange("p a c -> p (a c)").bitcast(I32), 0)
 
         offsets = keep.tile([P, E * LIST_COLS], U16, name="offsets")
         nc.sync.dma_start(offsets[:], offs)
         x_w = keep.tile([P, PASSES, T], I32, name="x_w", align_bytes=64)
-        regrouped = keep.tile([P, STAGED], U8, name="regrouped", align_bytes=64)
 
         w1_raw = {}
         w2_raw = {}
 
-        def load_token_scales(queue):
+        def load_token_scales(q, queue):
             queue.dma_start(
-                out=x_sc[0 : 16 * PASSES, :].bitcast(I32), in_=x_scales.rearrange("s b t -> b s t").bitcast(I32)
+                out=x_sc[32 * q : 32 * q + 4 * PASSES, :].bitcast(I32),
+                in_=x_scales[:, 4 * q : 4 * q + 4, :].bitcast(I32),
             )
 
         def load_first(e):
@@ -99,97 +97,85 @@ def tile_moe_hot_s_mlp_gelu_kernel(
             w2_raw[e] = placed.tile(list(src.shape), U8, name="w2_%d" % e, align_bytes=64, offset=W2_RAW_AT[e])
             nc.sync.dma_start(out=w2_raw[e][:].bitcast(I32), in_=src.bitcast(I32))
 
-        def load_cold_first_scales(r, queue):
-            rows = w1c_scales.rearrange("e s (q r) c -> r q (e s) c", r=4)
-            queue.dma_start(out=w1c_sc[r:P:32].bitcast(I32), in_=rows[r].bitcast(I32))
+        def load_cold_scales(tile, scales, r, queue):
+            rows = scales.rearrange("e s (q r) c -> r q (e s) c", r=4)
+            queue.dma_start(out=tile[r:P:32].bitcast(I32), in_=rows[r].bitcast(I32))
 
-        def stage_second_scales(g, queue):
-            src = w2h_scales if g == 0 else w2c_scales[2 * g - HOT : 2 * g - HOT + 2]
+        def load_hot_scales(tile, scales, q, queue):
+            rows = scales.rearrange("e s b c -> (e s) b c")
             queue.dma_start(
-                out=staged[g : 16 * GROUPS : GROUPS].bitcast(I32),
-                in_=src.rearrange("e s b c -> b (e s) c").bitcast(I32),
+                out=tile[32 * q : 32 * q + 4 * rows.shape[0], :].bitcast(I32),
+                in_=rows[:, 4 * q : 4 * q + 4, :].bitcast(I32),
             )
 
-        def stage_hot_first_scales(queue):
-            queue.dma_start(
-                out=regrouped[0 : 16 * GROUPS, 2 * N : STAGED].bitcast(I32),
-                in_=w1h_scales.rearrange("e s b c -> b (e s) c").bitcast(I32),
-            )
-
-        def move_staged(q, queue):
-            queue.dma_start(
-                out=planes[32 * q : 32 * q + 4].bitcast(I32),
-                in_=regrouped[4 * GROUPS * q : 4 * GROUPS * (q + 1), :].bitcast(I32),
+        def deal_scales(out, in_):
+            nc.vector.tensor_copy(
+                out=out.rearrange("p a (t c i) -> p a c t i", t=4, i=LINE),
+                in_=in_.rearrange("p a (c i t) -> p a c t i", t=4, i=LINE),
             )
 
         def list_slice(first, last):
             return offsets[:, first * LIST_COLS : last * LIST_COLS]
 
-        slot_sc = keep.tile([P, E * C], U8, name="slot_sc", align_bytes=64)
-        early_words = placed.tile([P, PASSES, 2 * C], U32, name="early_words", align_bytes=64, offset=EARLY_WORDS_AT)
-        late_words = placed.tile([P, PASSES, 6 * C], U32, name="late_words", align_bytes=64, offset=LATE_WORDS_AT)
+        cold_sc = keep.tile([P, COLD * C], U8, name="cold_sc", align_bytes=64)
+        slot_words = keep.tile([P, PASSES, E * C], U32, name="slot_words", align_bytes=64)
         gathered = {}
 
-        def gather_scales():
-            for first in range(0, E, 3):
-                last = min(first + 3, E)
-                nc.vector.tensor_copy(out=slot_sc[:, first * C : last * C], in_=x_sc[:].indirect(list_slice(first, last)))
+        def gather_cold_scales():
+            half = COLD // 2
+            for f in range(0, COLD, half):
+                nc.vector.tensor_copy(
+                    out=cold_sc[:, f * C : (f + half) * C],
+                    in_=x_sc[:].indirect(list_slice(HOT + f, HOT + f + half)),
+                )
 
-        def move_token_scales(q, queue):
-            queue.dma_start(
-                out=slot_planes[32 * q : 32 * q + 4].bitcast(I32),
-                in_=slot_sc[4 * PASSES * q : 4 * PASSES * (q + 1), :].bitcast(I32),
-            )
+        def move_token_scales(r, queue):
+            queue.dma_start(out=cold_sc_pass1[r:P:32, :].bitcast(I32), in_=cold_sc[4 + r : P : 32, :].bitcast(I32))
 
         def gather_pair(first):
             for s in range(PASSES):
-                place = PAIRS.index(first)
-                words = early_words[:, s, :] if place == 0 else late_words[:, s, (place - 1) * 2 * C : place * 2 * C]
+                words = slot_words[:, s, first * C : (first + 2) * C]
                 nc.vector.tensor_copy(out=words, in_=x_w[:, s, :].bitcast(U32).indirect(list_slice(first, first + 2)))
                 for j in range(2):
                     gathered[first + j, s] = words[:, j * C : (j + 1) * C]
 
-        load_token_scales(nc.sync)
-        stage_hot_first_scales(nc.scalar)
         no_bias = keep.tile([P, 1], F32, name="no_bias")
         nc.scalar.activation(out=no_bias[:], in_=zero[:], func=GELU)
-        for g in range(GROUPS):
-            stage_second_scales(g, nc.scalar)
-        nc.sync.dma_start(out=x_w[:], in_=x_words.rearrange("s p t d -> p s (t d)").bitcast(I32))
-        load_cold_first_scales(0, nc.sync)
-        load_cold_first_scales(1, nc.sync)
-        load_first(2)
-        load_cold_first_scales(2, nc.sync)
-        load_cold_first_scales(3, nc.sync)
-
-        gather_scales()
-        for r in range(4):
-            move_token_scales(r, nc.sync)
-        gather_pair(2)
-        nc.vector.tensor_copy(
-            out=regrouped[:, 0 : 2 * N].rearrange("p (e t c i) -> p e c t i", e=2, t=4, i=LINE),
-            in_=staged[:].rearrange("p e (c i t) -> p e c t i", t=4, i=LINE),
-        )
-        nc.vector.memset(planes[:].rearrange("p a c -> p (a c)").bitcast(I32), 0)
-        for first in PAIRS[1:]:
-            gather_pair(first)
-        load_first(4)
-        load_second(2)
         for q in range(4):
-            move_staged(q, nc.sync)
+            load_token_scales(q, nc.sync)
+        nc.sync.dma_start(out=x_w[:], in_=x_words.rearrange("s p t d -> p s (t d)").bitcast(I32))
+        load_first(2)
+        for r in range(4):
+            load_cold_scales(w1c_sc, w1c_scales, r, nc.sync if r % 2 else nc.scalar)
+
+        gather_cold_scales()
+        for r in range(4):
+            move_token_scales(r, nc.scalar)
+        hot_sc = keep.tile([P, HOT * C], U8, name="hot_sc", align_bytes=64)
+        nc.vector.tensor_copy(out=hot_sc[:], in_=x_sc[:].indirect(list_slice(0, HOT)))
+        for first in PAIRS:
+            gather_pair(first)
+
+        load_first(4)
+        for r in range(4):
+            load_cold_scales(w2c_sc, w2c_scales, r, nc.sync)
         load_first(6)
+        load_second(2)
         load_second(4)
         load_first(0)
+        for q in range(4):
+            load_hot_scales(w1h_sc, w1h_scales, q, nc.sync)
         load_first(1)
         load_second(6)
         load_second(0)
+        for q in range(4):
+            load_hot_scales(w2h_sc[:, 0, :], w2h_scales, q, nc.sync)
 
         y_codes = keep.tile([P, E * C], U32, name="y_codes", align_bytes=64)
         y_scales = keep.tile([P, E * C], U8, name="y_scales", align_bytes=64)
         out_rows = out_0.rearrange("(m t) j -> m t j", t=4)
         out_words = out_1[0].rearrange("p j d -> p (j d)").bitcast(I32)
 
-        h_acc = {}
         h_act = {}
         h_turned = {}
         h_grouped = {}
@@ -197,16 +183,18 @@ def tile_moe_hot_s_mlp_gelu_kernel(
         dealt = {}
         y_acc = {}
         y_rows = {}
+        y_grouped = {}
 
         def first_layer(e):
             acc = psum.tile([P, H], F32, name="h_acc%d" % e, offset=BANK * H_BANK[e])
             for s in range(PASSES):
                 if e < HOT:
-                    words, plane = w1_raw[e][:, s, :].bitcast(FP8X4), planes[:, PASSES * e + s, 2 * N : STAGED]
+                    words, plane = w1_raw[e][:, s, :].bitcast(FP8X4), w1h_sc[4 * (PASSES * e + s) : P, :]
+                    x_plane = hot_sc[4 * s : P, e * C : (e + 1) * C]
                 else:
                     f = e - HOT
                     words, plane = w1_raw[e][:, s, :].bitcast(FP4X4), w1c_sc[:, PASSES * f + s, :]
-                x_plane = slot_planes[:, s, e * C : (e + 1) * C]
+                    x_plane = (cold_sc, cold_sc_pass1)[s][:, f * C : (f + 1) * C]
                 nc.tensor.matmul_mx(
                     out=acc[:], lhsT=gathered[e, s].bitcast(FP8X4), lhsT_scale=x_plane,
                     rhs=words, rhs_scale=plane, start=(s == 0), stop=(s == PASSES - 1),
@@ -222,7 +210,7 @@ def tile_moe_hot_s_mlp_gelu_kernel(
 
         def turn(first):
             pairs = h_act[first][:].rearrange("p j i -> p (j i)").bitcast(F32)
-            turned = psum.tile([P, 4, C], F32, name="h_turned%d" % first, offset=BANK * TURN_BANK)
+            turned = psum.tile([P, 4, C], F32, name="h_turned%d" % first, offset=BANK * TURN_BANK[first])
             for block in range(4):
                 nc.tensor.transpose(turned[:, block, :], pairs[:, block * P : (block + 1) * P], ident[:])
             h_turned[first] = turned
@@ -237,7 +225,7 @@ def tile_moe_hot_s_mlp_gelu_kernel(
             h_grouped[first] = grouped
 
         def quantise_hidden(first):
-            codes = keep.tile([P, 2 * C], U32, name="h_codes%d" % first, align_bytes=64)
+            codes = placed.tile([P, 2 * C], U32, name="h_codes%d" % first, align_bytes=64, offset=H_CODES_AT[first])
             scales = keep.tile([P, 2 * C], U8, name="h_scales%d" % first, align_bytes=64)
             nc.vector.quantize_mx(out=codes[:].bitcast(FP8X4), scales=scales[:], in_=h_grouped[first][:])
             h_quant[first] = (codes, scales)
@@ -249,11 +237,18 @@ def tile_moe_hot_s_mlp_gelu_kernel(
                 out=words[:].bitcast(word_dtype).rearrange("p e (t c i) -> p e c t i", t=4, i=LINE // word_bytes),
                 in_=w2_raw[first][:].bitcast(word_dtype).rearrange("p e (c i t) -> p e c t i", t=4, i=LINE // word_bytes),
             )
-            dealt[first] = (words, word_bytes, FP8X4 if first < HOT else FP4X4)
+            if first < HOT:
+                planes = keep.tile([P, 1, N], U8, name="w2_planes%d" % first, align_bytes=64)
+                deal_scales(planes[:], w2h_sc[:])
+                dealt[first] = (words, word_bytes, FP8X4, [planes[4 * j : P, 0, :] for j in range(2)])
+            else:
+                planes = keep.tile([P, 2, N], U8, name="w2_planes%d" % first, align_bytes=64)
+                deal_scales(planes[:], w2c_sc[:, first - HOT : first - HOT + 2, :])
+                dealt[first] = (words, word_bytes, FP4X4, [planes[:, j, :] for j in range(2)])
 
         def second_layer(first):
             codes, scales = h_quant[first]
-            words, word_bytes, mx_dtype = dealt[first]
+            words, word_bytes, mx_dtype, planes = dealt[first]
             rows = keep.tile([P, 4, 2 * C], F32, name="y_rows%d" % first)
             y_rows[first] = rows
             for j in range(2):
@@ -263,7 +258,7 @@ def tile_moe_hot_s_mlp_gelu_kernel(
                     nc.tensor.matmul_mx(
                         out=acc[:, t, :],
                         lhsT=words[:, j, t * P * word_bytes : (t + 1) * P * word_bytes].bitcast(mx_dtype),
-                        lhsT_scale=planes[:, first // 2, j * N + t * P : j * N + (t + 1) * P],
+                        lhsT_scale=planes[j][:, t * P : (t + 1) * P],
                         rhs=codes[:, mine].bitcast(FP8X4), rhs_scale=scales[:, mine], start=True, stop=True,
                     )
                 y_acc[first + j] = acc
@@ -275,66 +270,65 @@ def tile_moe_hot_s_mlp_gelu_kernel(
             if j == 1:
                 nc.sync.dma_start(out=out_rows[:, :, first * C : (first + 2) * C], in_=rows[:])
 
-        def planes_out(first):
-            grouped = placed.tile([P, 2 * C, 4], BF16, name="y_grouped%d" % first, align_bytes=64, offset=Y_GROUPED_AT[first])
-            cols = slice(first * C, (first + 2) * C)
-            nc.vector.tensor_copy(out=grouped[:], in_=y_rows[first][:].rearrange("p t j -> p j t"))
+        def planes_out(first, start=0, stop=2):
+            if start == 0:
+                y_grouped[first] = placed.tile(
+                    [P, 2 * C, 4], BF16, name="y_grouped%d" % first, align_bytes=64, offset=Y_GROUPED_AT[first]
+                )
+            grouped = y_grouped[first][:, start * C : stop * C, :]
+            cols = slice((first + start) * C, (first + stop) * C)
+            nc.vector.tensor_copy(out=grouped, in_=y_rows[first][:, :, start * C : stop * C].rearrange("p t j -> p j t"))
             nc.vector.quantize_mx(
-                out=y_codes[:, cols].bitcast(FP8X4), scales=y_scales[:, cols],
-                in_=grouped[:].rearrange("p j t -> p (j t)"),
+                out=y_codes[:, cols].bitcast(FP8X4), scales=y_scales[:, cols], in_=grouped.rearrange("p j t -> p (j t)")
             )
 
         def store_codes(first, last):
             done = slice(first * C, last * C)
             nc.sync.dma_start(out=out_words[:, done], in_=y_codes[:, done].bitcast(I32))
 
-        first_layer(2)
-        first_layer(3)
-        first_layer(4)
+        for e in range(HOT, HOT + 4):
+            first_layer(e)
         turn(2)
         group_hidden(2)
-        first_layer(5)
-        deal_second(2)
-        quantise_hidden(2)
         turn(4)
-        second_layer(2)
         group_hidden(4)
-        quantise_hidden(4)
-        hand_out(2)
-        hand_out(3)
         first_layer(6)
         first_layer(7)
+        deal_second(2)
+        quantise_hidden(2)
         deal_second(4)
-        second_layer(4)
-        hand_out(4)
+        quantise_hidden(4)
+        second_layer(2)
+        first_layer(0)
+        first_layer(1)
         turn(6)
         group_hidden(6)
         quantise_hidden(6)
-        first_layer(0)
-        first_layer(1)
+        hand_out(2)
+        hand_out(3)
+        second_layer(4)
         deal_second(6)
         turn(0)
         group_hidden(0)
-        quantise_hidden(0)
         second_layer(6)
         deal_second(0)
+        quantise_hidden(0)
         second_layer(0)
-        hand_out(5)
+        for e in PAIRS[1:]:
+            hand_out(e)
+            hand_out(e + 1)
         planes_out(2)
+        store_codes(2, 4)
         planes_out(4)
-        store_codes(2, 6)
-        hand_out(6)
-        hand_out(7)
-        hand_out(0)
-        hand_out(1)
         planes_out(6)
-        store_codes(6, 8)
-        planes_out(0)
+        store_codes(4, 8)
+        planes_out(0, 0, 1)
+        planes_out(0, 1, 2)
         store_codes(0, 2)
 
         for q in range(4):
             queue = nc.scalar if q < 2 else nc.sync
             queue.dma_start(
-                out=out_2[0, 4 * q : 4 * q + 4, :].bitcast(I32),
-                in_=y_scales[32 * q : 32 * q + 4, :].bitcast(I32),
+                out=out_2[0, q:16:4, :].bitcast(I32),
+                in_=y_scales[q:P:32, :].bitcast(I32),
             )

@@ -26,15 +26,14 @@ PAIRS = (2, 4, 6, 0)
 VECTOR_GROUPS = (6,)
 
 BANK = 2048
-W2H_SC_AT = 1024
 H_BANK = {2: 0, 3: 1, 4: 2, 5: 3, 6: 0, 7: 1, 0: 2, 1: 3}
 Y_BANK = {2: 5, 3: 6, 4: 2, 5: 3, 6: 2, 7: 3, 0: 5, 1: 6}
 TURN_BANK = {2: 4, 4: 7, 6: 4, 0: 7}
-W2_RAW_AT = {2: 26624, 4: 28672, 6: 30720, 0: 32768}
-H_GROUPED_AT = {2: 10240, 4: 12288, 6: 14336, 0: 16384}
-DEALT_AT = {2: 18432, 4: H_GROUPED_AT[2], 6: 8192, 0: 22528}
-Y_GROUPED_AT = {2: W2_RAW_AT[6], 4: H_GROUPED_AT[0] - 1024, 6: H_GROUPED_AT[0] + 1024, 0: 43008}
-H_CODES_AT = {2: W2_RAW_AT[2], 4: W2_RAW_AT[4], 6: 39936, 0: W2H_SC_AT}
+W2H_SC_AT = 2048
+W2C_SC_AT = 6144
+H_GROUPED_AT = {2: 16384, 4: 18432, 6: 20480, 0: 22528}
+H_CODES_AT = {2: W2C_SC_AT, 4: W2C_SC_AT + 1024, 6: 10240, 0: W2H_SC_AT + 256}
+Y_GROUPED_AT = {2: 12288, 4: W2H_SC_AT + 256 - 2048, 6: H_GROUPED_AT[0], 0: 14336}
 
 
 def tile_moe_hot_s_mlp_gelu_kernel(
@@ -48,10 +47,10 @@ def tile_moe_hot_s_mlp_gelu_kernel(
         ring = ctx.enter_context(tc.tile_pool(name="ring", bufs=3))
         psum = ctx.enter_context(tc.psum_pool(name="psum", bufs=1))
 
-        zero = keep.tile([P, 1], F32, name="zero")
-        nc.gpsimd.memset(zero[:], 0.0)
         x_sc = keep.tile([P, T], U8, name="x_sc", align_bytes=64)
         nc.gpsimd.memset(x_sc[:].bitcast(I32), 0)
+        zero = keep.tile([P, 1], F32, name="zero")
+        nc.gpsimd.memset(zero[:], 0.0)
         ident = keep.tile([P, P], F32, name="ident")
         make_identity(nc, ident[:])
         w1c_sc = keep.tile([P, COLD * PASSES, H], U8, name="w1c_sc", align_bytes=64)
@@ -60,7 +59,7 @@ def tile_moe_hot_s_mlp_gelu_kernel(
         nc.vector.memset(cold_sc_pass1[:].bitcast(I32), 0)
         w1h_sc = keep.tile([P, H], U8, name="w1h_sc", align_bytes=64)
         nc.vector.memset(w1h_sc[:].bitcast(I32), 0)
-        w2c_sc = keep.tile([P, COLD, N], U8, name="w2c_sc", align_bytes=64)
+        w2c_sc = placed.tile([P, COLD, N], U8, name="w2c_sc", align_bytes=64, offset=W2C_SC_AT)
         nc.vector.memset(w2c_sc[:].rearrange("p a c -> p (a c)").bitcast(I32), 0)
         w2h_sc = placed.tile([P, 1, N], U8, name="w2h_sc", align_bytes=64, offset=W2H_SC_AT)
         nc.vector.memset(w2h_sc[:].rearrange("p a c -> p (a c)").bitcast(I32), 0)
@@ -94,7 +93,7 @@ def tile_moe_hot_s_mlp_gelu_kernel(
                 src = w2h_words.rearrange("e s p n d -> p (e s) (n d)")
             else:
                 src = w2c_words[e - HOT : e - HOT + 2].rearrange("f s p b -> p (f s) b")
-            w2_raw[e] = placed.tile(list(src.shape), U8, name="w2_%d" % e, align_bytes=64, offset=W2_RAW_AT[e])
+            w2_raw[e] = keep.tile(list(src.shape), U8, name="w2_%d" % e, align_bytes=64)
             nc.sync.dma_start(out=w2_raw[e][:].bitcast(I32), in_=src.bitcast(I32))
 
         def load_cold_scales(tile, scales, r, queue):
@@ -157,10 +156,10 @@ def tile_moe_hot_s_mlp_gelu_kernel(
             gather_pair(first)
 
         load_first(4)
+        load_second(2)
         for r in range(4):
             load_cold_scales(w2c_sc, w2c_scales, r, nc.sync)
         load_first(6)
-        load_second(2)
         load_second(4)
         load_first(0)
         for q in range(4):
@@ -182,6 +181,8 @@ def tile_moe_hot_s_mlp_gelu_kernel(
         h_quant = {}
         dealt = {}
         y_acc = {}
+        w2c_planes = keep.tile([P, COLD, N], U8, name="w2c_planes", align_bytes=64)
+        deal_scales(w2c_planes[:], w2c_sc[:])
         y_rows = {}
         y_grouped = {}
 
@@ -232,19 +233,17 @@ def tile_moe_hot_s_mlp_gelu_kernel(
 
         def deal_second(first):
             word_dtype, word_bytes = (I32, 4) if first < HOT else (U16, 2)
-            words = placed.tile([P, 2, N * word_bytes], U8, name="w2_words%d" % first, align_bytes=64, offset=DEALT_AT[first])
+            words = keep.tile([P, 2, N * word_bytes], U8, name="w2_words%d" % first, align_bytes=64)
             nc.vector.tensor_copy(
                 out=words[:].bitcast(word_dtype).rearrange("p e (t c i) -> p e c t i", t=4, i=LINE // word_bytes),
                 in_=w2_raw[first][:].bitcast(word_dtype).rearrange("p e (c i t) -> p e c t i", t=4, i=LINE // word_bytes),
             )
             if first < HOT:
-                planes = keep.tile([P, 1, N], U8, name="w2_planes%d" % first, align_bytes=64)
+                planes = keep.tile([P, 1, N], U8, name="w2h_planes", align_bytes=64)
                 deal_scales(planes[:], w2h_sc[:])
                 dealt[first] = (words, word_bytes, FP8X4, [planes[4 * j : P, 0, :] for j in range(2)])
             else:
-                planes = keep.tile([P, 2, N], U8, name="w2_planes%d" % first, align_bytes=64)
-                deal_scales(planes[:], w2c_sc[:, first - HOT : first - HOT + 2, :])
-                dealt[first] = (words, word_bytes, FP4X4, [planes[:, j, :] for j in range(2)])
+                dealt[first] = (words, word_bytes, FP4X4, [w2c_planes[:, first - HOT + j, :] for j in range(2)])
 
         def second_layer(first):
             codes, scales = h_quant[first]
@@ -312,14 +311,16 @@ def tile_moe_hot_s_mlp_gelu_kernel(
         group_hidden(0)
         second_layer(6)
         deal_second(0)
-        quantise_hidden(0)
-        second_layer(0)
-        for e in PAIRS[1:]:
-            hand_out(e)
-            hand_out(e + 1)
+        hand_out(4)
+        hand_out(5)
         planes_out(2)
         store_codes(2, 4)
         planes_out(4)
+        quantise_hidden(0)
+        second_layer(0)
+        for e in PAIRS[2:]:
+            hand_out(e)
+            hand_out(e + 1)
         planes_out(6)
         store_codes(4, 8)
         planes_out(0, 0, 1)

@@ -143,13 +143,15 @@ def tile_moe_hot_s_mlp_gelu_kernel(
         for q in range(4):
             load_token_scales(q, nc.sync)
         nc.sync.dma_start(out=x_w[:], in_=x_words.rearrange("s p t d -> p s (t d)").bitcast(I32))
+        load_cold_scales(w1c_sc, w1c_scales, 0, nc.sync)
+        load_cold_scales(w1c_sc, w1c_scales, 1, nc.sync)
         load_first(2)
-        for r in range(4):
-            load_cold_scales(w1c_sc, w1c_scales, r, nc.sync if r % 2 else nc.scalar)
+        load_cold_scales(w1c_sc, w1c_scales, 2, nc.sync)
+        load_cold_scales(w1c_sc, w1c_scales, 3, nc.sync)
 
         gather_cold_scales()
         for r in range(4):
-            move_token_scales(r, nc.scalar)
+            move_token_scales(r, nc.sync)
         hot_sc = keep.tile([P, HOT * C], U8, name="hot_sc", align_bytes=64)
         nc.vector.tensor_copy(out=hot_sc[:], in_=x_sc[:].indirect(list_slice(0, HOT)))
         for first in PAIRS:

@@ -278,7 +278,10 @@ def tile_moe_hot_s_mlp_gelu_kernel(
                 )
             grouped = y_grouped[first][:, start * C : stop * C, :]
             cols = slice((first + start) * C, (first + stop) * C)
-            nc.vector.tensor_copy(out=grouped, in_=y_rows[first][:, :, start * C : stop * C].rearrange("p t j -> p j t"))
+            nc.vector.tensor_copy(
+                out=grouped.rearrange("p (c i) t -> p c t i", i=4),
+                in_=y_rows[first][:, :, start * C : stop * C].rearrange("p t (c i) -> p c t i", i=4),
+            )
             nc.vector.quantize_mx(
                 out=y_codes[:, cols].bitcast(FP8X4), scales=y_scales[:, cols], in_=grouped.rearrange("p j t -> p (j t)")
             )

@@ -53,14 +53,14 @@ def tile_moe_hot_s_mlp_gelu_kernel(
         nc.gpsimd.memset(zero[:], 0.0)
         ident = keep.tile([P, P], F32, name="ident")
         make_identity(nc, ident[:])
+        w2c_sc = placed.tile([P, COLD, N], U8, name="w2c_sc", align_bytes=64, offset=W2C_SC_AT)
+        nc.gpsimd.memset(w2c_sc[:].rearrange("p a c -> p (a c)").bitcast(I32), 0)
         w1c_sc = keep.tile([P, COLD * PASSES, H], U8, name="w1c_sc", align_bytes=64)
         nc.vector.memset(w1c_sc[:].rearrange("p a c -> p (a c)").bitcast(I32), 0)
         cold_sc_pass1 = keep.tile([P, COLD * C], U8, name="cold_sc_pass1", align_bytes=64)
         nc.vector.memset(cold_sc_pass1[:].bitcast(I32), 0)
         w1h_sc = keep.tile([P, H], U8, name="w1h_sc", align_bytes=64)
         nc.vector.memset(w1h_sc[:].bitcast(I32), 0)
-        w2c_sc = placed.tile([P, COLD, N], U8, name="w2c_sc", align_bytes=64, offset=W2C_SC_AT)
-        nc.vector.memset(w2c_sc[:].rearrange("p a c -> p (a c)").bitcast(I32), 0)
         w2h_sc = placed.tile([P, 1, N], U8, name="w2h_sc", align_bytes=64, offset=W2H_SC_AT)
         nc.vector.memset(w2h_sc[:].rearrange("p a c -> p (a c)").bitcast(I32), 0)
 
@@ -138,10 +138,10 @@ def tile_moe_hot_s_mlp_gelu_kernel(
                 for j in range(2):
                     gathered[first + j, s] = words[:, j * C : (j + 1) * C]
 
+        for q in range(4):
+            load_token_scales(q, nc.scalar if q < 2 else nc.sync)
         no_bias = keep.tile([P, 1], F32, name="no_bias")
         nc.scalar.activation(out=no_bias[:], in_=zero[:], func=GELU)
-        for q in range(4):
-            load_token_scales(q, nc.sync)
         nc.sync.dma_start(out=x_w[:], in_=x_words.rearrange("s p t d -> p s (t d)").bitcast(I32))
         load_cold_scales(w1c_sc, w1c_scales, 0, nc.sync)
         load_cold_scales(w1c_sc, w1c_scales, 1, nc.sync)
@@ -320,14 +320,15 @@ def tile_moe_hot_s_mlp_gelu_kernel(
         hand_out(5)
         planes_out(2)
         store_codes(2, 4)
-        planes_out(4)
         quantise_hidden(0)
         second_layer(0)
+        planes_out(4)
+        store_codes(4, 6)
         for e in PAIRS[2:]:
             hand_out(e)
             hand_out(e + 1)
         planes_out(6)
-        store_codes(4, 8)
+        store_codes(6, 8)
         planes_out(0, 0, 1)
         planes_out(0, 1, 2)
         store_codes(0, 2)

@@ -23,17 +23,18 @@ LIST_COLS = C // 16
 LINE = 16
 
 PAIRS = (2, 4, 6, 0)
-VECTOR_GROUPS = (6,)
 
 BANK = 2048
 H_BANK = {2: 0, 3: 1, 4: 2, 5: 3, 6: 0, 7: 1, 0: 2, 1: 3}
-Y_BANK = {2: 5, 3: 6, 4: 2, 5: 3, 6: 2, 7: 3, 0: 5, 1: 6}
 TURN_BANK = {2: 4, 4: 7, 6: 4, 0: 7}
+Y_BANK = {2: 5, 3: 6, 4: 2, 5: 3, 6: 2, 7: 3, 0: 5, 1: 6}
 W2H_SC_AT = 2048
-W2C_SC_AT = 6144
+W2_RAW_AT = {2: 6144, 4: 8192, 6: 10240, 0: 28672}
 H_GROUPED_AT = {2: 16384, 4: 18432, 6: 20480, 0: 22528}
-H_CODES_AT = {2: W2C_SC_AT, 4: W2C_SC_AT + 1024, 6: 10240, 0: W2H_SC_AT + 256}
-Y_GROUPED_AT = {2: 12288, 4: W2H_SC_AT + 256 - 2048, 6: H_GROUPED_AT[0], 0: 14336}
+H_CODES_AT = {2: W2_RAW_AT[2], 4: W2_RAW_AT[4], 6: 12288, 0: W2H_SC_AT + 256}
+PLANES_AT = {2: 13312, 4: H_GROUPED_AT[2], 6: H_GROUPED_AT[2] + 1024}
+Y_GROUPED_AT = {2: 24576, 4: W2H_SC_AT + 256 - 2048, 6: H_GROUPED_AT[0], 0: 14336}
+VECTOR_TURN = 6
 
 
 def tile_moe_hot_s_mlp_gelu_kernel(
@@ -53,7 +54,7 @@ def tile_moe_hot_s_mlp_gelu_kernel(
         nc.gpsimd.memset(zero[:], 0.0)
         ident = keep.tile([P, P], F32, name="ident")
         make_identity(nc, ident[:])
-        w2c_sc = placed.tile([P, COLD, N], U8, name="w2c_sc", align_bytes=64, offset=W2C_SC_AT)
+        w2c_sc = keep.tile([P, COLD, N], U8, name="w2c_sc", align_bytes=64)
         nc.gpsimd.memset(w2c_sc[:].rearrange("p a c -> p (a c)").bitcast(I32), 0)
         w1c_sc = keep.tile([P, COLD * PASSES, H], U8, name="w1c_sc", align_bytes=64)
         nc.vector.memset(w1c_sc[:].rearrange("p a c -> p (a c)").bitcast(I32), 0)
@@ -77,15 +78,14 @@ def tile_moe_hot_s_mlp_gelu_kernel(
                 in_=x_scales[:, 4 * q : 4 * q + 4, :].bitcast(I32),
             )
 
-        def load_first(e):
+        def load_first(e, count=1):
             if e < HOT:
                 src = w1h_words[e].rearrange("s p i d -> p s (i d)")
-                tile = keep.tile(list(src.shape), U8, name="w1_%d" % e, align_bytes=64)
-                w1_raw[e] = tile[:]
             else:
-                src = w1c_words[e - HOT : e - HOT + 2].rearrange("f s p b -> p (f s) b")
-                tile = keep.tile(list(src.shape), U8, name="w1_%d" % e, align_bytes=64)
-                w1_raw[e], w1_raw[e + 1] = tile[:, 0:PASSES, :], tile[:, PASSES : 2 * PASSES, :]
+                src = w1c_words[e - HOT : e - HOT + count].rearrange("f s p b -> p (f s) b")
+            tile = keep.tile(list(src.shape), U8, name="w1_%d" % e, align_bytes=64)
+            for j in range(count):
+                w1_raw[e + j] = tile[:, j * PASSES : (j + 1) * PASSES, :]
             nc.sync.dma_start(out=tile[:].bitcast(I32), in_=src.bitcast(I32))
 
         def load_second(e):
@@ -93,7 +93,7 @@ def tile_moe_hot_s_mlp_gelu_kernel(
                 src = w2h_words.rearrange("e s p n d -> p (e s) (n d)")
             else:
                 src = w2c_words[e - HOT : e - HOT + 2].rearrange("f s p b -> p (f s) b")
-            w2_raw[e] = keep.tile(list(src.shape), U8, name="w2_%d" % e, align_bytes=64)
+            w2_raw[e] = placed.tile(list(src.shape), U8, name="w2_%d" % e, align_bytes=64, offset=W2_RAW_AT[e])
             nc.sync.dma_start(out=w2_raw[e][:].bitcast(I32), in_=src.bitcast(I32))
 
         def load_cold_scales(tile, scales, r, queue):
@@ -145,7 +145,7 @@ def tile_moe_hot_s_mlp_gelu_kernel(
         nc.sync.dma_start(out=x_w[:], in_=x_words.rearrange("s p t d -> p s (t d)").bitcast(I32))
         load_cold_scales(w1c_sc, w1c_scales, 0, nc.sync)
         load_cold_scales(w1c_sc, w1c_scales, 1, nc.sync)
-        load_first(2)
+        load_first(2, 2)
         load_cold_scales(w1c_sc, w1c_scales, 2, nc.sync)
         load_cold_scales(w1c_sc, w1c_scales, 3, nc.sync)
 
@@ -157,11 +157,12 @@ def tile_moe_hot_s_mlp_gelu_kernel(
         for first in PAIRS:
             gather_pair(first)
 
-        load_first(4)
-        load_second(2)
+        load_first(4, 2)
         for r in range(4):
             load_cold_scales(w2c_sc, w2c_scales, r, nc.sync)
         load_first(6)
+        load_second(2)
+        load_first(7)
         load_second(4)
         load_first(0)
         for q in range(4):
@@ -183,8 +184,7 @@ def tile_moe_hot_s_mlp_gelu_kernel(
         h_quant = {}
         dealt = {}
         y_acc = {}
-        w2c_planes = keep.tile([P, COLD, N], U8, name="w2c_planes", align_bytes=64)
-        deal_scales(w2c_planes[:], w2c_sc[:])
+        cold_planes = {}
         y_rows = {}
         y_grouped = {}
 
@@ -220,7 +220,7 @@ def tile_moe_hot_s_mlp_gelu_kernel(
 
         def group_hidden(first):
             grouped = placed.tile([P, 8 * C], BF16, name="h_grouped%d" % first, align_bytes=64, offset=H_GROUPED_AT[first])
-            copy = nc.vector.tensor_copy if first in VECTOR_GROUPS else nc.scalar.copy
+            copy = nc.vector.tensor_copy if first == VECTOR_TURN else nc.scalar.copy
             copy(
                 out=grouped[:].bitcast(F32).rearrange("p (e j u) -> p e j u", e=2, u=2),
                 in_=h_turned[first][:].rearrange("p (e u) j -> p e j u", u=2),
@@ -232,6 +232,11 @@ def tile_moe_hot_s_mlp_gelu_kernel(
             scales = keep.tile([P, 2 * C], U8, name="h_scales%d" % first, align_bytes=64)
             nc.vector.quantize_mx(out=codes[:].bitcast(FP8X4), scales=scales[:], in_=h_grouped[first][:])
             h_quant[first] = (codes, scales)
+
+        def deal_cold_planes(first):
+            planes = placed.tile([P, 2, N], U8, name="w2c_planes%d" % first, align_bytes=64, offset=PLANES_AT[first])
+            deal_scales(planes[:], w2c_sc[:, first - HOT : first - HOT + 2, :])
+            cold_planes[first] = planes
 
         def deal_second(first):
             word_dtype, word_bytes = (I32, 4) if first < HOT else (U16, 2)
@@ -245,14 +250,12 @@ def tile_moe_hot_s_mlp_gelu_kernel(
                 deal_scales(planes[:], w2h_sc[:])
                 dealt[first] = (words, word_bytes, FP8X4, [planes[4 * j : P, 0, :] for j in range(2)])
             else:
-                dealt[first] = (words, word_bytes, FP4X4, [w2c_planes[:, first - HOT + j, :] for j in range(2)])
+                dealt[first] = (words, word_bytes, FP4X4, [cold_planes[first][:, j, :] for j in range(2)])
 
-        def second_layer(first):
+        def second_layer(first, experts=(0, 1)):
             codes, scales = h_quant[first]
             words, word_bytes, mx_dtype, planes = dealt[first]
-            rows = keep.tile([P, 4, 2 * C], F32, name="y_rows%d" % first)
-            y_rows[first] = rows
-            for j in range(2):
+            for j in experts:
                 acc = psum.tile([P, 4, C], F32, name="y_acc%d" % (first + j), offset=BANK * Y_BANK[first + j])
                 mine = slice(j * C, (j + 1) * C)
                 for t in range(4):
@@ -266,24 +269,28 @@ def tile_moe_hot_s_mlp_gelu_kernel(
 
         def hand_out(e):
             first, j = e - e % 2, e % 2
+            if j == 0:
+                y_rows[first] = keep.tile([P, 4, 2 * C], F32, name="y_rows%d" % first, align_bytes=64)
             rows = y_rows[first]
             nc.scalar.copy(out=rows[:, :, j * C : (j + 1) * C], in_=y_acc[e][:])
             if j == 1:
                 nc.sync.dma_start(out=out_rows[:, :, first * C : (first + 2) * C], in_=rows[:])
 
-        def planes_out(first, start=0, stop=2):
+        def round_out(first, start=0, stop=2):
             if start == 0:
                 y_grouped[first] = placed.tile(
                     [P, 2 * C, 4], BF16, name="y_grouped%d" % first, align_bytes=64, offset=Y_GROUPED_AT[first]
                 )
-            grouped = y_grouped[first][:, start * C : stop * C, :]
-            cols = slice((first + start) * C, (first + stop) * C)
             nc.vector.tensor_copy(
-                out=grouped.rearrange("p (c i) t -> p c t i", i=4),
+                out=y_grouped[first][:, start * C : stop * C, :].rearrange("p (c i) t -> p c t i", i=4),
                 in_=y_rows[first][:, :, start * C : stop * C].rearrange("p t (c i) -> p c t i", i=4),
             )
+
+        def quantise_out(first, start=0, stop=2):
+            cols = slice((first + start) * C, (first + stop) * C)
             nc.vector.quantize_mx(
-                out=y_codes[:, cols].bitcast(FP8X4), scales=y_scales[:, cols], in_=grouped.rearrange("p j t -> p (j t)")
+                out=y_codes[:, cols].bitcast(FP8X4), scales=y_scales[:, cols],
+                in_=y_grouped[first][:, start * C : stop * C, :].rearrange("p j t -> p (j t)"),
             )
 
         def store_codes(first, last):
@@ -298,8 +305,11 @@ def tile_moe_hot_s_mlp_gelu_kernel(
         group_hidden(4)
         first_layer(6)
         first_layer(7)
+        deal_cold_planes(2)
         deal_second(2)
         quantise_hidden(2)
+        deal_cold_planes(4)
+        deal_cold_planes(6)
         deal_second(4)
         quantise_hidden(4)
         second_layer(2)
@@ -307,30 +317,34 @@ def tile_moe_hot_s_mlp_gelu_kernel(
         first_layer(1)
         turn(6)
         group_hidden(6)
-        quantise_hidden(6)
         hand_out(2)
         hand_out(3)
+        round_out(2)
+        quantise_hidden(6)
+        quantise_out(2)
+        store_codes(2, 4)
         second_layer(4)
         deal_second(6)
         turn(0)
+        hand_out(4)
+        hand_out(5)
         group_hidden(0)
         second_layer(6)
         deal_second(0)
-        hand_out(4)
-        hand_out(5)
-        planes_out(2)
-        store_codes(2, 4)
         quantise_hidden(0)
         second_layer(0)
-        planes_out(4)
-        store_codes(4, 6)
+        round_out(4)
         for e in PAIRS[2:]:
             hand_out(e)
             hand_out(e + 1)
-        planes_out(6)
+        round_out(6)
+        quantise_out(4)
+        round_out(0, 0, 1)
+        quantise_out(6)
+        round_out(0, 1, 2)
+        quantise_out(0)
+        store_codes(4, 6)
         store_codes(6, 8)
-        planes_out(0, 0, 1)
-        planes_out(0, 1, 2)
         store_codes(0, 2)
 
         for q in range(4):

@@ -21,20 +21,22 @@ PASSES = K // 512
 COLD = E - HOT
 LIST_COLS = C // 16
 LINE = 16
-
-PAIRS = (2, 4, 6, 0)
+ALIGN = 256
 
 BANK = 2048
 H_BANK = {2: 0, 3: 1, 4: 2, 5: 3, 6: 0, 7: 1, 0: 2, 1: 3}
-TURN_BANK = {2: 4, 4: 7, 6: 4, 0: 7}
-Y_BANK = {2: 5, 3: 6, 4: 2, 5: 3, 6: 2, 7: 3, 0: 5, 1: 6}
-W2H_SC_AT = 2048
-W2_RAW_AT = {2: 6144, 4: 8192, 6: 10240, 0: 28672}
-H_GROUPED_AT = {2: 16384, 4: 18432, 6: 20480, 0: 22528}
-H_CODES_AT = {2: W2_RAW_AT[2], 4: W2_RAW_AT[4], 6: 12288, 0: W2H_SC_AT + 256}
-PLANES_AT = {2: 13312, 4: H_GROUPED_AT[2], 6: H_GROUPED_AT[2] + 1024}
-Y_GROUPED_AT = {2: 24576, 4: W2H_SC_AT + 256 - 2048, 6: H_GROUPED_AT[0], 0: 14336}
+TURN_BANK = {2: 4, 4: 7, 6: 4, 0: 7, 1: 4}
+Y_BANK = {2: 5, 3: 6, 4: 0, 5: 1, 6: 2, 7: 3, 0: 5, 1: 6}
+W1_AT = {7: 0}
+W2_AT = {2: 4096, 0: 8192}
+H_SCALES_AT = {2: W2_AT[2], 4: W1_AT[7], 0: W2_AT[0], 1: W2_AT[0] + 256}
+PLANES_AT = {4: W1_AT[7] + 256, 6: W1_AT[7] + 1280}
+Y_GROUPED_AT = {6: W2_AT[0] + 512}
 VECTOR_TURN = 6
+
+
+def group_size(first):
+    return 1 if first < HOT else 2
 
 
 def tile_moe_hot_s_mlp_gelu_kernel(
@@ -45,136 +47,126 @@ def tile_moe_hot_s_mlp_gelu_kernel(
     with ExitStack() as ctx:
         keep = ctx.enter_context(tc.tile_pool(name="keep", bufs=1))
         placed = ctx.enter_context(tc.tile_pool(name="placed", bufs=1))
-        ring = ctx.enter_context(tc.tile_pool(name="ring", bufs=3))
         psum = ctx.enter_context(tc.psum_pool(name="psum", bufs=1))
 
-        x_sc = keep.tile([P, T], U8, name="x_sc", align_bytes=64)
-        nc.gpsimd.memset(x_sc[:].bitcast(I32), 0)
-        zero = keep.tile([P, 1], F32, name="zero")
+        def held(shape, dtype, name, at=None):
+            if at is None:
+                return keep.tile(shape, dtype, name=name, align_bytes=ALIGN)
+            return placed.tile(shape, dtype, name=name, align_bytes=ALIGN, offset=at)
+
+        def zeroed(shape, name, engine):
+            tile = held(shape, U8, name)
+            flat = tile[:] if len(shape) == 2 else tile[:].rearrange("p a c -> p (a c)")
+            engine.memset(flat.bitcast(I32), 0)
+            return tile
+
+        x_sc = zeroed([P, T], "x_sc", nc.gpsimd)
+        zero = held([P, 1], F32, "zero")
         nc.gpsimd.memset(zero[:], 0.0)
-        ident = keep.tile([P, P], F32, name="ident")
+        ident = held([P, P], F32, "ident")
         make_identity(nc, ident[:])
-        w2c_sc = keep.tile([P, COLD, N], U8, name="w2c_sc", align_bytes=64)
-        nc.gpsimd.memset(w2c_sc[:].rearrange("p a c -> p (a c)").bitcast(I32), 0)
-        w1c_sc = keep.tile([P, COLD * PASSES, H], U8, name="w1c_sc", align_bytes=64)
-        nc.vector.memset(w1c_sc[:].rearrange("p a c -> p (a c)").bitcast(I32), 0)
-        cold_sc_pass1 = keep.tile([P, COLD * C], U8, name="cold_sc_pass1", align_bytes=64)
-        nc.vector.memset(cold_sc_pass1[:].bitcast(I32), 0)
-        w1h_sc = keep.tile([P, H], U8, name="w1h_sc", align_bytes=64)
-        nc.vector.memset(w1h_sc[:].bitcast(I32), 0)
-        w2h_sc = placed.tile([P, 1, N], U8, name="w2h_sc", align_bytes=64, offset=W2H_SC_AT)
-        nc.vector.memset(w2h_sc[:].rearrange("p a c -> p (a c)").bitcast(I32), 0)
+        w2c_sc = zeroed([P, COLD, N], "w2c_sc", nc.gpsimd)
+        w1c_sc = zeroed([P, COLD * PASSES, H], "w1c_sc", nc.vector)
+        moved_sc = zeroed([P, COLD * C], "moved_sc", nc.vector)
+        w1h_sc = zeroed([P, H], "w1h_sc", nc.vector)
+        w2h_sc = zeroed([P, 1, N], "w2h_sc", nc.vector)
 
-        offsets = keep.tile([P, E * LIST_COLS], U16, name="offsets")
+        offsets = held([P, E * LIST_COLS], U16, "offsets")
         nc.sync.dma_start(offsets[:], offs)
-        x_w = keep.tile([P, PASSES, T], I32, name="x_w", align_bytes=64)
-
-        w1_raw = {}
-        w2_raw = {}
-
-        def load_token_scales(q, queue):
+        for q in range(4):
+            queue = nc.scalar if q < 2 else nc.sync
             queue.dma_start(
                 out=x_sc[32 * q : 32 * q + 4 * PASSES, :].bitcast(I32),
                 in_=x_scales[:, 4 * q : 4 * q + 4, :].bitcast(I32),
             )
+        no_bias = held([P, 1], F32, "no_bias")
+        nc.scalar.activation(out=no_bias[:], in_=zero[:], func=GELU)
+        x_w = held([P, PASSES, T], I32, "x_w")
+        nc.sync.dma_start(out=x_w[:], in_=x_words.rearrange("s p t d -> p s (t d)").bitcast(I32))
 
-        def load_first(e, count=1):
-            if e < HOT:
-                src = w1h_words[e].rearrange("s p i d -> p s (i d)")
-            else:
-                src = w1c_words[e - HOT : e - HOT + count].rearrange("f s p b -> p (f s) b")
-            tile = keep.tile(list(src.shape), U8, name="w1_%d" % e, align_bytes=64)
-            for j in range(count):
-                w1_raw[e + j] = tile[:, j * PASSES : (j + 1) * PASSES, :]
+        w1_raw = {}
+        w2_raw = {}
+
+        def load_words(src, name, at=None):
+            tile = held(list(src.shape), U8, name, at)
             nc.sync.dma_start(out=tile[:].bitcast(I32), in_=src.bitcast(I32))
+            return tile
+
+        def load_cold_first(e, count):
+            src = w1c_words[e - HOT : e - HOT + count].rearrange("f s p b -> p (f s) b")
+            tile = load_words(src, "w1_%d" % e, W1_AT.get(e))
+            for a in range(count * PASSES):
+                w1_raw[e + a // PASSES, a % PASSES] = tile[:, a, :]
+
+        def load_hot_first(start, stop):
+            src = w1h_words.rearrange("e s p i d -> p (e s) (i d)")[:, start:stop, :]
+            tile = load_words(src, "w1h_%d" % start)
+            for a in range(start, stop):
+                w1_raw[a // PASSES, a % PASSES] = tile[:, a - start, :]
 
         def load_second(e):
             if e < HOT:
-                src = w2h_words.rearrange("e s p n d -> p (e s) (n d)")
+                src = w2h_words[e].rearrange("s p n d -> p s (n d)")
             else:
                 src = w2c_words[e - HOT : e - HOT + 2].rearrange("f s p b -> p (f s) b")
-            w2_raw[e] = placed.tile(list(src.shape), U8, name="w2_%d" % e, align_bytes=64, offset=W2_RAW_AT[e])
-            nc.sync.dma_start(out=w2_raw[e][:].bitcast(I32), in_=src.bitcast(I32))
+            w2_raw[e] = load_words(src, "w2_%d" % e, W2_AT.get(e))
 
-        def load_cold_scales(tile, scales, r, queue):
+        def load_cold_scales(tile, scales):
             rows = scales.rearrange("e s (q r) c -> r q (e s) c", r=4)
-            queue.dma_start(out=tile[r:P:32].bitcast(I32), in_=rows[r].bitcast(I32))
+            for r in range(4):
+                nc.sync.dma_start(out=tile[r:P:32].bitcast(I32), in_=rows[r].bitcast(I32))
 
-        def load_hot_scales(tile, scales, q, queue):
+        def load_hot_scales(tile, scales):
             rows = scales.rearrange("e s b c -> (e s) b c")
-            queue.dma_start(
-                out=tile[32 * q : 32 * q + 4 * rows.shape[0], :].bitcast(I32),
-                in_=rows[:, 4 * q : 4 * q + 4, :].bitcast(I32),
-            )
-
-        def deal_scales(out, in_):
-            nc.vector.tensor_copy(
-                out=out.rearrange("p a (t c i) -> p a c t i", t=4, i=LINE),
-                in_=in_.rearrange("p a (c i t) -> p a c t i", t=4, i=LINE),
-            )
+            for q in range(4):
+                nc.sync.dma_start(
+                    out=tile[32 * q : 32 * q + 4 * rows.shape[0], :].bitcast(I32),
+                    in_=rows[:, 4 * q : 4 * q + 4, :].bitcast(I32),
+                )
 
         def list_slice(first, last):
             return offsets[:, first * LIST_COLS : last * LIST_COLS]
 
-        cold_sc = keep.tile([P, COLD * C], U8, name="cold_sc", align_bytes=64)
-        slot_words = keep.tile([P, PASSES, E * C], U32, name="slot_words", align_bytes=64)
-        gathered = {}
+        cold_sc = held([P, COLD * C], U8, "cold_sc")
+        hot_sc = held([P, HOT * C], U8, "hot_sc")
+        slot_words = held([P, PASSES, E * C], U32, "slot_words")
 
-        def gather_cold_scales():
-            half = COLD // 2
-            for f in range(0, COLD, half):
+        def gather_words(first):
+            for s in range(PASSES):
                 nc.vector.tensor_copy(
-                    out=cold_sc[:, f * C : (f + half) * C],
-                    in_=x_sc[:].indirect(list_slice(HOT + f, HOT + f + half)),
+                    out=slot_words[:, s, first * C : (first + 2) * C],
+                    in_=x_w[:, s, :].bitcast(U32).indirect(list_slice(first, first + 2)),
                 )
 
-        def move_token_scales(r, queue):
-            queue.dma_start(out=cold_sc_pass1[r:P:32, :].bitcast(I32), in_=cold_sc[4 + r : P : 32, :].bitcast(I32))
-
-        def gather_pair(first):
-            for s in range(PASSES):
-                words = slot_words[:, s, first * C : (first + 2) * C]
-                nc.vector.tensor_copy(out=words, in_=x_w[:, s, :].bitcast(U32).indirect(list_slice(first, first + 2)))
-                for j in range(2):
-                    gathered[first + j, s] = words[:, j * C : (j + 1) * C]
-
-        for q in range(4):
-            load_token_scales(q, nc.scalar if q < 2 else nc.sync)
-        no_bias = keep.tile([P, 1], F32, name="no_bias")
-        nc.scalar.activation(out=no_bias[:], in_=zero[:], func=GELU)
-        nc.sync.dma_start(out=x_w[:], in_=x_words.rearrange("s p t d -> p s (t d)").bitcast(I32))
-        load_cold_scales(w1c_sc, w1c_scales, 0, nc.sync)
-        load_cold_scales(w1c_sc, w1c_scales, 1, nc.sync)
-        load_first(2, 2)
-        load_cold_scales(w1c_sc, w1c_scales, 2, nc.sync)
-        load_cold_scales(w1c_sc, w1c_scales, 3, nc.sync)
-
-        gather_cold_scales()
+        load_cold_scales(w1c_sc, w1c_scales)
+        load_cold_first(2, 1)
+        load_cold_first(3, 1)
+        half = COLD // 2
+        for f in range(0, COLD, half):
+            nc.vector.tensor_copy(
+                out=cold_sc[:, f * C : (f + half) * C], in_=x_sc[:].indirect(list_slice(HOT + f, HOT + f + half))
+            )
         for r in range(4):
-            move_token_scales(r, nc.sync)
-        hot_sc = keep.tile([P, HOT * C], U8, name="hot_sc", align_bytes=64)
+            nc.sync.dma_start(out=moved_sc[r:P:32, :].bitcast(I32), in_=cold_sc[4 + r : P : 32, :].bitcast(I32))
         nc.vector.tensor_copy(out=hot_sc[:], in_=x_sc[:].indirect(list_slice(0, HOT)))
-        for first in PAIRS:
-            gather_pair(first)
-
-        load_first(4, 2)
-        for r in range(4):
-            load_cold_scales(w2c_sc, w2c_scales, r, nc.sync)
-        load_first(6)
+        for first in (2, 4, 6, 0):
+            gather_words(first)
+        load_cold_first(4, 2)
+        load_cold_first(6, 1)
+        load_cold_scales(w2c_sc, w2c_scales)
         load_second(2)
-        load_first(7)
+        load_cold_first(7, 1)
         load_second(4)
-        load_first(0)
-        for q in range(4):
-            load_hot_scales(w1h_sc, w1h_scales, q, nc.sync)
-        load_first(1)
         load_second(6)
+        load_hot_scales(w1h_sc, w1h_scales)
+        load_hot_first(0, 3)
+        load_hot_first(3, 4)
+        load_hot_scales(w2h_sc[:, 0, :], w2h_scales)
         load_second(0)
-        for q in range(4):
-            load_hot_scales(w2h_sc[:, 0, :], w2h_scales, q, nc.sync)
+        load_second(1)
 
-        y_codes = keep.tile([P, E * C], U32, name="y_codes", align_bytes=64)
-        y_scales = keep.tile([P, E * C], U8, name="y_scales", align_bytes=64)
+        y_codes = held([P, E * C], U32, "y_codes")
+        y_scales = held([P, E * C], U8, "y_scales")
         out_rows = out_0.rearrange("(m t) j -> m t j", t=4)
         out_words = out_1[0].rearrange("p j d -> p (j d)").bitcast(I32)
 
@@ -182,170 +174,176 @@ def tile_moe_hot_s_mlp_gelu_kernel(
         h_turned = {}
         h_grouped = {}
         h_quant = {}
-        dealt = {}
+        dealt_words = {}
+        dealt_planes = {}
         y_acc = {}
-        cold_planes = {}
         y_rows = {}
         y_grouped = {}
+
+        def deal_words(first):
+            word_dtype, word_bytes = (U32, 4) if first < HOT else (U16, 2)
+            raw = w2_raw[first]
+            words = held(list(raw.shape), U8, "w2_words%d" % first)
+            nc.vector.tensor_copy(
+                out=words[:].bitcast(word_dtype).rearrange("p e (t c i) -> p e c t i", t=4, i=LINE // word_bytes),
+                in_=raw[:].bitcast(word_dtype).rearrange("p e (c i t) -> p e c t i", t=4, i=LINE // word_bytes),
+            )
+            for j in range(raw.shape[1]):
+                dealt_words[first + j] = words[:, j, :]
+
+        def deal_planes(first):
+            src = w2h_sc[:] if first < HOT else w2c_sc[:, first - HOT : first - HOT + 2, :]
+            planes = held(list(src.shape), U8, "w2_planes%d" % first, PLANES_AT.get(first))
+            nc.vector.tensor_copy(
+                out=planes[:].rearrange("p a (t c i) -> p a c t i", t=4, i=LINE),
+                in_=src.rearrange("p a (c i t) -> p a c t i", t=4, i=LINE),
+            )
+            for j in range(2):
+                dealt_planes[first + j] = planes[4 * j : P, 0, :] if first < HOT else planes[:, j, :]
 
         def first_layer(e):
             acc = psum.tile([P, H], F32, name="h_acc%d" % e, offset=BANK * H_BANK[e])
             for s in range(PASSES):
                 if e < HOT:
-                    words, plane = w1_raw[e][:, s, :].bitcast(FP8X4), w1h_sc[4 * (PASSES * e + s) : P, :]
+                    words, plane = w1_raw[e, s].bitcast(FP8X4), w1h_sc[4 * (PASSES * e + s) : P, :]
                     x_plane = hot_sc[4 * s : P, e * C : (e + 1) * C]
                 else:
                     f = e - HOT
-                    words, plane = w1_raw[e][:, s, :].bitcast(FP4X4), w1c_sc[:, PASSES * f + s, :]
-                    x_plane = (cold_sc, cold_sc_pass1)[s][:, f * C : (f + 1) * C]
+                    words, plane = w1_raw[e, s].bitcast(FP4X4), w1c_sc[:, PASSES * f + s, :]
+                    x_plane = (cold_sc, moved_sc)[s][:, f * C : (f + 1) * C]
                 nc.tensor.matmul_mx(
-                    out=acc[:], lhsT=gathered[e, s].bitcast(FP8X4), lhsT_scale=x_plane,
+                    out=acc[:], lhsT=slot_words[:, s, e * C : (e + 1) * C].bitcast(FP8X4), lhsT_scale=x_plane,
                     rhs=words, rhs_scale=plane, start=(s == 0), stop=(s == PASSES - 1),
                 )
-            if e % 2 == 0:
-                h_act[e] = ring.tile([P, 2, H], BF16, name="act", tag="act", align_bytes=64)
+            first = e if e < HOT else e - e % 2
+            if e == first:
+                h_act[e] = held([P, group_size(e), H], BF16, "h_act%d" % e)
             nc.scalar.activation(
-                out=h_act[e - e % 2][:, e % 2, :].rearrange("p (u m d) -> p u m d", u=2, d=2),
+                out=h_act[first][:, e - first, :].rearrange("p (u m d) -> p u m d", u=2, d=2),
                 in_=acc[:].rearrange("p (m u d) -> p u m d", u=2, d=2),
                 func=GELU,
                 bias=no_bias[:],
             )
 
         def turn(first):
+            blocks = 2 * group_size(first)
             pairs = h_act[first][:].rearrange("p j i -> p (j i)").bitcast(F32)
-            turned = psum.tile([P, 4, C], F32, name="h_turned%d" % first, offset=BANK * TURN_BANK[first])
-            for block in range(4):
+            turned = psum.tile([P, blocks, C], F32, name="h_turned%d" % first, offset=BANK * TURN_BANK[first])
+            for block in range(blocks):
                 nc.tensor.transpose(turned[:, block, :], pairs[:, block * P : (block + 1) * P], ident[:])
             h_turned[first] = turned
 
         def group_hidden(first):
-            grouped = placed.tile([P, 8 * C], BF16, name="h_grouped%d" % first, align_bytes=64, offset=H_GROUPED_AT[first])
+            grouped = held([P, 4 * group_size(first) * C], BF16, "h_grouped%d" % first)
             copy = nc.vector.tensor_copy if first == VECTOR_TURN else nc.scalar.copy
             copy(
-                out=grouped[:].bitcast(F32).rearrange("p (e j u) -> p e j u", e=2, u=2),
+                out=grouped[:].bitcast(F32).rearrange("p (e j u) -> p e j u", j=C, u=2),
                 in_=h_turned[first][:].rearrange("p (e u) j -> p e j u", u=2),
             )
             h_grouped[first] = grouped
 
         def quantise_hidden(first):
-            codes = placed.tile([P, 2 * C], U32, name="h_codes%d" % first, align_bytes=64, offset=H_CODES_AT[first])
-            scales = keep.tile([P, 2 * C], U8, name="h_scales%d" % first, align_bytes=64)
+            width = group_size(first) * C
+            codes = held([P, width], U32, "h_codes%d" % first)
+            scales = held([P, width], U8, "h_scales%d" % first, H_SCALES_AT.get(first))
             nc.vector.quantize_mx(out=codes[:].bitcast(FP8X4), scales=scales[:], in_=h_grouped[first][:])
-            h_quant[first] = (codes, scales)
+            for j in range(group_size(first)):
+                h_quant[first + j] = (codes[:, j * C : (j + 1) * C], scales[:, j * C : (j + 1) * C])
 
-        def deal_cold_planes(first):
-            planes = placed.tile([P, 2, N], U8, name="w2c_planes%d" % first, align_bytes=64, offset=PLANES_AT[first])
-            deal_scales(planes[:], w2c_sc[:, first - HOT : first - HOT + 2, :])
-            cold_planes[first] = planes
-
-        def deal_second(first):
-            word_dtype, word_bytes = (I32, 4) if first < HOT else (U16, 2)
-            words = keep.tile([P, 2, N * word_bytes], U8, name="w2_words%d" % first, align_bytes=64)
-            nc.vector.tensor_copy(
-                out=words[:].bitcast(word_dtype).rearrange("p e (t c i) -> p e c t i", t=4, i=LINE // word_bytes),
-                in_=w2_raw[first][:].bitcast(word_dtype).rearrange("p e (c i t) -> p e c t i", t=4, i=LINE // word_bytes),
-            )
-            if first < HOT:
-                planes = keep.tile([P, 1, N], U8, name="w2h_planes", align_bytes=64)
-                deal_scales(planes[:], w2h_sc[:])
-                dealt[first] = (words, word_bytes, FP8X4, [planes[4 * j : P, 0, :] for j in range(2)])
-            else:
-                dealt[first] = (words, word_bytes, FP4X4, [cold_planes[first][:, j, :] for j in range(2)])
-
-        def second_layer(first, experts=(0, 1)):
-            codes, scales = h_quant[first]
-            words, word_bytes, mx_dtype, planes = dealt[first]
-            for j in experts:
-                acc = psum.tile([P, 4, C], F32, name="y_acc%d" % (first + j), offset=BANK * Y_BANK[first + j])
-                mine = slice(j * C, (j + 1) * C)
-                for t in range(4):
-                    nc.tensor.matmul_mx(
-                        out=acc[:, t, :],
-                        lhsT=words[:, j, t * P * word_bytes : (t + 1) * P * word_bytes].bitcast(mx_dtype),
-                        lhsT_scale=planes[j][:, t * P : (t + 1) * P],
-                        rhs=codes[:, mine].bitcast(FP8X4), rhs_scale=scales[:, mine], start=True, stop=True,
-                    )
-                y_acc[first + j] = acc
+        def second_layer(e):
+            codes, scales = h_quant[e]
+            word_bytes, mx_dtype = (4, FP8X4) if e < HOT else (2, FP4X4)
+            acc = psum.tile([P, 4, C], F32, name="y_acc%d" % e, offset=BANK * Y_BANK[e])
+            for t in range(4):
+                nc.tensor.matmul_mx(
+                    out=acc[:, t, :],
+                    lhsT=dealt_words[e][:, t * P * word_bytes : (t + 1) * P * word_bytes].bitcast(mx_dtype),
+                    lhsT_scale=dealt_planes[e][:, t * P : (t + 1) * P],
+                    rhs=codes.bitcast(FP8X4), rhs_scale=scales, start=True, stop=True,
+                )
+            y_acc[e] = acc
 
         def hand_out(e):
             first, j = e - e % 2, e % 2
             if j == 0:
-                y_rows[first] = keep.tile([P, 4, 2 * C], F32, name="y_rows%d" % first, align_bytes=64)
+                y_rows[first] = held([P, 4, 2 * C], F32, "y_rows%d" % first)
             rows = y_rows[first]
             nc.scalar.copy(out=rows[:, :, j * C : (j + 1) * C], in_=y_acc[e][:])
-            if j == 1:
-                nc.sync.dma_start(out=out_rows[:, :, first * C : (first + 2) * C], in_=rows[:])
+
+        def store_rows(first):
+            nc.sync.dma_start(out=out_rows[:, :, first * C : (first + 2) * C], in_=y_rows[first][:])
 
         def round_out(first, start=0, stop=2):
             if start == 0:
-                y_grouped[first] = placed.tile(
-                    [P, 2 * C, 4], BF16, name="y_grouped%d" % first, align_bytes=64, offset=Y_GROUPED_AT[first]
-                )
+                y_grouped[first] = held([P, 2 * C, 4], BF16, "y_grouped%d" % first, Y_GROUPED_AT.get(first))
             nc.vector.tensor_copy(
                 out=y_grouped[first][:, start * C : stop * C, :].rearrange("p (c i) t -> p c t i", i=4),
                 in_=y_rows[first][:, :, start * C : stop * C].rearrange("p t (c i) -> p c t i", i=4),
             )
 
-        def quantise_out(first, start=0, stop=2):
-            cols = slice((first + start) * C, (first + stop) * C)
+        def quantise_out(first):
+            cols = slice(first * C, (first + 2) * C)
             nc.vector.quantize_mx(
                 out=y_codes[:, cols].bitcast(FP8X4), scales=y_scales[:, cols],
-                in_=y_grouped[first][:, start * C : stop * C, :].rearrange("p j t -> p (j t)"),
+                in_=y_grouped[first][:].rearrange("p j t -> p (j t)"),
             )
 
-        def store_codes(first, last):
-            done = slice(first * C, last * C)
+        def store_codes(first):
+            done = slice(first * C, (first + 2) * C)
             nc.sync.dma_start(out=out_words[:, done], in_=y_codes[:, done].bitcast(I32))
 
-        for e in range(HOT, HOT + 4):
+        for e in (2, 3, 4, 5):
             first_layer(e)
         turn(2)
         group_hidden(2)
+        first_layer(6)
         turn(4)
         group_hidden(4)
-        first_layer(6)
         first_layer(7)
-        deal_cold_planes(2)
-        deal_second(2)
+        deal_planes(2)
+        deal_words(2)
         quantise_hidden(2)
-        deal_cold_planes(4)
-        deal_cold_planes(6)
-        deal_second(4)
+        deal_words(4)
+        deal_planes(4)
         quantise_hidden(4)
-        second_layer(2)
-        first_layer(0)
-        first_layer(1)
+        deal_planes(6)
+        for e in (2, 3):
+            second_layer(e)
+            hand_out(e)
         turn(6)
         group_hidden(6)
-        hand_out(2)
-        hand_out(3)
-        round_out(2)
+        deal_words(6)
         quantise_hidden(6)
-        quantise_out(2)
-        store_codes(2, 4)
-        second_layer(4)
-        deal_second(6)
-        turn(0)
-        hand_out(4)
-        hand_out(5)
-        group_hidden(0)
-        second_layer(6)
-        deal_second(0)
-        quantise_hidden(0)
-        second_layer(0)
-        round_out(4)
-        for e in PAIRS[2:]:
+        for e in (4, 5):
+            second_layer(e)
             hand_out(e)
-            hand_out(e + 1)
-        round_out(6)
+        first_layer(0)
+        first_layer(1)
+        round_out(2)
+        round_out(4)
+        quantise_out(2)
         quantise_out(4)
-        round_out(0, 0, 1)
+        for e in range(HOT):
+            turn(e)
+            group_hidden(e)
+            second_layer(6 + e)
+            hand_out(6 + e)
+        deal_planes(0)
+        for e in range(HOT):
+            deal_words(e)
+        for e in range(HOT):
+            quantise_hidden(e)
+        for e in range(HOT):
+            second_layer(e)
+            hand_out(e)
+        round_out(6)
         quantise_out(6)
+        round_out(0, 0, 1)
         round_out(0, 1, 2)
         quantise_out(0)
-        store_codes(4, 6)
-        store_codes(6, 8)
-        store_codes(0, 2)
+        for first in (2, 4, 6, 0):
+            store_rows(first)
+            store_codes(first)
 
         for q in range(4):
             queue = nc.scalar if q < 2 else nc.sync

@@ -33,6 +33,7 @@ H_SCALES_AT = {2: W2_AT[2], 4: W1_AT[7], 0: W2_AT[0], 1: W2_AT[0] + 256}
 PLANES_AT = {4: W1_AT[7] + 256, 6: W1_AT[7] + 1280}
 Y_GROUPED_AT = {6: W2_AT[0] + 512}
 VECTOR_TURN = 6
+OUT_GROUPS = ((2, 6), (6, 8), (0, 2))
 
 
 def group_size(first):
@@ -263,34 +264,36 @@ def tile_moe_hot_s_mlp_gelu_kernel(
                 )
             y_acc[e] = acc
 
+        def out_group(e):
+            return [group for group in OUT_GROUPS if group[0] <= e < group[1]][0]
+
         def hand_out(e):
-            first, j = e - e % 2, e % 2
-            if j == 0:
-                y_rows[first] = held([P, 4, 2 * C], F32, "y_rows%d" % first)
-            rows = y_rows[first]
-            nc.scalar.copy(out=rows[:, :, j * C : (j + 1) * C], in_=y_acc[e][:])
+            first, last = out_group(e)
+            if e == first:
+                y_rows[first] = held([P, 4, (last - first) * C], F32, "y_rows%d" % first)
+            nc.scalar.copy(out=y_rows[first][:, :, (e - first) * C : (e - first + 1) * C], in_=y_acc[e][:])
 
-        def store_rows(first):
-            nc.sync.dma_start(out=out_rows[:, :, first * C : (first + 2) * C], in_=y_rows[first][:])
-
-        def round_out(first, start=0, stop=2):
-            if start == 0:
-                y_grouped[first] = held([P, 2 * C, 4], BF16, "y_grouped%d" % first, Y_GROUPED_AT.get(first))
+        def round_out(start, stop):
+            first, last = out_group(start)
+            if start == first:
+                y_grouped[first] = held([P, (last - first) * C, 4], BF16, "y_grouped%d" % first, Y_GROUPED_AT.get(first))
+            cols = slice((start - first) * C, (stop - first) * C)
             nc.vector.tensor_copy(
-                out=y_grouped[first][:, start * C : stop * C, :].rearrange("p (c i) t -> p c t i", i=4),
-                in_=y_rows[first][:, :, start * C : stop * C].rearrange("p t (c i) -> p c t i", i=4),
+                out=y_grouped[first][:, cols, :].rearrange("p (c i) t -> p c t i", i=4),
+                in_=y_rows[first][:, :, cols].rearrange("p t (c i) -> p c t i", i=4),
             )
 
         def quantise_out(first):
-            cols = slice(first * C, (first + 2) * C)
+            cols = slice(first * C, out_group(first)[1] * C)
             nc.vector.quantize_mx(
                 out=y_codes[:, cols].bitcast(FP8X4), scales=y_scales[:, cols],
                 in_=y_grouped[first][:].rearrange("p j t -> p (j t)"),
             )
 
-        def store_codes(first):
-            done = slice(first * C, (first + 2) * C)
-            nc.sync.dma_start(out=out_words[:, done], in_=y_codes[:, done].bitcast(I32))
+        def store_group(first, last):
+            cols = slice(first * C, last * C)
+            nc.sync.dma_start(out=out_rows[:, :, cols], in_=y_rows[first][:])
+            nc.sync.dma_start(out=out_words[:, cols], in_=y_codes[:, cols].bitcast(I32))
 
         for e in (2, 3, 4, 5):
             first_layer(e)
@@ -313,21 +316,20 @@ def tile_moe_hot_s_mlp_gelu_kernel(
         turn(6)
         group_hidden(6)
         deal_words(6)
-        quantise_hidden(6)
         for e in (4, 5):
             second_layer(e)
             hand_out(e)
         first_layer(0)
         first_layer(1)
-        round_out(2)
-        round_out(4)
-        quantise_out(2)
-        quantise_out(4)
+        round_out(2, 4)
+        round_out(4, 6)
+        quantise_hidden(6)
         for e in range(HOT):
             turn(e)
             group_hidden(e)
             second_layer(6 + e)
             hand_out(6 + e)
+        quantise_out(2)
         deal_planes(0)
         for e in range(HOT):
             deal_words(e)
@@ -336,14 +338,13 @@ def tile_moe_hot_s_mlp_gelu_kernel(
         for e in range(HOT):
             second_layer(e)
             hand_out(e)
-        round_out(6)
+        round_out(6, 8)
         quantise_out(6)
-        round_out(0, 0, 1)
-        round_out(0, 1, 2)
+        round_out(0, 1)
+        round_out(1, 2)
         quantise_out(0)
-        for first in (2, 4, 6, 0):
-            store_rows(first)
-            store_codes(first)
+        for first, last in OUT_GROUPS:
+            store_group(first, last)
 
         for q in range(4):
             queue = nc.scalar if q < 2 else nc.sync

from contextlib import ExitStack

import concourse.mybir as mybir
from concourse.masks import make_identity

K, T, E, C, H, N, HOT = 1024, 512, 8, 128, 512, 512, 2
FLOPS = 2 * E * C * (K * H + H * N)

F32 = mybir.dt.float32
BF16 = mybir.dt.bfloat16
I32 = mybir.dt.int32
U32 = mybir.dt.uint32
U16 = mybir.dt.uint16
U8 = mybir.dt.uint8
FP8X4 = mybir.dt.float8_e4m3fn_x4
FP4X4 = mybir.dt.float4_e2m1fn_x4
GELU = mybir.ActivationFunctionType.Gelu_apprx_tanh

P = 128
PASSES = K // 512
COLD = E - HOT
LIST_COLS = C // 16
LINE = 16
ALIGN = 256

BANK = 2048
H_BANK = {2: 0, 3: 1, 4: 2, 5: 3, 6: 0, 7: 1, 0: 2, 1: 3}
TURN_BANK = {2: 4, 4: 7, 6: 4, 0: 7, 1: 4}
Y_BANK = {2: 5, 3: 6, 4: 0, 5: 1, 6: 2, 7: 3, 0: 5, 1: 6}
W1_AT = {7: 0}
W2_AT = {2: 4096, 0: 8192}
H_SCALES_AT = {2: W2_AT[2], 4: W1_AT[7], 0: W2_AT[0], 1: W2_AT[0] + 256}
PLANES_AT = {4: W1_AT[7] + 256, 6: W1_AT[7] + 1280}
Y_GROUPED_AT = {6: W2_AT[0] + 512}
VECTOR_TURN = 6
OUT_GROUPS = ((2, 6), (6, 8), (0, 2))


def group_size(first):
    return 1 if first < HOT else 2


def tile_moe_hot_s_mlp_gelu_kernel(
    tc, x_words, x_scales, w1h_words, w1h_scales, w2h_words, w2h_scales,
    w1c_words, w1c_scales, w2c_words, w2c_scales, offs, out_0, out_1, out_2,
):
    nc = tc.nc
    with ExitStack() as ctx:
        keep = ctx.enter_context(tc.tile_pool(name="keep", bufs=1))
        placed = ctx.enter_context(tc.tile_pool(name="placed", bufs=1))
        psum = ctx.enter_context(tc.psum_pool(name="psum", bufs=1))

        def held(shape, dtype, name, at=None):
            if at is None:
                return keep.tile(shape, dtype, name=name, align_bytes=ALIGN)
            return placed.tile(shape, dtype, name=name, align_bytes=ALIGN, offset=at)

        def zeroed(shape, name, engine):
            tile = held(shape, U8, name)
            flat = tile[:] if len(shape) == 2 else tile[:].rearrange("p a c -> p (a c)")
            engine.memset(flat.bitcast(I32), 0)
            return tile

        x_sc = zeroed([P, T], "x_sc", nc.gpsimd)
        zero = held([P, 1], F32, "zero")
        nc.gpsimd.memset(zero[:], 0.0)
        ident = held([P, P], F32, "ident")
        make_identity(nc, ident[:])
        w2c_sc = zeroed([P, COLD, N], "w2c_sc", nc.gpsimd)
        w1c_sc = zeroed([P, COLD * PASSES, H], "w1c_sc", nc.vector)
        moved_sc = zeroed([P, COLD * C], "moved_sc", nc.vector)
        w1h_sc = zeroed([P, H], "w1h_sc", nc.vector)
        w2h_sc = zeroed([P, 1, N], "w2h_sc", nc.vector)

        offsets = held([P, E * LIST_COLS], U16, "offsets")
        nc.sync.dma_start(offsets[:], offs)
        for q in range(4):
            queue = nc.scalar if q < 2 else nc.sync
            queue.dma_start(
                out=x_sc[32 * q : 32 * q + 4 * PASSES, :].bitcast(I32),
                in_=x_scales[:, 4 * q : 4 * q + 4, :].bitcast(I32),
            )
        no_bias = held([P, 1], F32, "no_bias")
        nc.scalar.activation(out=no_bias[:], in_=zero[:], func=GELU)
        x_w = held([P, PASSES, T], I32, "x_w")
        nc.sync.dma_start(out=x_w[:], in_=x_words.rearrange("s p t d -> p s (t d)").bitcast(I32))

        w1_raw = {}
        w2_raw = {}

        def load_words(src, name, at=None):
            tile = held(list(src.shape), U8, name, at)
            nc.sync.dma_start(out=tile[:].bitcast(I32), in_=src.bitcast(I32))
            return tile

        def load_cold_first(e, count):
            src = w1c_words[e - HOT : e - HOT + count].rearrange("f s p b -> p (f s) b")
            tile = load_words(src, "w1_%d" % e, W1_AT.get(e))
            for a in range(count * PASSES):
                w1_raw[e + a // PASSES, a % PASSES] = tile[:, a, :]

        def load_hot_first(start, stop):
            src = w1h_words.rearrange("e s p i d -> p (e s) (i d)")[:, start:stop, :]
            tile = load_words(src, "w1h_%d" % start)
            for a in range(start, stop):
                w1_raw[a // PASSES, a % PASSES] = tile[:, a - start, :]

        def load_second(e):
            if e < HOT:
                src = w2h_words[e].rearrange("s p n d -> p s (n d)")
            else:
                src = w2c_words[e - HOT : e - HOT + 2].rearrange("f s p b -> p (f s) b")
            w2_raw[e] = load_words(src, "w2_%d" % e, W2_AT.get(e))

        def load_cold_scales(tile, scales):
            rows = scales.rearrange("e s (q r) c -> r q (e s) c", r=4)
            for r in range(4):
                nc.sync.dma_start(out=tile[r:P:32].bitcast(I32), in_=rows[r].bitcast(I32))

        def load_hot_scales(tile, scales):
            rows = scales.rearrange("e s b c -> (e s) b c")
            for q in range(4):
                nc.sync.dma_start(
                    out=tile[32 * q : 32 * q + 4 * rows.shape[0], :].bitcast(I32),
                    in_=rows[:, 4 * q : 4 * q + 4, :].bitcast(I32),
                )

        def list_slice(first, last):
            return offsets[:, first * LIST_COLS : last * LIST_COLS]

        cold_sc = held([P, COLD * C], U8, "cold_sc")
        hot_sc = held([P, HOT * C], U8, "hot_sc")
        slot_words = held([P, PASSES, E * C], U32, "slot_words")

        def gather_words(first):
            for s in range(PASSES):
                nc.vector.tensor_copy(
                    out=slot_words[:, s, first * C : (first + 2) * C],
                    in_=x_w[:, s, :].bitcast(U32).indirect(list_slice(first, first + 2)),
                )

        load_cold_scales(w1c_sc, w1c_scales)
        load_cold_first(2, 1)
        load_cold_first(3, 1)
        half = COLD // 2
        for f in range(0, COLD, half):
            nc.vector.tensor_copy(
                out=cold_sc[:, f * C : (f + half) * C], in_=x_sc[:].indirect(list_slice(HOT + f, HOT + f + half))
            )
        for r in range(4):
            nc.sync.dma_start(out=moved_sc[r:P:32, :].bitcast(I32), in_=cold_sc[4 + r : P : 32, :].bitcast(I32))
        nc.vector.tensor_copy(out=hot_sc[:], in_=x_sc[:].indirect(list_slice(0, HOT)))
        for first in (2, 4, 6, 0):
            gather_words(first)
        load_cold_first(4, 2)
        load_cold_first(6, 1)
        load_cold_scales(w2c_sc, w2c_scales)
        load_second(2)
        load_cold_first(7, 1)
        load_second(4)
        load_second(6)
        load_hot_scales(w1h_sc, w1h_scales)
        load_hot_first(0, 3)
        load_hot_first(3, 4)
        load_hot_scales(w2h_sc[:, 0, :], w2h_scales)
        load_second(0)
        load_second(1)

        y_codes = held([P, E * C], U32, "y_codes")
        y_scales = held([P, E * C], U8, "y_scales")
        out_rows = out_0.rearrange("(m t) j -> m t j", t=4)
        out_words = out_1[0].rearrange("p j d -> p (j d)").bitcast(I32)

        h_act = {}
        h_turned = {}
        h_grouped = {}
        h_quant = {}
        dealt_words = {}
        dealt_planes = {}
        y_acc = {}
        y_rows = {}
        y_grouped = {}

        def deal_words(first):
            word_dtype, word_bytes = (U32, 4) if first < HOT else (U16, 2)
            raw = w2_raw[first]
            words = held(list(raw.shape), U8, "w2_words%d" % first)
            nc.vector.tensor_copy(
                out=words[:].bitcast(word_dtype).rearrange("p e (t c i) -> p e c t i", t=4, i=LINE // word_bytes),
                in_=raw[:].bitcast(word_dtype).rearrange("p e (c i t) -> p e c t i", t=4, i=LINE // word_bytes),
            )
            for j in range(raw.shape[1]):
                dealt_words[first + j] = words[:, j, :]

        def deal_planes(first):
            src = w2h_sc[:] if first < HOT else w2c_sc[:, first - HOT : first - HOT + 2, :]
            planes = held(list(src.shape), U8, "w2_planes%d" % first, PLANES_AT.get(first))
            nc.vector.tensor_copy(
                out=planes[:].rearrange("p a (t c i) -> p a c t i", t=4, i=LINE),
                in_=src.rearrange("p a (c i t) -> p a c t i", t=4, i=LINE),
            )
            for j in range(2):
                dealt_planes[first + j] = planes[4 * j : P, 0, :] if first < HOT else planes[:, j, :]

        def first_layer(e):
            acc = psum.tile([P, H], F32, name="h_acc%d" % e, offset=BANK * H_BANK[e])
            for s in range(PASSES):
                if e < HOT:
                    words, plane = w1_raw[e, s].bitcast(FP8X4), w1h_sc[4 * (PASSES * e + s) : P, :]
                    x_plane = hot_sc[4 * s : P, e * C : (e + 1) * C]
                else:
                    f = e - HOT
                    words, plane = w1_raw[e, s].bitcast(FP4X4), w1c_sc[:, PASSES * f + s, :]
                    x_plane = (cold_sc, moved_sc)[s][:, f * C : (f + 1) * C]
                nc.tensor.matmul_mx(
                    out=acc[:], lhsT=slot_words[:, s, e * C : (e + 1) * C].bitcast(FP8X4), lhsT_scale=x_plane,
                    rhs=words, rhs_scale=plane, start=(s == 0), stop=(s == PASSES - 1),
                )
            first = e if e < HOT else e - e % 2
            if e == first:
                h_act[e] = held([P, group_size(e), H], BF16, "h_act%d" % e)
            nc.scalar.activation(
                out=h_act[first][:, e - first, :].rearrange("p (u m d) -> p u m d", u=2, d=2),
                in_=acc[:].rearrange("p (m u d) -> p u m d", u=2, d=2),
                func=GELU,
                bias=no_bias[:],
            )

        def turn(first):
            blocks = 2 * group_size(first)
            pairs = h_act[first][:].rearrange("p j i -> p (j i)").bitcast(F32)
            turned = psum.tile([P, blocks, C], F32, name="h_turned%d" % first, offset=BANK * TURN_BANK[first])
            for block in range(blocks):
                nc.tensor.transpose(turned[:, block, :], pairs[:, block * P : (block + 1) * P], ident[:])
            h_turned[first] = turned

        def group_hidden(first):
            grouped = held([P, 4 * group_size(first) * C], BF16, "h_grouped%d" % first)
            copy = nc.vector.tensor_copy if first == VECTOR_TURN else nc.scalar.copy
            copy(
                out=grouped[:].bitcast(F32).rearrange("p (e j u) -> p e j u", j=C, u=2),
                in_=h_turned[first][:].rearrange("p (e u) j -> p e j u", u=2),
            )
            h_grouped[first] = grouped

        def quantise_hidden(first):
            width = group_size(first) * C
            codes = held([P, width], U32, "h_codes%d" % first)
            scales = held([P, width], U8, "h_scales%d" % first, H_SCALES_AT.get(first))
            nc.vector.quantize_mx(out=codes[:].bitcast(FP8X4), scales=scales[:], in_=h_grouped[first][:])
            for j in range(group_size(first)):
                h_quant[first + j] = (codes[:, j * C : (j + 1) * C], scales[:, j * C : (j + 1) * C])

        def second_layer(e):
            codes, scales = h_quant[e]
            word_bytes, mx_dtype = (4, FP8X4) if e < HOT else (2, FP4X4)
            acc = psum.tile([P, 4, C], F32, name="y_acc%d" % e, offset=BANK * Y_BANK[e])
            for t in range(4):
                nc.tensor.matmul_mx(
                    out=acc[:, t, :],
                    lhsT=dealt_words[e][:, t * P * word_bytes : (t + 1) * P * word_bytes].bitcast(mx_dtype),
                    lhsT_scale=dealt_planes[e][:, t * P : (t + 1) * P],
                    rhs=codes.bitcast(FP8X4), rhs_scale=scales, start=True, stop=True,
                )
            y_acc[e] = acc

        def out_group(e):
            return [group for group in OUT_GROUPS if group[0] <= e < group[1]][0]

        def hand_out(e):
            first, last = out_group(e)
            if e == first:
                y_rows[first] = held([P, 4, (last - first) * C], F32, "y_rows%d" % first)
            nc.scalar.copy(out=y_rows[first][:, :, (e - first) * C : (e - first + 1) * C], in_=y_acc[e][:])

        def round_out(start, stop):
            first, last = out_group(start)
            if start == first:
                y_grouped[first] = held([P, (last - first) * C, 4], BF16, "y_grouped%d" % first, Y_GROUPED_AT.get(first))
            cols = slice((start - first) * C, (stop - first) * C)
            nc.vector.tensor_copy(
                out=y_grouped[first][:, cols, :].rearrange("p (c i) t -> p c t i", i=4),
                in_=y_rows[first][:, :, cols].rearrange("p t (c i) -> p c t i", i=4),
            )

        def quantise_out(first):
            cols = slice(first * C, out_group(first)[1] * C)
            nc.vector.quantize_mx(
                out=y_codes[:, cols].bitcast(FP8X4), scales=y_scales[:, cols],
                in_=y_grouped[first][:].rearrange("p j t -> p (j t)"),
            )

        def store_group(first, last):
            cols = slice(first * C, last * C)
            nc.sync.dma_start(out=out_rows[:, :, cols], in_=y_rows[first][:])
            nc.sync.dma_start(out=out_words[:, cols], in_=y_codes[:, cols].bitcast(I32))

        for e in (2, 3, 4, 5):
            first_layer(e)
        turn(2)
        group_hidden(2)
        first_layer(6)
        turn(4)
        group_hidden(4)
        first_layer(7)
        deal_planes(2)
        deal_words(2)
        quantise_hidden(2)
        deal_words(4)
        deal_planes(4)
        quantise_hidden(4)
        deal_planes(6)
        for e in (2, 3):
            second_layer(e)
            hand_out(e)
        turn(6)
        group_hidden(6)
        deal_words(6)
        for e in (4, 5):
            second_layer(e)
            hand_out(e)
        first_layer(0)
        first_layer(1)
        round_out(2, 4)
        round_out(4, 6)
        quantise_hidden(6)
        for e in range(HOT):
            turn(e)
            group_hidden(e)
            second_layer(6 + e)
            hand_out(6 + e)
        quantise_out(2)
        deal_planes(0)
        for e in range(HOT):
            deal_words(e)
        for e in range(HOT):
            quantise_hidden(e)
        for e in range(HOT):
            second_layer(e)
            hand_out(e)
        round_out(6, 8)
        quantise_out(6)
        round_out(0, 1)
        round_out(1, 2)
        quantise_out(0)
        for first, last in OUT_GROUPS:
            store_group(first, last)

        for q in range(4):
            queue = nc.scalar if q < 2 else nc.sync
            queue.dma_start(
                out=out_2[0, q:16:4, :].bitcast(I32),
                in_=y_scales[q:P:32, :].bitcast(I32),
            )
